import numpy as np
import ml_dtypes


def mxq(x, axis, fmt="e4m3"):
    dtype, down = {"e4m3": (ml_dtypes.float8_e4m3fn, 7), "e5m2": (ml_dtypes.float8_e5m2, 14)}[fmt]
    v = np.moveaxis(np.asarray(x, np.float32).astype(ml_dtypes.bfloat16).astype(np.float64), axis, -1)
    blocks = v.reshape(v.shape[:-1] + (-1, 32))
    amax = np.abs(blocks).max(-1, keepdims=True)
    byte = np.maximum(np.where(amax > 0, np.frexp(amax)[1] - 1 + 127, 0) - down, 1)
    scale = np.exp2(byte - 127.0)
    codes = (blocks / scale).astype(np.float32).astype(dtype).astype(np.float64)
    return np.moveaxis((codes * scale).reshape(v.shape), -1, axis)


WIDE = False


def mx_kscale(k):
    if not WIDE:
        return np.ones(k)
    levels = np.array([10, -10, 5, -5, 0])
    if k % 512:
        return np.exp2(np.random.permutation(np.resize(levels, k // 32))).repeat(32)
    a = np.empty((k // 512, 16))
    for p in range(k // 512):
        a[p, :8] = np.random.permutation(np.resize(levels, 8))
        for g in range(8):
            far = levels[np.abs(levels - a[p, g]) >= 10]
            a[p, g + 8] = far[np.random.randint(len(far))]
    return np.exp2(a.ravel()).repeat(32)


def f64(x):
    return np.asarray(x).astype(np.float64)


def striped(idx):
    return np.tile(idx.reshape(-1, 16).T, (8, 1)).astype(np.uint16)


def unstriped(offs):
    return offs[:16].T.reshape(-1).astype(np.int64)


def pack_weight(w):
    k, n = w.shape
    w = f64(np.asarray(w, np.float32).astype(ml_dtypes.bfloat16)).reshape(k // 32, 32, n)
    amax = np.abs(w).max(1)
    byte = np.clip(np.where(amax > 0, np.frexp(amax)[1] - 1 + 127 - 7, 1), 1, 254)
    scaled = (w * np.exp2(127.0 - byte)[:, None, :]).reshape(k, n).astype(np.float32)
    words = np.ascontiguousarray(scaled.reshape(k // 512, 128, 4, n).transpose(0, 1, 3, 2)).astype(ml_dtypes.float8_e4m3fn).view(np.uint8)
    return words, np.ascontiguousarray(byte.astype(np.uint8).reshape(k // 512, 16, n))


def unpack_weight(words, scales):
    g, p, n, _ = words.shape
    vals = np.ascontiguousarray(words).view(ml_dtypes.float8_e4m3fn).astype(np.float64) * np.repeat(np.exp2(scales.astype(np.float64) - 127.0), 8, axis=1)[..., None]
    return vals.transpose(0, 1, 3, 2).reshape(g * 512, n)


def silu(v):
    return v / (1.0 + np.exp(-np.maximum(v, -700.0)))


K, T, S, N = 1024, 1024, 512, 256
P = 2 ** 7


def setup_inputs():
    n = np.random.standard_normal
    s = mx_kscale(K)[:, None]
    packed_w1 = pack_weight(n((K, N)) / np.sqrt(K) / s)
    return {
        "xT": (n((K, T)) * s).astype(np.float32),
        "mean": np.tile(0.3 * np.random.standard_normal(T), (P, 1)).astype(np.float32),
        "inv": np.tile(np.random.uniform(0.5, 2.0, T), (P, 1)).astype(np.float32),
        "gsum": n((N, 1)).astype(np.float32),
        "b": (0.3 * n((N, 1))).astype(np.float32),
        "w1_words": packed_w1[0],
        "w1_scales": packed_w1[1],
        "offs": striped(np.random.permutation(T)[:S]),
    }


def reference(xT, mean, inv, gsum, b, w1_words, w1_scales, offs):
    xq = mxq(f64(xT)[:, unstriped(offs)], 0, "e4m3")
    y = unpack_weight(w1_words, w1_scales).T @ xq
    mg = f64(mean)[:1][:, unstriped(offs)]
    ig = f64(inv)[:1][:, unstriped(offs)]
    return silu((y - (f64(gsum) * mg)) * ig + f64(b))

@@ -1,0 +1,177 @@
+from contextlib import ExitStack
+
+import concourse.mybir as mybir
+from concourse.masks import make_identity
+
+K, T, S, N = 1024, 1024, 512, 256
+FLOPS = 2 * K * S * N
+
+F32 = mybir.dt.float32
+BF16 = mybir.dt.bfloat16
+I32 = mybir.dt.int32
+U32 = mybir.dt.uint32
+U16 = mybir.dt.uint16
+U8 = mybir.dt.uint8
+FP8X4 = mybir.dt.float8_e4m3fn_x4
+ACT = mybir.ActivationFunctionType
+
+P = 128
+PACK = 4
+K_PASS = P * PACK
+PASSES = K // K_PASS
+BLOCKS = S // P
+HALVES = N // P
+LIST_COLS = P // 16
+STAT_ROWS = 16
+
+
+def tile_picked_lnfold_silu_l_kernel(tc, xT, mean, inv, gsum, b, w1_words, w1_scales, offs, out):
+    nc = tc.nc
+    with ExitStack() as ctx:
+        keep = ctx.enter_context(tc.tile_pool(name="keep", bufs=1))
+        psum = ctx.enter_context(tc.psum_pool(name="psum", bufs=1))
+
+        offsets = keep.tile([P, S // 16], U16, name="offsets")
+        nc.sync.dma_start(offsets[:], offs)
+
+        warm_in = keep.tile([P, 1], F32, name="warm_in")
+        warm_out = keep.tile([P, 1], F32, name="warm_out")
+        nc.vector.memset(warm_in[:], 0.0)
+        nc.scalar.activation(warm_out[:], warm_in[:], ACT.Silu)
+
+        stats = keep.tile([P, T], F32, name="stats")
+        nc.sync.dma_start(stats[0:STAT_ROWS, :], mean[0:STAT_ROWS, :])
+        nc.sync.dma_start(stats[STAT_ROWS : 2 * STAT_ROWS, :], inv[0:STAT_ROWS, :])
+        nc.vector.memset(stats[32:64, :], 0.0)
+        nc.vector.memset(stats[64:P, :], 0.0)
+
+        planes = [keep.tile([P, T], F32, name="plane%d" % i) for i in range(PASSES * PACK)]
+        w_codes = [keep.tile([P, N], U32, name="w_codes%d" % z, align_bytes=64) for z in range(PASSES)]
+
+        def load_plane(i):
+            z, t = divmod(i, PACK)
+            nc.sync.dma_start(planes[i][:], xT[K_PASS * z + t : K_PASS * (z + 1) : PACK, :])
+
+        def load_w(z):
+            nc.sync.dma_start(w_codes[z][:].bitcast(I32), w1_words[z].rearrange("p n t -> p (n t)").bitcast(I32))
+
+        for i in range(6):
+            load_plane(i)
+        load_w(0)
+        load_plane(6)
+        load_plane(7)
+        load_w(1)
+
+        ident = keep.tile([P, P], F32, name="ident")
+        make_identity(nc, ident[:])
+        g_col = keep.tile([P, HALVES], F32, name="g_col")
+        b_col = keep.tile([P, HALVES], F32, name="b_col")
+        nc.gpsimd.dma_start(g_col[:], gsum.rearrange("(p h) o -> p (h o)", h=HALVES))
+        nc.gpsimd.dma_start(b_col[:], b.rearrange("(p h) o -> p (h o)", h=HALVES))
+        w_scales = keep.tile([P, PASSES, N], U8, name="w_scales", align_bytes=64)
+        nc.gpsimd.memset(w_scales[:].bitcast(I32), 0)
+        for q in range(4):
+            nc.gpsimd.dma_start(
+                w_scales[32 * q : 32 * q + 4, :, :].bitcast(I32),
+                w1_scales[:, 4 * q : 4 * q + 4, :].rearrange("z r c -> r z c").bitcast(I32),
+            )
+
+        picked = keep.tile([P, S], F32, name="picked")
+        nc.vector.tensor_copy(picked[:], stats[:].indirect(offsets[:]))
+        turned = psum.tile([P, BLOCKS, P], F32, name="turned", tag="acc0")
+        for c in range(BLOCKS):
+            nc.tensor.transpose(turned[:, c, :], picked[:, c * P : (c + 1) * P], ident[:])
+        g_rows = psum.tile([P, HALVES, P], F32, name="g_rows", tag="acc1")
+        for h in range(HALVES):
+            nc.tensor.transpose(g_rows[:, h, :], g_col[:, h : h + 1].to_broadcast([P, P]), ident[:])
+        inv_col = keep.tile([P, BLOCKS], F32, name="inv_col")
+        neg_inv = keep.tile([P, BLOCKS], F32, name="neg_inv")
+        shift = keep.tile([P, BLOCKS], F32, name="shift")
+        nc.scalar.activation(inv_col[:], turned[:, :, STAT_ROWS], ACT.Copy)
+        nc.scalar.activation(neg_inv[:], turned[:, :, STAT_ROWS], ACT.Copy, scale=-1.0)
+        for c in range(BLOCKS):
+            nc.scalar.activation(shift[:, c : c + 1], turned[:, c, 0:1], ACT.Copy, scale=neg_inv[:, c : c + 1])
+        sums = []
+        for c in range(BLOCKS):
+            term = keep.tile([P, HALVES, P], F32, name="term%d" % c)
+            nc.scalar.activation(term[:], g_rows[:], ACT.Copy, scale=shift[:, c : c + 1])
+            bank = psum.tile([P, HALVES, P], F32, name="sum%d" % c)
+            for h in range(HALVES):
+                nc.tensor.matmul(bank[:, h, :], term[:, h, :], ident[:], start=(h == 0), stop=False, is_transpose=True)
+            sums.append(bank)
+
+        pairs = [keep.tile([P, 2, S], BF16, name="pair%d" % u) for u in range(4)]
+
+        def gather(i, lo, hi):
+            nc.vector.tensor_copy(
+                pairs[i // 2][:, i % 2, lo * P : hi * P],
+                planes[i][:].indirect(offsets[:, lo * LIST_COLS : hi * LIST_COLS]),
+            )
+
+        woven0 = keep.tile([P, S, PACK], BF16, name="woven0", align_bytes=64)
+        for u in range(2):
+            gather(2 * u, 0, BLOCKS)
+            gather(2 * u + 1, 0, BLOCKS)
+            nc.scalar.copy(woven0[:, :, 2 * u : 2 * u + 2], pairs[u][:].rearrange("p e n -> p n e"))
+        codes0 = keep.tile([P, S], U32, name="codes0", align_bytes=64)
+        scales0 = keep.tile([P, S], U8, name="scales0", align_bytes=64)
+        nc.vector.quantize_mx(codes0[:].bitcast(FP8X4), scales0[:], woven0[:].rearrange("p n t -> p (n t)"))
+        accs = []
+        for c in range(BLOCKS):
+            acc = psum.tile([P, N], F32, name="y%d" % c, tag="acc%d" % c)
+            nc.tensor.matmul_mx(
+                acc[:],
+                lhsT=codes0[:, c * P : (c + 1) * P].bitcast(FP8X4),
+                lhsT_scale=scales0[:, c * P : (c + 1) * P],
+                rhs=w_codes[0][:].bitcast(FP8X4),
+                rhs_scale=w_scales[:, 0, :],
+                start=True,
+                stop=False,
+            )
+            accs.append(acc)
+
+        woven1 = [keep.tile([P, P, PACK], BF16, name="woven1_%d" % c, align_bytes=64) for c in range(BLOCKS)]
+        gather(4, 0, BLOCKS)
+        gather(5, 0, BLOCKS)
+        for c in range(BLOCKS):
+            nc.scalar.copy(woven1[c][:, :, 0:2], pairs[2][:, :, c * P : (c + 1) * P].rearrange("p e n -> p n e"))
+        gather(6, 0, BLOCKS)
+
+        out_rows = out.rearrange("(p h) j -> p h j", h=HALVES)
+
+        def weave(c):
+            nc.vector.tensor_copy(woven1[c][:, :, 2:4], pairs[3][:, :, c * P : (c + 1) * P].rearrange("p e n -> p n e"))
+
+        def finish(c):
+            codes = keep.tile([P, P], U32, name="codes1_%d" % c, align_bytes=64)
+            scales = keep.tile([P, P], U8, name="scales1_%d" % c, align_bytes=64)
+            nc.vector.quantize_mx(codes[:].bitcast(FP8X4), scales[:], woven1[c][:].rearrange("p n t -> p (n t)"))
+            nc.tensor.matmul_mx(
+                accs[c][:],
+                lhsT=codes[:].bitcast(FP8X4),
+                lhsT_scale=scales[:],
+                rhs=w_codes[1][:].bitcast(FP8X4),
+                rhs_scale=w_scales[:, 1, :],
+                start=False,
+                stop=True,
+            )
+            scaled = keep.tile([P, HALVES, P], F32, name="scaled%d" % c)
+            nc.scalar.activation(
+                scaled[:], accs[c][:].rearrange("j (p h) -> j h p", h=HALVES), ACT.Copy, scale=inv_col[:, c : c + 1]
+            )
+            for h in range(HALVES):
+                nc.tensor.matmul(
+                    sums[c][:, h, :], scaled[:, h, :], ident[:], start=False, stop=(h == HALVES - 1), is_transpose=True
+                )
+            result = keep.tile([P, HALVES, P], F32, name="result%d" % c)
+            for h in range(HALVES):
+                nc.scalar.activation(result[:, h, :], sums[c][:, h, :], ACT.Silu, bias=b_col[:, h : h + 1])
+            nc.sync.dma_start(out_rows[:, :, c * P : (c + 1) * P], result[:])
+
+        for step in range(BLOCKS + 2):
+            if step < BLOCKS:
+                gather(7, step, step + 1)
+            if 1 <= step <= BLOCKS:
+                weave(step - 1)
+            if step >= 2:
+                finish(step - 2)

@@ -43,9 +43,9 @@ def tile_picked_lnfold_silu_l_kernel(tc, xT, mean, inv, gsum, b, w1_words, w1_sc
         nc.sync.dma_start(stats[0:STAT_ROWS, :], mean[0:STAT_ROWS, :])
         nc.sync.dma_start(stats[STAT_ROWS : 2 * STAT_ROWS, :], inv[0:STAT_ROWS, :])
         nc.vector.memset(stats[32:64, :], 0.0)
-        nc.vector.memset(stats[64:P, :], 0.0)
+        nc.gpsimd.memset(stats[64:P, :], 0.0)
 
-        planes = [keep.tile([P, T], F32, name="plane%d" % i) for i in range(PASSES * PACK)]
+        planes = [keep.tile([P, T], F32, name="plane%d" % i, align_bytes=64) for i in range(PASSES * PACK)]
         w_codes = [keep.tile([P, N], U32, name="w_codes%d" % z, align_bytes=64) for z in range(PASSES)]
 
         def load_plane(i):
@@ -55,26 +55,36 @@ def tile_picked_lnfold_silu_l_kernel(tc, xT, mean, inv, gsum, b, w1_words, w1_sc
         def load_w(z):
             nc.sync.dma_start(w_codes[z][:].bitcast(I32), w1_words[z].rearrange("p n t -> p (n t)").bitcast(I32))
 
-        for i in range(6):
+        w_scales = keep.tile([P, PASSES, N], U8, name="w_scales", align_bytes=64)
+        nc.vector.memset(w_scales[:].bitcast(I32), 0)
+        g_col = keep.tile([P, HALVES], F32, name="g_col")
+        b_col = keep.tile([P, HALVES], F32, name="b_col")
+
+        def load_w_scales(q):
+            nc.sync.dma_start(
+                w_scales[32 * q : 32 * q + 4, :, :].bitcast(I32),
+                w1_scales[:, 4 * q : 4 * q + 4, :].rearrange("z r c -> r z c").bitcast(I32),
+            )
+
+        for i in range(3):
             load_plane(i)
-        load_w(0)
-        load_plane(6)
+        nc.sync.dma_start(g_col[:], gsum.rearrange("(p h) o -> p (h o)", h=HALVES))
+        nc.sync.dma_start(b_col[:], b.rearrange("(p h) o -> p (h o)", h=HALVES))
+        for i in range(3, 7):
+            load_plane(i)
+            load_w_scales(i - 3)
         load_plane(7)
+        load_w(0)
         load_w(1)
 
         ident = keep.tile([P, P], F32, name="ident")
         make_identity(nc, ident[:])
-        g_col = keep.tile([P, HALVES], F32, name="g_col")
-        b_col = keep.tile([P, HALVES], F32, name="b_col")
-        nc.gpsimd.dma_start(g_col[:], gsum.rearrange("(p h) o -> p (h o)", h=HALVES))
-        nc.gpsimd.dma_start(b_col[:], b.rearrange("(p h) o -> p (h o)", h=HALVES))
-        w_scales = keep.tile([P, PASSES, N], U8, name="w_scales", align_bytes=64)
-        nc.gpsimd.memset(w_scales[:].bitcast(I32), 0)
-        for q in range(4):
-            nc.gpsimd.dma_start(
-                w_scales[32 * q : 32 * q + 4, :, :].bitcast(I32),
-                w1_scales[:, 4 * q : 4 * q + 4, :].rearrange("z r c -> r z c").bitcast(I32),
-            )
+
+        flat0 = keep.tile([P, PACK, S], BF16, name="flat0")
+        pair = keep.tile([P, 2, S], BF16, name="pair")
+        rounded0 = keep.tile([P, T], BF16, name="rounded0")
+        nc.scalar.copy(rounded0[:], planes[0][:])
+        nc.scalar.activation(flat0[:, 0, :], rounded0[:].indirect(offsets[:]), ACT.Copy)
 
         picked = keep.tile([P, S], F32, name="picked")
         nc.vector.tensor_copy(picked[:], stats[:].indirect(offsets[:]))
@@ -84,10 +94,16 @@ def tile_picked_lnfold_silu_l_kernel(tc, xT, mean, inv, gsum, b, w1_words, w1_sc
         g_rows = psum.tile([P, HALVES, P], F32, name="g_rows", tag="acc1")
         for h in range(HALVES):
             nc.tensor.transpose(g_rows[:, h, :], g_col[:, h : h + 1].to_broadcast([P, P]), ident[:])
-        inv_col = keep.tile([P, BLOCKS], F32, name="inv_col")
+        b_bank = psum.tile([P, HALVES, P], F32, name="b_bank", tag="acc2")
+        for h in range(HALVES):
+            nc.tensor.transpose(b_bank[:, h, :], b_col[:, h : h + 1].to_broadcast([P, P]), ident[:])
+        b_rows = keep.tile([P, HALVES, P], F32, name="b_rows")
+        nc.scalar.copy(b_rows[:], b_bank[:])
+        inv_col = [keep.tile([P, 1], F32, name="inv_col%d" % c, tag="shared%d" % c, align_bytes=64) for c in range(BLOCKS)]
         neg_inv = keep.tile([P, BLOCKS], F32, name="neg_inv")
         shift = keep.tile([P, BLOCKS], F32, name="shift")
-        nc.scalar.activation(inv_col[:], turned[:, :, STAT_ROWS], ACT.Copy)
+        for c in range(BLOCKS):
+            nc.scalar.activation(inv_col[c][:], turned[:, c, STAT_ROWS : STAT_ROWS + 1], ACT.Copy)
         nc.scalar.activation(neg_inv[:], turned[:, :, STAT_ROWS], ACT.Copy, scale=-1.0)
         for c in range(BLOCKS):
             nc.scalar.activation(shift[:, c : c + 1], turned[:, c, 0:1], ACT.Copy, scale=neg_inv[:, c : c + 1])
@@ -97,23 +113,26 @@ def tile_picked_lnfold_silu_l_kernel(tc, xT, mean, inv, gsum, b, w1_words, w1_sc
             nc.scalar.activation(term[:], g_rows[:], ACT.Copy, scale=shift[:, c : c + 1])
             bank = psum.tile([P, HALVES, P], F32, name="sum%d" % c)
             for h in range(HALVES):
-                nc.tensor.matmul(bank[:, h, :], term[:, h, :], ident[:], start=(h == 0), stop=False, is_transpose=True)
+                nc.tensor.matmul(bank[:, h, :], b_rows[:, h, :], ident[:], start=(h == 0), stop=False, is_transpose=True)
+            for h in range(HALVES):
+                nc.tensor.matmul(bank[:, h, :], term[:, h, :], ident[:], start=False, stop=False, is_transpose=True)
             sums.append(bank)
 
-        pairs = [keep.tile([P, 2, S], BF16, name="pair%d" % u) for u in range(4)]
 
-        def gather(i, lo, hi):
-            nc.vector.tensor_copy(
-                pairs[i // 2][:, i % 2, lo * P : hi * P],
-                planes[i][:].indirect(offsets[:, lo * LIST_COLS : hi * LIST_COLS]),
-            )
+        def gather(i):
+            nc.vector.tensor_copy(flat0[:, i, :] if i < PACK else pair[:, i - PACK, :], planes[i][:].indirect(offsets[:]))
 
         woven0 = keep.tile([P, S, PACK], BF16, name="woven0", align_bytes=64)
-        for u in range(2):
-            gather(2 * u, 0, BLOCKS)
-            gather(2 * u + 1, 0, BLOCKS)
-            nc.scalar.copy(woven0[:, :, 2 * u : 2 * u + 2], pairs[u][:].rearrange("p e n -> p n e"))
-        codes0 = keep.tile([P, S], U32, name="codes0", align_bytes=64)
+        for i in range(1, PACK):
+            gather(i)
+        nc.scalar.copy(
+            woven0[:].rearrange("p (c i) t -> p c t i", i=4), flat0[:].rearrange("p t (c i) -> p c t i", i=4)
+        )
+        gather(4)
+        gather(5)
+        late = keep.tile([P, BLOCKS + 2, P], BF16, name="late")
+        nc.vector.tensor_copy(late[:, 0:BLOCKS, :].rearrange("p c n -> p (c n)"), planes[6][:].indirect(offsets[:]))
+        codes0 = keep.tile([P, S], U32, name="codes0", tag="plane6", align_bytes=64)
         scales0 = keep.tile([P, S], U8, name="scales0", align_bytes=64)
         nc.vector.quantize_mx(codes0[:].bitcast(FP8X4), scales0[:], woven0[:].rearrange("p n t -> p (n t)"))
         accs = []
@@ -131,19 +150,23 @@ def tile_picked_lnfold_silu_l_kernel(tc, xT, mean, inv, gsum, b, w1_words, w1_sc
             accs.append(acc)
 
         woven1 = [keep.tile([P, P, PACK], BF16, name="woven1_%d" % c, align_bytes=64) for c in range(BLOCKS)]
-        gather(4, 0, BLOCKS)
-        gather(5, 0, BLOCKS)
         for c in range(BLOCKS):
-            nc.scalar.copy(woven1[c][:, :, 0:2], pairs[2][:, :, c * P : (c + 1) * P].rearrange("p e n -> p n e"))
-        gather(6, 0, BLOCKS)
+            nc.scalar.copy(woven1[c][:, :, 0:2], pair[:, :, c * P : (c + 1) * P].rearrange("p e n -> p n e"))
 
         out_rows = out.rearrange("(p h) j -> p h j", h=HALVES)
 
+        def gather_last(c):
+            nc.vector.tensor_copy(
+                late[:, BLOCKS + c % 2, :],
+                planes[7][:].indirect(offsets[:, c * LIST_COLS : (c + 1) * LIST_COLS]),
+            )
+
         def weave(c):
-            nc.vector.tensor_copy(woven1[c][:, :, 2:4], pairs[3][:, :, c * P : (c + 1) * P].rearrange("p e n -> p n e"))
+            slot = BLOCKS + c % 2
+            nc.vector.tensor_copy(woven1[c][:, :, 2:4], late[:, c : slot + 1 : slot - c, :].rearrange("p e n -> p n e"))
 
         def finish(c):
-            codes = keep.tile([P, P], U32, name="codes1_%d" % c, align_bytes=64)
+            codes = keep.tile([P, P], U32, name="codes1_%d" % c, tag="shared%d" % (c - 2) if c >= 2 else "codes1_%d" % c, align_bytes=64)
             scales = keep.tile([P, P], U8, name="scales1_%d" % c, align_bytes=64)
             nc.vector.quantize_mx(codes[:].bitcast(FP8X4), scales[:], woven1[c][:].rearrange("p n t -> p (n t)"))
             nc.tensor.matmul_mx(
@@ -156,22 +179,20 @@ def tile_picked_lnfold_silu_l_kernel(tc, xT, mean, inv, gsum, b, w1_words, w1_sc
                 stop=True,
             )
             scaled = keep.tile([P, HALVES, P], F32, name="scaled%d" % c)
-            nc.scalar.activation(
-                scaled[:], accs[c][:].rearrange("j (p h) -> j h p", h=HALVES), ACT.Copy, scale=inv_col[:, c : c + 1]
-            )
+            by_half = accs[c][:].rearrange("j (p h) -> j h p", h=HALVES)
+            if c < 2:
+                nc.scalar.activation(scaled[:], by_half, ACT.Copy, scale=inv_col[c][:])
+            else:
+                nc.vector.tensor_scalar(scaled[:], by_half, inv_col[c][:], None, mybir.AluOpType.mult)
             for h in range(HALVES):
                 nc.tensor.matmul(
                     sums[c][:, h, :], scaled[:, h, :], ident[:], start=False, stop=(h == HALVES - 1), is_transpose=True
                 )
             result = keep.tile([P, HALVES, P], F32, name="result%d" % c)
-            for h in range(HALVES):
-                nc.scalar.activation(result[:, h, :], sums[c][:, h, :], ACT.Silu, bias=b_col[:, h : h + 1])
+            nc.scalar.activation(result[:], sums[c][:], ACT.Silu)
             nc.sync.dma_start(out_rows[:, :, c * P : (c + 1) * P], result[:])
 
-        for step in range(BLOCKS + 2):
-            if step < BLOCKS:
-                gather(7, step, step + 1)
-            if 1 <= step <= BLOCKS:
-                weave(step - 1)
-            if step >= 2:
-                finish(step - 2)
+        for first in range(0, BLOCKS, 2):
+            for stage in (gather_last, weave, finish):
+                stage(first)
+                stage(first + 1)

@@ -40,8 +40,8 @@ def tile_picked_lnfold_silu_l_kernel(tc, xT, mean, inv, gsum, b, w1_words, w1_sc
         nc.scalar.activation(warm_out[:], warm_in[:], ACT.Silu)
 
         stats = keep.tile([P, T], F32, name="stats")
-        nc.sync.dma_start(stats[0:STAT_ROWS, :], mean[0:STAT_ROWS, :])
-        nc.sync.dma_start(stats[STAT_ROWS : 2 * STAT_ROWS, :], inv[0:STAT_ROWS, :])
+        nc.sync.dma_start(stats[0 : 2 * STAT_ROWS : 2, :], mean[0:STAT_ROWS, :])
+        nc.sync.dma_start(stats[1 : 2 * STAT_ROWS : 2, :], inv[0:STAT_ROWS, :])
         nc.vector.memset(stats[32:64, :], 0.0)
         nc.gpsimd.memset(stats[64:P, :], 0.0)
 
@@ -103,8 +103,8 @@ def tile_picked_lnfold_silu_l_kernel(tc, xT, mean, inv, gsum, b, w1_words, w1_sc
         neg_inv = keep.tile([P, BLOCKS], F32, name="neg_inv")
         shift = keep.tile([P, BLOCKS], F32, name="shift")
         for c in range(BLOCKS):
-            nc.scalar.activation(inv_col[c][:], turned[:, c, STAT_ROWS : STAT_ROWS + 1], ACT.Copy)
-        nc.scalar.activation(neg_inv[:], turned[:, :, STAT_ROWS], ACT.Copy, scale=-1.0)
+            nc.scalar.activation(inv_col[c][:], turned[:, c, 1:2], ACT.Copy)
+        nc.scalar.activation(neg_inv[:], turned[:, :, 1], ACT.Copy, scale=-1.0)
         for c in range(BLOCKS):
             nc.scalar.activation(shift[:, c : c + 1], turned[:, c, 0:1], ACT.Copy, scale=neg_inv[:, c : c + 1])
         sums = []

@@ -14,6 +14,7 @@ U16 = mybir.dt.uint16
 U8 = mybir.dt.uint8
 FP8X4 = mybir.dt.float8_e4m3fn_x4
 ACT = mybir.ActivationFunctionType
+MULT = mybir.AluOpType.mult
 
 P = 128
 PACK = 4
@@ -22,7 +23,12 @@ PASSES = K // K_PASS
 BLOCKS = S // P
 HALVES = N // P
 LIST_COLS = P // 16
-STAT_ROWS = 16
+MEAN_ROW, INV_ROW = P - 2, P - 1
+
+LOADS = ((0, T),), ((0, T),), ((0, T // 2), (T // 2, T)), ((0, T // 2), (T // 2, T))
+VECTOR_SHARE = (640, 640, 0, 256)
+OVERLAP = 16
+SCALAR_WEAVES = 4
 
 
 def tile_picked_lnfold_silu_l_kernel(tc, xT, mean, inv, gsum, b, w1_words, w1_scales, offs, out):
@@ -40,150 +46,166 @@ def tile_picked_lnfold_silu_l_kernel(tc, xT, mean, inv, gsum, b, w1_words, w1_sc
         nc.scalar.activation(warm_out[:], warm_in[:], ACT.Silu)
 
         stats = keep.tile([P, T], F32, name="stats")
-        nc.sync.dma_start(stats[0 : 2 * STAT_ROWS : 2, :], mean[0:STAT_ROWS, :])
-        nc.sync.dma_start(stats[1 : 2 * STAT_ROWS : 2, :], inv[0:STAT_ROWS, :])
-        nc.vector.memset(stats[32:64, :], 0.0)
-        nc.gpsimd.memset(stats[64:P, :], 0.0)
+        nc.sync.dma_start(stats[MEAN_ROW : MEAN_ROW + 1, :], mean[0:1, :])
+        nc.sync.dma_start(stats[INV_ROW : INV_ROW + 1, :], inv[0:1, :])
+        nc.vector.memset(stats[0:MEAN_ROW, :], 0.0)
 
-        planes = [keep.tile([P, T], F32, name="plane%d" % i, align_bytes=64) for i in range(PASSES * PACK)]
-        w_codes = [keep.tile([P, N], U32, name="w_codes%d" % z, align_bytes=64) for z in range(PASSES)]
-
-        def load_plane(i):
-            z, t = divmod(i, PACK)
-            nc.sync.dma_start(planes[i][:], xT[K_PASS * z + t : K_PASS * (z + 1) : PACK, :])
-
-        def load_w(z):
-            nc.sync.dma_start(w_codes[z][:].bitcast(I32), w1_words[z].rearrange("p n t -> p (n t)").bitcast(I32))
-
-        w_scales = keep.tile([P, PASSES, N], U8, name="w_scales", align_bytes=64)
-        nc.vector.memset(w_scales[:].bitcast(I32), 0)
         g_col = keep.tile([P, HALVES], F32, name="g_col")
         b_col = keep.tile([P, HALVES], F32, name="b_col")
+        nc.sync.dma_start(g_col[:], gsum.rearrange("(p h) o -> p (h o)", h=HALVES))
+        nc.sync.dma_start(b_col[:], b.rearrange("(p h) o -> p (h o)", h=HALVES))
 
-        def load_w_scales(q):
+        chain = keep.tile([P, 3 * T - 2 * OVERLAP], U32, name="chain", align_bytes=64)
+        in_chain = {(2, T // 2): 0, (3, T // 2): 2 * (T - OVERLAP)}
+        raw = {}
+        for i, ranges in enumerate(LOADS):
+            z, u = divmod(i, 2)
+            rows = xT[K_PASS * z : K_PASS * (z + 1), :].rearrange("(p t) c -> p t c", t=PACK)[:, 2 * u : 2 * u + 2, :]
+            for lo, hi in ranges:
+                if (i, hi) in in_chain:
+                    at = in_chain[i, hi]
+                    raw[i, hi] = chain[:, at : at + T].bitcast(F32).rearrange("p (e c) -> p e c", e=2)
+                else:
+                    own = keep.tile([P, 2, hi - lo], F32, name="raw%d_%d" % (i, hi), align_bytes=64)
+                    raw[i, hi] = own[:]
+                nc.sync.dma_start(raw[i, hi], rows[:, :, lo:hi])
+
+        w_codes = keep.tile([P, PASSES, N], U32, name="w_codes", align_bytes=64)
+        nc.sync.dma_start(w_codes[:].bitcast(I32), w1_words.rearrange("z p n t -> p z (n t)").bitcast(I32))
+        w_scales = keep.tile([P, PASSES, N], U8, name="w_scales", align_bytes=64)
+        nc.gpsimd.memset(w_scales[:].bitcast(I32), 0)
+        for q in range(4):
             nc.sync.dma_start(
                 w_scales[32 * q : 32 * q + 4, :, :].bitcast(I32),
                 w1_scales[:, 4 * q : 4 * q + 4, :].rearrange("z r c -> r z c").bitcast(I32),
             )
 
-        for i in range(3):
-            load_plane(i)
-        nc.sync.dma_start(g_col[:], gsum.rearrange("(p h) o -> p (h o)", h=HALVES))
-        nc.sync.dma_start(b_col[:], b.rearrange("(p h) o -> p (h o)", h=HALVES))
-        for i in range(3, 7):
-            load_plane(i)
-            load_w_scales(i - 3)
-        load_plane(7)
-        load_w(0)
-        load_w(1)
-
         ident = keep.tile([P, P], F32, name="ident")
         make_identity(nc, ident[:])
 
-        flat0 = keep.tile([P, PACK, S], BF16, name="flat0")
-        pair = keep.tile([P, 2, S], BF16, name="pair")
-        rounded0 = keep.tile([P, T], BF16, name="rounded0")
-        nc.scalar.copy(rounded0[:], planes[0][:])
-        nc.scalar.activation(flat0[:, 0, :], rounded0[:].indirect(offsets[:]), ACT.Copy)
-
-        picked = keep.tile([P, S], F32, name="picked")
-        nc.vector.tensor_copy(picked[:], stats[:].indirect(offsets[:]))
-        turned = psum.tile([P, BLOCKS, P], F32, name="turned", tag="acc0")
-        for c in range(BLOCKS):
-            nc.tensor.transpose(turned[:, c, :], picked[:, c * P : (c + 1) * P], ident[:])
-        g_rows = psum.tile([P, HALVES, P], F32, name="g_rows", tag="acc1")
+        g_bank = psum.tile([P, HALVES, P], F32, name="g_bank", tag="acc1")
         for h in range(HALVES):
-            nc.tensor.transpose(g_rows[:, h, :], g_col[:, h : h + 1].to_broadcast([P, P]), ident[:])
+            nc.tensor.transpose(g_bank[:, h, :], g_col[:, h : h + 1].to_broadcast([P, P]), ident[:])
         b_bank = psum.tile([P, HALVES, P], F32, name="b_bank", tag="acc2")
         for h in range(HALVES):
             nc.tensor.transpose(b_bank[:, h, :], b_col[:, h : h + 1].to_broadcast([P, P]), ident[:])
+        window0 = keep.tile([P, T], U32, name="window0", align_bytes=64)
+        windows = [window0[:]]
         b_rows = keep.tile([P, HALVES, P], F32, name="b_rows")
         nc.scalar.copy(b_rows[:], b_bank[:])
-        inv_col = [keep.tile([P, 1], F32, name="inv_col%d" % c, tag="shared%d" % c, align_bytes=64) for c in range(BLOCKS)]
-        neg_inv = keep.tile([P, BLOCKS], F32, name="neg_inv")
-        shift = keep.tile([P, BLOCKS], F32, name="shift")
-        for c in range(BLOCKS):
-            nc.scalar.activation(inv_col[c][:], turned[:, c, 1:2], ACT.Copy)
-        nc.scalar.activation(neg_inv[:], turned[:, :, 1], ACT.Copy, scale=-1.0)
-        for c in range(BLOCKS):
-            nc.scalar.activation(shift[:, c : c + 1], turned[:, c, 0:1], ACT.Copy, scale=neg_inv[:, c : c + 1])
-        sums = []
-        for c in range(BLOCKS):
+        turned = []
+        for first, tag in ((0, "acc0"), (2, "acc3")):
+            picked = keep.tile([P, 2 * P], F32, name="picked%d" % first)
+            nc.vector.tensor_copy(picked[:], stats[:].indirect(offsets[:, first * LIST_COLS : (first + 2) * LIST_COLS]))
+            bank = psum.tile([P, 2, P], F32, name="turned%d" % first, tag=tag)
+            for c in range(2):
+                nc.tensor.transpose(bank[:, c, :], picked[:, c * P : (c + 1) * P], ident[:])
+            turned.append(bank)
+        inv_cols = [keep.tile([P, 2], F32, name="inv_cols%d" % j) for j in range(2)]
+        shift = keep.tile([P, 2], F32, name="shift")
+        neg_g_rows = windows[0][:, T - N : T].bitcast(F32).rearrange("p (h n) -> p h n", h=HALVES)
+        nc.vector.tensor_scalar(neg_g_rows, g_bank[:], -1.0, None, MULT)
+        nc.vector.tensor_copy(inv_cols[1][:], turned[1][:, :, INV_ROW])
+        nc.vector.scalar_tensor_tensor(shift[:], turned[1][:, :, MEAN_ROW], -1.0, inv_cols[1][:], MULT, MULT)
+
+        def lay_sum(c):
             term = keep.tile([P, HALVES, P], F32, name="term%d" % c)
-            nc.scalar.activation(term[:], g_rows[:], ACT.Copy, scale=shift[:, c : c + 1])
+            if c < 2:
+                nc.vector.tensor_scalar(term[:], neg_g_rows, turned[0][:, c, MEAN_ROW : MEAN_ROW + 1], turned[0][:, c, INV_ROW : INV_ROW + 1], MULT, MULT)
+            else:
+                nc.scalar.activation(term[:], g_bank[:], ACT.Copy, scale=shift[:, c - 2 : c - 1])
             bank = psum.tile([P, HALVES, P], F32, name="sum%d" % c)
             for h in range(HALVES):
                 nc.tensor.matmul(bank[:, h, :], b_rows[:, h, :], ident[:], start=(h == 0), stop=False, is_transpose=True)
             for h in range(HALVES):
                 nc.tensor.matmul(bank[:, h, :], term[:, h, :], ident[:], start=False, stop=False, is_transpose=True)
-            sums.append(bank)
+            return bank
 
+        def cast(i):
+            if i == 3:
+                windows.append(chain[:, T - OVERLAP : 2 * T - OVERLAP])
+            elif i > 0:
+                window = keep.tile([P, T], U32, name="window%d" % i, tag="raw%d_%d" % (i - 1, T), align_bytes=64)
+                windows.append(window[:])
 
-        def gather(i):
-            nc.vector.tensor_copy(flat0[:, i, :] if i < PACK else pair[:, i - PACK, :], planes[i][:].indirect(offsets[:]))
+            def words(lo, hi):
+                return windows[i][:, lo:hi].bitcast(BF16).rearrange("p (c e) -> p c e", e=2)
 
-        woven0 = keep.tile([P, S, PACK], BF16, name="woven0", align_bytes=64)
-        for i in range(1, PACK):
-            gather(i)
-        nc.scalar.copy(
-            woven0[:].rearrange("p (c i) t -> p c t i", i=4), flat0[:].rearrange("p t (c i) -> p c t i", i=4)
-        )
-        gather(4)
-        gather(5)
-        late = keep.tile([P, BLOCKS + 2, P], BF16, name="late")
-        nc.vector.tensor_copy(late[:, 0:BLOCKS, :].rearrange("p c n -> p (c n)"), planes[6][:].indirect(offsets[:]))
-        codes0 = keep.tile([P, S], U32, name="codes0", tag="plane6", align_bytes=64)
-        scales0 = keep.tile([P, S], U8, name="scales0", align_bytes=64)
-        nc.vector.quantize_mx(codes0[:].bitcast(FP8X4), scales0[:], woven0[:].rearrange("p n t -> p (n t)"))
-        accs = []
-        for c in range(BLOCKS):
-            acc = psum.tile([P, N], F32, name="y%d" % c, tag="acc%d" % c)
-            nc.tensor.matmul_mx(
-                acc[:],
-                lhsT=codes0[:, c * P : (c + 1) * P].bitcast(FP8X4),
-                lhsT_scale=scales0[:, c * P : (c + 1) * P],
-                rhs=w_codes[0][:].bitcast(FP8X4),
-                rhs_scale=w_scales[:, 0, :],
-                start=True,
-                stop=False,
-            )
-            accs.append(acc)
+            cut = T - VECTOR_SHARE[i]
+            for lo, hi in LOADS[i]:
+                end = min(hi, cut)
+                nc.scalar.copy(words(lo, end), raw[i, hi][:, :, 0 : end - lo].rearrange("p e c -> p c e"))
+            last = LOADS[i][-1][0]
+            if cut < T:
+                nc.vector.tensor_copy(words(cut, T), raw[i, T][:, :, cut - last :].rearrange("p e c -> p c e"))
 
-        woven1 = [keep.tile([P, P, PACK], BF16, name="woven1_%d" % c, align_bytes=64) for c in range(BLOCKS)]
-        for c in range(BLOCKS):
-            nc.scalar.copy(woven1[c][:, :, 0:2], pair[:, :, c * P : (c + 1) * P].rearrange("p e n -> p n e"))
-
-        out_rows = out.rearrange("(p h) j -> p h j", h=HALVES)
-
-        def gather_last(c):
+        def gather(i, flat, first, end):
             nc.vector.tensor_copy(
-                late[:, BLOCKS + c % 2, :],
-                planes[7][:].indirect(offsets[:, c * LIST_COLS : (c + 1) * LIST_COLS]),
+                flat[:, first:end, i % 2, :],
+                windows[i].indirect(offsets[:, first * LIST_COLS : end * LIST_COLS]),
             )
 
-        def weave(c):
-            slot = BLOCKS + c % 2
-            nc.vector.tensor_copy(woven1[c][:, :, 2:4], late[:, c : slot + 1 : slot - c, :].rearrange("p e n -> p n e"))
+        def weave(z, flat, first, end, on_scalar, tag):
+            woven = keep.tile([P, (end - first) * P * 2], U32, name="woven%d_%d" % (z, first), tag=tag, align_bytes=64)
+            if on_scalar:
+                nc.scalar.copy(
+                    woven[:].rearrange("p (c n u) -> p c n u", n=P, u=2),
+                    flat[:, first:end, :, :].rearrange("p c u n -> p c n u"),
+                )
+            else:
+                nc.vector.tensor_copy(
+                    woven[:].bitcast(I32).rearrange("p (c n u) -> p c n u", n=P, u=2),
+                    flat[:, first:end, :, :].bitcast(I32).rearrange("p c u n -> p c n u"),
+                )
+            return woven
 
-        def finish(c):
-            codes = keep.tile([P, P], U32, name="codes1_%d" % c, tag="shared%d" % (c - 2) if c >= 2 else "codes1_%d" % c, align_bytes=64)
-            scales = keep.tile([P, P], U8, name="scales1_%d" % c, align_bytes=64)
-            nc.vector.quantize_mx(codes[:].bitcast(FP8X4), scales[:], woven1[c][:].rearrange("p n t -> p (n t)"))
+        def quantize(z, first, end, woven):
+            codes = keep.tile([P, (end - first) * P], U32, name="codes%d_%d" % (z, first), align_bytes=64)
+            scales = keep.tile([P, (end - first) * P], U8, name="scales%d_%d" % (z, first), align_bytes=64)
+            nc.vector.quantize_mx(codes[:].bitcast(FP8X4), scales[:], woven[:].bitcast(BF16))
+            return codes, scales
+
+        def multiply(z, c, first, codes, scales):
+            cols = slice((c - first) * P, (c - first + 1) * P)
             nc.tensor.matmul_mx(
                 accs[c][:],
-                lhsT=codes[:].bitcast(FP8X4),
-                lhsT_scale=scales[:],
-                rhs=w_codes[1][:].bitcast(FP8X4),
-                rhs_scale=w_scales[:, 1, :],
-                start=False,
-                stop=True,
+                lhsT=codes[:, cols].bitcast(FP8X4),
+                lhsT_scale=scales[:, cols],
+                rhs=w_codes[:, z, :].bitcast(FP8X4),
+                rhs_scale=w_scales[:, z, :],
+                start=(z == 0),
+                stop=(z == PASSES - 1),
             )
+
+        flat0 = keep.tile([P, BLOCKS, 2, P], U32, name="flat0", align_bytes=64)
+        sums = [lay_sum(c) for c in range(BLOCKS)]
+        cast(0)
+        nc.scalar.copy(inv_cols[0][:], turned[0][:, :, INV_ROW])
+        gather(0, flat0, 0, BLOCKS - 1)
+        cast(1)
+        gather(0, flat0, BLOCKS - 1, BLOCKS)
+        gather(1, flat0, 0, 2)
+        gather(1, flat0, 2, BLOCKS)
+        accs = [psum.tile([P, N], F32, name="y%d" % c, tag="acc%d" % c) for c in range(BLOCKS)]
+        woven0 = [weave(0, flat0, first, first + 2, False, "reused%d" % first) for first in (0, 2)]
+        cast(2)
+        for first in (0, 2):
+            codes, scales = quantize(0, first, first + 2, woven0[first // 2])
+            for c in range(first, first + 2):
+                multiply(0, c, first, codes, scales)
+        flat1 = keep.tile([P, BLOCKS, 2, P], U32, name="flat1", align_bytes=64)
+        gather(2, flat1, 0, BLOCKS - 1)
+        cast(3)
+        gather(2, flat1, BLOCKS - 1, BLOCKS)
+        out_rows = out.rearrange("(p h) j -> p h j", h=HALVES)
+
+        def finish(c):
             scaled = keep.tile([P, HALVES, P], F32, name="scaled%d" % c)
             by_half = accs[c][:].rearrange("j (p h) -> j h p", h=HALVES)
-            if c < 2:
-                nc.scalar.activation(scaled[:], by_half, ACT.Copy, scale=inv_col[c][:])
+            if c == 0:
+                nc.scalar.activation(scaled[:], by_half, ACT.Copy, scale=inv_cols[c // 2][:, c % 2 : c % 2 + 1])
             else:
-                nc.vector.tensor_scalar(scaled[:], by_half, inv_col[c][:], None, mybir.AluOpType.mult)
+                nc.vector.tensor_scalar(scaled[:], by_half, inv_cols[c // 2][:, c % 2 : c % 2 + 1], None, MULT)
             for h in range(HALVES):
                 nc.tensor.matmul(
                     sums[c][:, h, :], scaled[:, h, :], ident[:], start=False, stop=(h == HALVES - 1), is_transpose=True
@@ -192,7 +214,12 @@ def tile_picked_lnfold_silu_l_kernel(tc, xT, mean, inv, gsum, b, w1_words, w1_sc
             nc.scalar.activation(result[:], sums[c][:], ACT.Silu)
             nc.sync.dma_start(out_rows[:, :, c * P : (c + 1) * P], result[:])
 
-        for first in range(0, BLOCKS, 2):
-            for stage in (gather_last, weave, finish):
-                stage(first)
-                stage(first + 1)
+        woven1 = []
+        for c in range(BLOCKS):
+            gather(3, flat1, c, c + 1)
+            woven1.append(weave(1, flat1, c, c + 1, c < SCALAR_WEAVES, "woven1_%d" % c))
+        for c in range(BLOCKS):
+            codes, scales = quantize(1, c, c + 1, woven1[c])
+            multiply(1, c, c, codes, scales)
+        for c in range(BLOCKS):
+            finish(c)

@@ -52,8 +52,8 @@ def tile_picked_lnfold_silu_l_kernel(tc, xT, mean, inv, gsum, b, w1_words, w1_sc
 
         g_col = keep.tile([P, HALVES], F32, name="g_col")
         b_col = keep.tile([P, HALVES], F32, name="b_col")
-        nc.sync.dma_start(g_col[:], gsum.rearrange("(p h) o -> p (h o)", h=HALVES))
-        nc.sync.dma_start(b_col[:], b.rearrange("(p h) o -> p (h o)", h=HALVES))
+        nc.scalar.dma_start(g_col[:], gsum.rearrange("(p h) o -> p (h o)", h=HALVES))
+        nc.scalar.dma_start(b_col[:], b.rearrange("(p h) o -> p (h o)", h=HALVES))
 
         chain = keep.tile([P, 3 * T - 2 * OVERLAP], U32, name="chain", align_bytes=64)
         in_chain = {(2, T // 2): 0, (3, T // 2): 2 * (T - OVERLAP)}

@@ -26,7 +26,7 @@ LIST_COLS = P // 16
 MEAN_ROW, INV_ROW = P - 2, P - 1
 
 LOADS = ((0, T),), ((0, T),), ((0, T // 2), (T // 2, T)), ((0, T // 2), (T // 2, T))
-VECTOR_SHARE = (640, 640, 0, 256)
+VECTOR_SHARE = (672, 640, 0, 192)
 OVERLAP = 16
 SCALAR_WEAVES = 4
 
@@ -103,8 +103,8 @@ def tile_picked_lnfold_silu_l_kernel(tc, xT, mean, inv, gsum, b, w1_words, w1_sc
             turned.append(bank)
         inv_cols = [keep.tile([P, 2], F32, name="inv_cols%d" % j) for j in range(2)]
         shift = keep.tile([P, 2], F32, name="shift")
-        neg_g_rows = windows[0][:, T - N : T].bitcast(F32).rearrange("p (h n) -> p h n", h=HALVES)
-        nc.vector.tensor_scalar(neg_g_rows, g_bank[:], -1.0, None, MULT)
+        neg_g_rows = windows[0][:, N : 2 * N].bitcast(F32).rearrange("p (h n) -> p h n", h=HALVES)
+        nc.scalar.activation(neg_g_rows, g_bank[:], ACT.Copy, scale=-1.0)
         nc.vector.tensor_copy(inv_cols[1][:], turned[1][:, :, INV_ROW])
         nc.vector.scalar_tensor_tensor(shift[:], turned[1][:, :, MEAN_ROW], -1.0, inv_cols[1][:], MULT, MULT)
 
@@ -194,25 +194,34 @@ def tile_picked_lnfold_silu_l_kernel(tc, xT, mean, inv, gsum, b, w1_words, w1_sc
             for c in range(first, first + 2):
                 multiply(0, c, first, codes, scales)
         flat1 = keep.tile([P, BLOCKS, 2, P], U32, name="flat1", align_bytes=64)
-        gather(2, flat1, 0, BLOCKS - 1)
+        gather(2, flat1, 0, BLOCKS)
         cast(3)
-        gather(2, flat1, BLOCKS - 1, BLOCKS)
         out_rows = out.rearrange("(p h) j -> p h j", h=HALVES)
 
         def finish(c):
-            scaled = keep.tile([P, HALVES, P], F32, name="scaled%d" % c)
             by_half = accs[c][:].rearrange("j (p h) -> j h p", h=HALVES)
-            if c == 0:
-                nc.scalar.activation(scaled[:], by_half, ACT.Copy, scale=inv_cols[c // 2][:, c % 2 : c % 2 + 1])
-            else:
-                nc.vector.tensor_scalar(scaled[:], by_half, inv_cols[c // 2][:, c % 2 : c % 2 + 1], None, MULT)
-            for h in range(HALVES):
-                nc.tensor.matmul(
-                    sums[c][:, h, :], scaled[:, h, :], ident[:], start=False, stop=(h == HALVES - 1), is_transpose=True
-                )
+            factor = inv_cols[c // 2][:, c % 2 : c % 2 + 1]
+            step = 1 if c in (0, BLOCKS - 1) else HALVES
+            for first in range(0, HALVES, step):
+                scaled = keep.tile([P, step, P], F32, name="scaled%d_%d" % (c, first))
+                if c == 0:
+                    nc.scalar.activation(scaled[:], by_half[:, first : first + step, :], ACT.Copy, scale=factor)
+                else:
+                    nc.vector.tensor_scalar(scaled[:], by_half[:, first : first + step, :], factor, None, MULT)
+                for h in range(first, first + step):
+                    nc.tensor.matmul(
+                        sums[c][:, h, :],
+                        scaled[:, h - first, :],
+                        ident[:],
+                        start=False,
+                        stop=(h == HALVES - 1),
+                        is_transpose=True,
+                    )
             result = keep.tile([P, HALVES, P], F32, name="result%d" % c)
-            nc.scalar.activation(result[:], sums[c][:], ACT.Silu)
-            nc.sync.dma_start(out_rows[:, :, c * P : (c + 1) * P], result[:])
+            step = 1 if c == BLOCKS - 1 else HALVES
+            for h in range(0, HALVES, step):
+                nc.scalar.activation(result[:, h : h + step, :], sums[c][:, h : h + step, :], ACT.Silu)
+                nc.sync.dma_start(out_rows[:, h : h + step, c * P : (c + 1) * P], result[:, h : h + step, :])
 
         woven1 = []
         for c in range(BLOCKS):

@@ -25,9 +25,8 @@ HALVES = N // P
 LIST_COLS = P // 16
 MEAN_ROW, INV_ROW = P - 2, P - 1
 
-LOADS = ((0, T),), ((0, T),), ((0, T // 2), (T // 2, T)), ((0, T // 2), (T // 2, T))
-VECTOR_SHARE = (672, 640, 0, 192)
-OVERLAP = 16
+LOADS = ((0, T),), ((0, T),), ((0, T),), ((0, T // 2), (T // 2, T))
+VECTOR_SHARE = (672, 640, 256, 320)
 SCALAR_WEAVES = 4
 
 
@@ -55,20 +54,20 @@ def tile_picked_lnfold_silu_l_kernel(tc, xT, mean, inv, gsum, b, w1_words, w1_sc
         nc.scalar.dma_start(g_col[:], gsum.rearrange("(p h) o -> p (h o)", h=HALVES))
         nc.scalar.dma_start(b_col[:], b.rearrange("(p h) o -> p (h o)", h=HALVES))
 
-        chain = keep.tile([P, 3 * T - 2 * OVERLAP], U32, name="chain", align_bytes=64)
-        in_chain = {(2, T // 2): 0, (3, T // 2): 2 * (T - OVERLAP)}
         raw = {}
         for i, ranges in enumerate(LOADS):
             z, u = divmod(i, 2)
             rows = xT[K_PASS * z : K_PASS * (z + 1), :].rearrange("(p t) c -> p t c", t=PACK)[:, 2 * u : 2 * u + 2, :]
             for lo, hi in ranges:
-                if (i, hi) in in_chain:
-                    at = in_chain[i, hi]
-                    raw[i, hi] = chain[:, at : at + T].bitcast(F32).rearrange("p (e c) -> p e c", e=2)
+                own = keep.tile([P, 2, hi - lo], F32, name="raw%d_%d" % (i, hi), align_bytes=64)
+                raw[i, hi] = own[:]
+                if i == 2:
+                    for part in (slice(0, 3 * T // 2), slice(3 * T // 2, 2 * T)):
+                        nc.sync.dma_start(
+                            own[:].rearrange("p e c -> p (e c)")[:, part], rows.rearrange("p e c -> p (e c)")[:, part]
+                        )
                 else:
-                    own = keep.tile([P, 2, hi - lo], F32, name="raw%d_%d" % (i, hi), align_bytes=64)
-                    raw[i, hi] = own[:]
-                nc.sync.dma_start(raw[i, hi], rows[:, :, lo:hi])
+                    nc.sync.dma_start(own[:], rows[:, :, lo:hi])
 
         w_codes = keep.tile([P, PASSES, N], U32, name="w_codes", align_bytes=64)
         nc.sync.dma_start(w_codes[:].bitcast(I32), w1_words.rearrange("z p n t -> p z (n t)").bitcast(I32))
@@ -123,7 +122,7 @@ def tile_picked_lnfold_silu_l_kernel(tc, xT, mean, inv, gsum, b, w1_words, w1_sc
 
         def cast(i):
             if i == 3:
-                windows.append(chain[:, T - OVERLAP : 2 * T - OVERLAP])
+                windows.append(raw[2, T].rearrange("p e c -> p (e c)")[:, 3 * T // 4 : 7 * T // 4].bitcast(U32))
             elif i > 0:
                 window = keep.tile([P, T], U32, name="window%d" % i, tag="raw%d_%d" % (i - 1, T), align_bytes=64)
                 windows.append(window[:])
@@ -131,13 +130,18 @@ def tile_picked_lnfold_silu_l_kernel(tc, xT, mean, inv, gsum, b, w1_words, w1_sc
             def words(lo, hi):
                 return windows[i][:, lo:hi].bitcast(BF16).rearrange("p (c e) -> p c e", e=2)
 
+            if i == 2:
+                mid = T // 2 + VECTOR_SHARE[i]
+                for lo, hi in ((0, T // 2), (mid, T)):
+                    nc.scalar.copy(words(lo, hi), raw[i, T][:, :, lo:hi].rearrange("p e c -> p c e"))
+                nc.vector.tensor_copy(words(T // 2, mid), raw[i, T][:, :, T // 2 : mid].rearrange("p e c -> p c e"))
+                return
             cut = T - VECTOR_SHARE[i]
             for lo, hi in LOADS[i]:
                 end = min(hi, cut)
                 nc.scalar.copy(words(lo, end), raw[i, hi][:, :, 0 : end - lo].rearrange("p e c -> p c e"))
             last = LOADS[i][-1][0]
-            if cut < T:
-                nc.vector.tensor_copy(words(cut, T), raw[i, T][:, :, cut - last :].rearrange("p e c -> p c e"))
+            nc.vector.tensor_copy(words(cut, T), raw[i, T][:, :, cut - last :].rearrange("p e c -> p c e"))
 
         def gather(i, flat, first, end):
             nc.vector.tensor_copy(

@@ -24,10 +24,9 @@ BLOCKS = S // P
 HALVES = N // P
 LIST_COLS = P // 16
 MEAN_ROW, INV_ROW = P - 2, P - 1
+HALF = T // 2
 
-LOADS = ((0, T),), ((0, T),), ((0, T),), ((0, T // 2), (T // 2, T))
-VECTOR_SHARE = (672, 640, 256, 320)
-SCALAR_WEAVES = 4
+CUTS = (480, 512, 352, 768)
 
 
 def tile_picked_lnfold_silu_l_kernel(tc, xT, mean, inv, gsum, b, w1_words, w1_scales, offs, out):
@@ -35,6 +34,17 @@ def tile_picked_lnfold_silu_l_kernel(tc, xT, mean, inv, gsum, b, w1_words, w1_sc
     with ExitStack() as ctx:
         keep = ctx.enter_context(tc.tile_pool(name="keep", bufs=1))
         psum = ctx.enter_context(tc.psum_pool(name="psum", bufs=1))
+
+        def pair_rows(i):
+            z, u = divmod(i, 2)
+            return xT[K_PASS * z : K_PASS * (z + 1), :].rearrange("(p t) c -> p t c", t=PACK)[:, 2 * u : 2 * u + 2, :]
+
+        def load_run(i, lo, hi):
+            nc.sync.dma_start(room[i][:, lo:hi], pair_rows(i).rearrange("p e c -> p (e c)")[:, lo:hi])
+
+        room = [keep.tile([P, 2 * T], F32, name="raw%d" % i, align_bytes=64) for i in range(3)]
+        raw = [room[i][:, 0 : 2 * T].rearrange("p (e c) -> p e c", e=2) for i in range(3)]
+        load_run(0, 0, T // 4)
 
         offsets = keep.tile([P, S // 16], U16, name="offsets")
         nc.sync.dma_start(offsets[:], offs)
@@ -44,30 +54,23 @@ def tile_picked_lnfold_silu_l_kernel(tc, xT, mean, inv, gsum, b, w1_words, w1_sc
         nc.vector.memset(warm_in[:], 0.0)
         nc.scalar.activation(warm_out[:], warm_in[:], ACT.Silu)
 
-        stats = keep.tile([P, T], F32, name="stats")
-        nc.sync.dma_start(stats[MEAN_ROW : MEAN_ROW + 1, :], mean[0:1, :])
-        nc.sync.dma_start(stats[INV_ROW : INV_ROW + 1, :], inv[0:1, :])
+        stats = keep.tile([P, T], F32, name="stats", align_bytes=64)
+        nc.scalar.dma_start(stats[MEAN_ROW : MEAN_ROW + 1, :], mean[0:1, :])
+        nc.scalar.dma_start(stats[INV_ROW : INV_ROW + 1, :], inv[0:1, :])
         nc.vector.memset(stats[0:MEAN_ROW, :], 0.0)
 
         g_col = keep.tile([P, HALVES], F32, name="g_col")
         b_col = keep.tile([P, HALVES], F32, name="b_col")
-        nc.scalar.dma_start(g_col[:], gsum.rearrange("(p h) o -> p (h o)", h=HALVES))
-        nc.scalar.dma_start(b_col[:], b.rearrange("(p h) o -> p (h o)", h=HALVES))
-
-        raw = {}
-        for i, ranges in enumerate(LOADS):
-            z, u = divmod(i, 2)
-            rows = xT[K_PASS * z : K_PASS * (z + 1), :].rearrange("(p t) c -> p t c", t=PACK)[:, 2 * u : 2 * u + 2, :]
-            for lo, hi in ranges:
-                own = keep.tile([P, 2, hi - lo], F32, name="raw%d_%d" % (i, hi), align_bytes=64)
-                raw[i, hi] = own[:]
-                if i == 2:
-                    for part in (slice(0, 3 * T // 2), slice(3 * T // 2, 2 * T)):
-                        nc.sync.dma_start(
-                            own[:].rearrange("p e c -> p (e c)")[:, part], rows.rearrange("p e c -> p (e c)")[:, part]
-                        )
-                else:
-                    nc.sync.dma_start(own[:], rows[:, :, lo:hi])
+        nc.sync.dma_start(b_col[:], b.rearrange("(p h) o -> p (h o)", h=HALVES))
+        load_run(0, T // 4, 3 * HALF)
+        nc.sync.dma_start(g_col[:], gsum.rearrange("(p h) o -> p (h o)", h=HALVES))
+        load_run(0, 3 * HALF, 2 * T)
+        for i in (1, 2):
+            load_run(i, 0, 3 * HALF)
+            load_run(i, 3 * HALF, 2 * T)
+        last = [keep.tile([P, 2, HALF], F32, name="last%d" % j, align_bytes=64) for j in range(2)]
+        for j in range(2):
+            nc.sync.dma_start(last[j][:], pair_rows(3)[:, :, j * HALF : (j + 1) * HALF])
 
         w_codes = keep.tile([P, PASSES, N], U32, name="w_codes", align_bytes=64)
         nc.sync.dma_start(w_codes[:].bitcast(I32), w1_words.rearrange("z p n t -> p z (n t)").bitcast(I32))
@@ -82,37 +85,37 @@ def tile_picked_lnfold_silu_l_kernel(tc, xT, mean, inv, gsum, b, w1_words, w1_sc
         ident = keep.tile([P, P], F32, name="ident")
         make_identity(nc, ident[:])
 
-        g_bank = psum.tile([P, HALVES, P], F32, name="g_bank", tag="acc1")
-        for h in range(HALVES):
-            nc.tensor.transpose(g_bank[:, h, :], g_col[:, h : h + 1].to_broadcast([P, P]), ident[:])
         b_bank = psum.tile([P, HALVES, P], F32, name="b_bank", tag="acc2")
         for h in range(HALVES):
             nc.tensor.transpose(b_bank[:, h, :], b_col[:, h : h + 1].to_broadcast([P, P]), ident[:])
-        window0 = keep.tile([P, T], U32, name="window0", align_bytes=64)
-        windows = [window0[:]]
         b_rows = keep.tile([P, HALVES, P], F32, name="b_rows")
         nc.scalar.copy(b_rows[:], b_bank[:])
         turned = []
-        for first, tag in ((0, "acc0"), (2, "acc3")):
-            picked = keep.tile([P, 2 * P], F32, name="picked%d" % first)
-            nc.vector.tensor_copy(picked[:], stats[:].indirect(offsets[:, first * LIST_COLS : (first + 2) * LIST_COLS]))
-            bank = psum.tile([P, 2, P], F32, name="turned%d" % first, tag=tag)
+        for j, tag in enumerate(("acc0", "acc3")):
+            picked = keep.tile([P, 2 * P], F32, name="picked%d" % j, align_bytes=64)
+            nc.vector.tensor_copy(picked[:], stats[:].indirect(offsets[:, 2 * j * LIST_COLS : (2 * j + 2) * LIST_COLS]))
+            bank = psum.tile([P, 2, P], F32, name="turned%d" % j, tag=tag)
             for c in range(2):
                 nc.tensor.transpose(bank[:, c, :], picked[:, c * P : (c + 1) * P], ident[:])
             turned.append(bank)
-        inv_cols = [keep.tile([P, 2], F32, name="inv_cols%d" % j) for j in range(2)]
-        shift = keep.tile([P, 2], F32, name="shift")
-        neg_g_rows = windows[0][:, N : 2 * N].bitcast(F32).rearrange("p (h n) -> p h n", h=HALVES)
-        nc.scalar.activation(neg_g_rows, g_bank[:], ACT.Copy, scale=-1.0)
-        nc.vector.tensor_copy(inv_cols[1][:], turned[1][:, :, INV_ROW])
-        nc.vector.scalar_tensor_tensor(shift[:], turned[1][:, :, MEAN_ROW], -1.0, inv_cols[1][:], MULT, MULT)
+        g_bank = psum.tile([P, HALVES, P], F32, name="g_bank", tag="acc1")
+        for h in range(HALVES):
+            nc.tensor.transpose(g_bank[:, h, :], g_col[:, h : h + 1].to_broadcast([P, P]), ident[:])
+        inv_cols = keep.tile([P, BLOCKS], F32, name="inv_cols")
+
+        def make_shift(c):
+            shift = keep.tile([P, 1], F32, name="shift%d" % c)
+            row = turned[c // 2][:, c % 2, :]
+            nc.vector.tensor_scalar(shift[:], row[:, MEAN_ROW : MEAN_ROW + 1], row[:, INV_ROW : INV_ROW + 1], -1.0, MULT, MULT)
+            return shift
+
+        def make_term(c):
+            term = keep.tile([P, HALVES, P], F32, name="term%d" % c)
+            nc.scalar.activation(term[:], g_bank[:], ACT.Copy, scale=shifts[c][:])
+            return term
 
         def lay_sum(c):
-            term = keep.tile([P, HALVES, P], F32, name="term%d" % c)
-            if c < 2:
-                nc.vector.tensor_scalar(term[:], neg_g_rows, turned[0][:, c, MEAN_ROW : MEAN_ROW + 1], turned[0][:, c, INV_ROW : INV_ROW + 1], MULT, MULT)
-            else:
-                nc.scalar.activation(term[:], g_bank[:], ACT.Copy, scale=shift[:, c - 2 : c - 1])
+            term = terms[c]
             bank = psum.tile([P, HALVES, P], F32, name="sum%d" % c)
             for h in range(HALVES):
                 nc.tensor.matmul(bank[:, h, :], b_rows[:, h, :], ident[:], start=(h == 0), stop=False, is_transpose=True)
@@ -120,91 +123,90 @@ def tile_picked_lnfold_silu_l_kernel(tc, xT, mean, inv, gsum, b, w1_words, w1_sc
                 nc.tensor.matmul(bank[:, h, :], term[:, h, :], ident[:], start=False, stop=False, is_transpose=True)
             return bank
 
-        def cast(i):
-            if i == 3:
-                windows.append(raw[2, T].rearrange("p e c -> p (e c)")[:, 3 * T // 4 : 7 * T // 4].bitcast(U32))
-            elif i > 0:
-                window = keep.tile([P, T], U32, name="window%d" % i, tag="raw%d_%d" % (i - 1, T), align_bytes=64)
-                windows.append(window[:])
+        def words(window, lo, hi):
+            return window[:, lo:hi].bitcast(BF16).rearrange("p (c e) -> p c e", e=2)
 
-            def words(lo, hi):
-                return windows[i][:, lo:hi].bitcast(BF16).rearrange("p (c e) -> p c e", e=2)
-
-            if i == 2:
-                mid = T // 2 + VECTOR_SHARE[i]
-                for lo, hi in ((0, T // 2), (mid, T)):
-                    nc.scalar.copy(words(lo, hi), raw[i, T][:, :, lo:hi].rearrange("p e c -> p c e"))
-                nc.vector.tensor_copy(words(T // 2, mid), raw[i, T][:, :, T // 2 : mid].rearrange("p e c -> p c e"))
-                return
-            cut = T - VECTOR_SHARE[i]
-            for lo, hi in LOADS[i]:
-                end = min(hi, cut)
-                nc.scalar.copy(words(lo, end), raw[i, hi][:, :, 0 : end - lo].rearrange("p e c -> p c e"))
-            last = LOADS[i][-1][0]
-            nc.vector.tensor_copy(words(cut, T), raw[i, T][:, :, cut - last :].rearrange("p e c -> p c e"))
-
-        def gather(i, flat, first, end):
-            nc.vector.tensor_copy(
-                flat[:, first:end, i % 2, :],
-                windows[i].indirect(offsets[:, first * LIST_COLS : end * LIST_COLS]),
-            )
-
-        def weave(z, flat, first, end, on_scalar, tag):
-            woven = keep.tile([P, (end - first) * P * 2], U32, name="woven%d_%d" % (z, first), tag=tag, align_bytes=64)
+        def cast(window, src, first, lo, hi, on_scalar):
+            piece = src[:, :, lo - first : hi - first].rearrange("p e c -> p c e")
             if on_scalar:
-                nc.scalar.copy(
-                    woven[:].rearrange("p (c n u) -> p c n u", n=P, u=2),
-                    flat[:, first:end, :, :].rearrange("p c u n -> p c n u"),
-                )
+                nc.scalar.copy(words(window, lo, hi), piece)
+            else:
+                nc.vector.tensor_copy(words(window, lo, hi), piece)
+
+        def gather(dst, window, first, end):
+            nc.vector.tensor_copy(dst, window.indirect(offsets[:, first * LIST_COLS : end * LIST_COLS]))
+
+        def weave(name, src, on_scalar):
+            blocks = src.shape[1]
+            woven = keep.tile([P, blocks * P * 2], U32, name=name, align_bytes=64)
+            if on_scalar:
+                nc.scalar.copy(woven[:].rearrange("p (c n u) -> p c n u", n=P, u=2), src.rearrange("p c u n -> p c n u"))
             else:
                 nc.vector.tensor_copy(
                     woven[:].bitcast(I32).rearrange("p (c n u) -> p c n u", n=P, u=2),
-                    flat[:, first:end, :, :].bitcast(I32).rearrange("p c u n -> p c n u"),
+                    src.bitcast(I32).rearrange("p c u n -> p c n u"),
                 )
             return woven
 
-        def quantize(z, first, end, woven):
+        def quantize_multiply(z, first, end, woven):
             codes = keep.tile([P, (end - first) * P], U32, name="codes%d_%d" % (z, first), align_bytes=64)
             scales = keep.tile([P, (end - first) * P], U8, name="scales%d_%d" % (z, first), align_bytes=64)
             nc.vector.quantize_mx(codes[:].bitcast(FP8X4), scales[:], woven[:].bitcast(BF16))
-            return codes, scales
-
-        def multiply(z, c, first, codes, scales):
-            cols = slice((c - first) * P, (c - first + 1) * P)
-            nc.tensor.matmul_mx(
-                accs[c][:],
-                lhsT=codes[:, cols].bitcast(FP8X4),
-                lhsT_scale=scales[:, cols],
-                rhs=w_codes[:, z, :].bitcast(FP8X4),
-                rhs_scale=w_scales[:, z, :],
-                start=(z == 0),
-                stop=(z == PASSES - 1),
-            )
+            for c in range(first, end):
+                cols = slice((c - first) * P, (c - first + 1) * P)
+                nc.tensor.matmul_mx(
+                    accs[c][:],
+                    lhsT=codes[:, cols].bitcast(FP8X4),
+                    lhsT_scale=scales[:, cols],
+                    rhs=w_codes[:, z, :].bitcast(FP8X4),
+                    rhs_scale=w_scales[:, z, :],
+                    start=(z == 0),
+                    stop=(z == PASSES - 1),
+                )
 
         flat0 = keep.tile([P, BLOCKS, 2, P], U32, name="flat0", align_bytes=64)
+        shifts = [make_shift(0), make_shift(1)]
+        window0 = keep.tile([P, T], U32, name="window0", tag="picked0", align_bytes=64)
+        window = window0[:]
+        cast(window, raw[0], 0, 0, CUTS[0], True)
+        cast(window, raw[0], 0, CUTS[0], T, False)
+        shifts.extend([make_shift(2), make_shift(3)])
+        terms = [make_term(0), make_term(1)]
+        gather(flat0[:, :, 0, :], window, 0, BLOCKS)
+        window1 = keep.tile([P, T], U32, name="window1", tag="raw0", align_bytes=64)
+        window = window1[:]
+        cast(window, raw[1], 0, 0, CUTS[1], True)
+        cast(window, raw[1], 0, CUTS[1], T, False)
+        gather(flat0[:, 0:2, 1, :], window, 0, 2)
+        gather(flat0[:, 2:4, 1, :], window, 2, 4)
+        terms.extend([make_term(2), make_term(3)])
+        for j in range(2):
+            nc.scalar.copy(inv_cols[:, 2 * j : 2 * j + 2], turned[j][:, :, INV_ROW])
         sums = [lay_sum(c) for c in range(BLOCKS)]
-        cast(0)
-        nc.scalar.copy(inv_cols[0][:], turned[0][:, :, INV_ROW])
-        gather(0, flat0, 0, BLOCKS - 1)
-        cast(1)
-        gather(0, flat0, BLOCKS - 1, BLOCKS)
-        gather(1, flat0, 0, 2)
-        gather(1, flat0, 2, BLOCKS)
         accs = [psum.tile([P, N], F32, name="y%d" % c, tag="acc%d" % c) for c in range(BLOCKS)]
-        woven0 = [weave(0, flat0, first, first + 2, False, "reused%d" % first) for first in (0, 2)]
-        cast(2)
-        for first in (0, 2):
-            codes, scales = quantize(0, first, first + 2, woven0[first // 2])
-            for c in range(first, first + 2):
-                multiply(0, c, first, codes, scales)
-        flat1 = keep.tile([P, BLOCKS, 2, P], U32, name="flat1", align_bytes=64)
-        gather(2, flat1, 0, BLOCKS)
-        cast(3)
+        window2 = keep.tile([P, T], U32, name="window2", tag="raw1", align_bytes=64)
+        window = window2[:]
+        cast(window, raw[2], 0, 0, CUTS[2], True)
+        cast(window, raw[2], 0, CUTS[2], HALF, False)
+        cast(window, raw[2], 0, HALF, T, False)
+        woven0a = weave("woven0a", flat0[:, 0:2, :, :], True)
+        woven0b = weave("woven0b", flat0[:, 2:4, :, :], True)
+        flat1 = keep.tile([P, 2 * BLOCKS, P], U32, name="flat1", align_bytes=64)
+        gather(flat1[:, 0:BLOCKS, :], window, 0, BLOCKS)
+        quantize_multiply(0, 0, 2, woven0a)
+        quantize_multiply(0, 2, 4, woven0b)
+
+        window3 = keep.tile([P, T], U32, name="window3", tag="flat0", align_bytes=64)
+        window = window3[:]
+        cast(window, last[0], 0, 0, HALF, True)
+        cast(window, last[1], HALF, HALF, CUTS[3], True)
+        cast(window, last[1], HALF, CUTS[3], T, False)
+
         out_rows = out.rearrange("(p h) j -> p h j", h=HALVES)
 
         def finish(c):
             by_half = accs[c][:].rearrange("j (p h) -> j h p", h=HALVES)
-            factor = inv_cols[c // 2][:, c % 2 : c % 2 + 1]
+            factor = inv_cols[:, c : c + 1]
             step = 1 if c in (0, BLOCKS - 1) else HALVES
             for first in range(0, HALVES, step):
                 scaled = keep.tile([P, step, P], F32, name="scaled%d_%d" % (c, first))
@@ -221,18 +223,23 @@ def tile_picked_lnfold_silu_l_kernel(tc, xT, mean, inv, gsum, b, w1_words, w1_sc
                         stop=(h == HALVES - 1),
                         is_transpose=True,
                     )
+
+        def leave(c):
             result = keep.tile([P, HALVES, P], F32, name="result%d" % c)
             step = 1 if c == BLOCKS - 1 else HALVES
             for h in range(0, HALVES, step):
                 nc.scalar.activation(result[:, h : h + step, :], sums[c][:, h : h + step, :], ACT.Silu)
                 nc.sync.dma_start(out_rows[:, h : h + step, c * P : (c + 1) * P], result[:, h : h + step, :])
 
-        woven1 = []
+        def fetch(c):
+            slot = BLOCKS + c
+            gather(flat1[:, slot, :], window, c, c + 1)
+            both = flat1[:, c : slot + 1 : slot - c, :].unsqueeze(1)
+            return weave("woven1_%d" % c, both, True)
+
+        woven1 = [fetch(c) for c in range(BLOCKS)]
         for c in range(BLOCKS):
-            gather(3, flat1, c, c + 1)
-            woven1.append(weave(1, flat1, c, c + 1, c < SCALAR_WEAVES, "woven1_%d" % c))
-        for c in range(BLOCKS):
-            codes, scales = quantize(1, c, c + 1, woven1[c])
-            multiply(1, c, c, codes, scales)
+            quantize_multiply(1, c, c + 1, woven1[c])
         for c in range(BLOCKS):
             finish(c)
+            leave(c)

@@ -26,13 +26,14 @@ LIST_COLS = P // 16
 MEAN_ROW, INV_ROW = P - 2, P - 1
 HALF = T // 2
 
-CUTS = (480, 512, 352, 768)
+CUTS = (352, 512, 512, 512)
 
 
 def tile_picked_lnfold_silu_l_kernel(tc, xT, mean, inv, gsum, b, w1_words, w1_scales, offs, out):
     nc = tc.nc
     with ExitStack() as ctx:
         keep = ctx.enter_context(tc.tile_pool(name="keep", bufs=1))
+        placed = ctx.enter_context(tc.tile_pool(name="placed", bufs=1))
         psum = ctx.enter_context(tc.psum_pool(name="psum", bufs=1))
 
         def pair_rows(i):
@@ -42,8 +43,10 @@ def tile_picked_lnfold_silu_l_kernel(tc, xT, mean, inv, gsum, b, w1_words, w1_sc
         def load_run(i, lo, hi):
             nc.sync.dma_start(room[i][:, lo:hi], pair_rows(i).rearrange("p e c -> p (e c)")[:, lo:hi])
 
-        room = [keep.tile([P, 2 * T], F32, name="raw%d" % i, align_bytes=64) for i in range(3)]
-        raw = [room[i][:, 0 : 2 * T].rearrange("p (e c) -> p e c", e=2) for i in range(3)]
+        room = [keep.tile([P, 2 * T], F32, name="raw%d" % i, align_bytes=64) for i in (0, 1, 3)]
+        raw2 = placed.tile([P, 2 * T], F32, name="raw2", align_bytes=64, offset=0)
+        room = room[0:2] + [raw2] + room[2:3]
+        raw = [room[i][:, 0 : 2 * T].rearrange("p (e c) -> p e c", e=2) for i in range(4)]
         load_run(0, 0, T // 4)
 
         offsets = keep.tile([P, S // 16], U16, name="offsets")
@@ -62,18 +65,17 @@ def tile_picked_lnfold_silu_l_kernel(tc, xT, mean, inv, gsum, b, w1_words, w1_sc
         g_col = keep.tile([P, HALVES], F32, name="g_col")
         b_col = keep.tile([P, HALVES], F32, name="b_col")
         nc.sync.dma_start(b_col[:], b.rearrange("(p h) o -> p (h o)", h=HALVES))
-        load_run(0, T // 4, 3 * HALF)
         nc.sync.dma_start(g_col[:], gsum.rearrange("(p h) o -> p (h o)", h=HALVES))
-        load_run(0, 3 * HALF, 2 * T)
-        for i in (1, 2):
+        load_run(0, T // 4, 2 * T)
+        load_run(1, 0, 3 * HALF)
+        load_run(1, 3 * HALF, 2 * T)
+        for i in (2, 3):
             load_run(i, 0, 3 * HALF)
             load_run(i, 3 * HALF, 2 * T)
-        last = [keep.tile([P, 2, HALF], F32, name="last%d" % j, align_bytes=64) for j in range(2)]
-        for j in range(2):
-            nc.sync.dma_start(last[j][:], pair_rows(3)[:, :, j * HALF : (j + 1) * HALF])
+        w_codes = [keep.tile([P, N], U32, name="w_codes%d" % z, align_bytes=64) for z in range(PASSES)]
+        for z in range(PASSES):
+            nc.sync.dma_start(w_codes[z][:].bitcast(I32), w1_words[z].rearrange("p n t -> p (n t)").bitcast(I32))
 
-        w_codes = keep.tile([P, PASSES, N], U32, name="w_codes", align_bytes=64)
-        nc.sync.dma_start(w_codes[:].bitcast(I32), w1_words.rearrange("z p n t -> p z (n t)").bitcast(I32))
         w_scales = keep.tile([P, PASSES, N], U8, name="w_scales", align_bytes=64)
         nc.gpsimd.memset(w_scales[:].bitcast(I32), 0)
         for q in range(4):
@@ -136,9 +138,9 @@ def tile_picked_lnfold_silu_l_kernel(tc, xT, mean, inv, gsum, b, w1_words, w1_sc
         def gather(dst, window, first, end):
             nc.vector.tensor_copy(dst, window.indirect(offsets[:, first * LIST_COLS : end * LIST_COLS]))
 
-        def weave(name, src, on_scalar):
+        def weave(name, src, on_scalar, tag=None):
             blocks = src.shape[1]
-            woven = keep.tile([P, blocks * P * 2], U32, name=name, align_bytes=64)
+            woven = keep.tile([P, blocks * P * 2], U32, name=name, tag=tag or name, align_bytes=64)
             if on_scalar:
                 nc.scalar.copy(woven[:].rearrange("p (c n u) -> p c n u", n=P, u=2), src.rearrange("p c u n -> p c n u"))
             else:
@@ -158,20 +160,22 @@ def tile_picked_lnfold_silu_l_kernel(tc, xT, mean, inv, gsum, b, w1_words, w1_sc
                     accs[c][:],
                     lhsT=codes[:, cols].bitcast(FP8X4),
                     lhsT_scale=scales[:, cols],
-                    rhs=w_codes[:, z, :].bitcast(FP8X4),
+                    rhs=w_codes[z][:].bitcast(FP8X4),
                     rhs_scale=w_scales[:, z, :],
                     start=(z == 0),
                     stop=(z == PASSES - 1),
                 )
 
-        flat0 = keep.tile([P, BLOCKS, 2, P], U32, name="flat0", align_bytes=64)
+        flat0 = placed.tile([P, BLOCKS, 2, P], U32, name="flat0", align_bytes=64, offset=8 * T)
         shifts = [make_shift(0), make_shift(1)]
+        nc.scalar.copy(inv_cols[:, 0:2], turned[0][:, :, INV_ROW])
         window0 = keep.tile([P, T], U32, name="window0", tag="picked0", align_bytes=64)
         window = window0[:]
         cast(window, raw[0], 0, 0, CUTS[0], True)
         cast(window, raw[0], 0, CUTS[0], T, False)
         shifts.extend([make_shift(2), make_shift(3)])
         terms = [make_term(0), make_term(1)]
+        nc.scalar.copy(inv_cols[:, 2:4], turned[1][:, :, INV_ROW])
         gather(flat0[:, :, 0, :], window, 0, BLOCKS)
         window1 = keep.tile([P, T], U32, name="window1", tag="raw0", align_bytes=64)
         window = window1[:]
@@ -180,27 +184,23 @@ def tile_picked_lnfold_silu_l_kernel(tc, xT, mean, inv, gsum, b, w1_words, w1_sc
         gather(flat0[:, 0:2, 1, :], window, 0, 2)
         gather(flat0[:, 2:4, 1, :], window, 2, 4)
         terms.extend([make_term(2), make_term(3)])
-        for j in range(2):
-            nc.scalar.copy(inv_cols[:, 2 * j : 2 * j + 2], turned[j][:, :, INV_ROW])
         sums = [lay_sum(c) for c in range(BLOCKS)]
         accs = [psum.tile([P, N], F32, name="y%d" % c, tag="acc%d" % c) for c in range(BLOCKS)]
         window2 = keep.tile([P, T], U32, name="window2", tag="raw1", align_bytes=64)
         window = window2[:]
         cast(window, raw[2], 0, 0, CUTS[2], True)
-        cast(window, raw[2], 0, CUTS[2], HALF, False)
-        cast(window, raw[2], 0, HALF, T, False)
+        cast(window, raw[2], 0, CUTS[2], T, False)
         woven0a = weave("woven0a", flat0[:, 0:2, :, :], True)
         woven0b = weave("woven0b", flat0[:, 2:4, :, :], True)
         flat1 = keep.tile([P, 2 * BLOCKS, P], U32, name="flat1", align_bytes=64)
         gather(flat1[:, 0:BLOCKS, :], window, 0, BLOCKS)
         quantize_multiply(0, 0, 2, woven0a)
-        quantize_multiply(0, 2, 4, woven0b)
 
-        window3 = keep.tile([P, T], U32, name="window3", tag="flat0", align_bytes=64)
+        window3 = placed.tile([P, T], U32, name="window3", align_bytes=64, offset=6 * T)
         window = window3[:]
-        cast(window, last[0], 0, 0, HALF, True)
-        cast(window, last[1], HALF, HALF, CUTS[3], True)
-        cast(window, last[1], HALF, CUTS[3], T, False)
+        cast(window, raw[3], 0, 0, HALF, True)
+        cast(window, raw[3], 0, CUTS[3], T, False)
+        quantize_multiply(0, 2, 4, woven0b)
 
         out_rows = out.rearrange("(p h) j -> p h j", h=HALVES)
 
@@ -231,14 +231,17 @@ def tile_picked_lnfold_silu_l_kernel(tc, xT, mean, inv, gsum, b, w1_words, w1_sc
                 nc.scalar.activation(result[:, h : h + step, :], sums[c][:, h : h + step, :], ACT.Silu)
                 nc.sync.dma_start(out_rows[:, h : h + step, c * P : (c + 1) * P], result[:, h : h + step, :])
 
-        def fetch(c):
-            slot = BLOCKS + c
-            gather(flat1[:, slot, :], window, c, c + 1)
-            both = flat1[:, c : slot + 1 : slot - c, :].unsqueeze(1)
-            return weave("woven1_%d" % c, both, True)
+        def both_pairs(c):
+            return flat1[:, c : c + BLOCKS + 1 : BLOCKS, :].unsqueeze(1)
 
-        woven1 = [fetch(c) for c in range(BLOCKS)]
+        woven1 = []
         for c in range(BLOCKS):
+            gather(flat1[:, BLOCKS + c, :], window, c, c + 1)
+            if c < BLOCKS - 1:
+                woven1.append(weave("woven1_%d" % c, both_pairs(c), True))
+        for c in range(BLOCKS):
+            if c == 2:
+                woven1.append(weave("woven1_3", both_pairs(BLOCKS - 1), False, "woven1_0"))
             quantize_multiply(1, c, c + 1, woven1[c])
         for c in range(BLOCKS):
             finish(c)

@@ -26,7 +26,7 @@ LIST_COLS = P // 16
 MEAN_ROW, INV_ROW = P - 2, P - 1
 HALF = T // 2
 
-CUTS = (352, 512, 512, 512)
+CUTS = (352, 512, 512, 832)
 
 
 def tile_picked_lnfold_silu_l_kernel(tc, xT, mean, inv, gsum, b, w1_words, w1_scales, offs, out):
@@ -43,10 +43,10 @@ def tile_picked_lnfold_silu_l_kernel(tc, xT, mean, inv, gsum, b, w1_words, w1_sc
         def load_run(i, lo, hi):
             nc.sync.dma_start(room[i][:, lo:hi], pair_rows(i).rearrange("p e c -> p (e c)")[:, lo:hi])
 
-        room = [keep.tile([P, 2 * T], F32, name="raw%d" % i, align_bytes=64) for i in (0, 1, 3)]
+        room = [keep.tile([P, 2 * T], F32, name="raw%d" % i, align_bytes=64) for i in (0, 1)]
         raw2 = placed.tile([P, 2 * T], F32, name="raw2", align_bytes=64, offset=0)
-        room = room[0:2] + [raw2] + room[2:3]
-        raw = [room[i][:, 0 : 2 * T].rearrange("p (e c) -> p e c", e=2) for i in range(4)]
+        room = room + [raw2]
+        raw = [room[i][:, 0 : 2 * T].rearrange("p (e c) -> p e c", e=2) for i in range(3)]
         load_run(0, 0, T // 4)
 
         offsets = keep.tile([P, S // 16], U16, name="offsets")
@@ -69,9 +69,11 @@ def tile_picked_lnfold_silu_l_kernel(tc, xT, mean, inv, gsum, b, w1_words, w1_sc
         load_run(0, T // 4, 2 * T)
         load_run(1, 0, 3 * HALF)
         load_run(1, 3 * HALF, 2 * T)
-        for i in (2, 3):
-            load_run(i, 0, 3 * HALF)
-            load_run(i, 3 * HALF, 2 * T)
+        load_run(2, 0, 3 * HALF)
+        load_run(2, 3 * HALF, 2 * T)
+        last = [keep.tile([P, 2, HALF], F32, name="last%d" % j, align_bytes=64) for j in range(2)]
+        for j in range(2):
+            nc.sync.dma_start(last[j][:], pair_rows(3)[:, :, j * HALF : (j + 1) * HALF])
         w_codes = [keep.tile([P, N], U32, name="w_codes%d" % z, align_bytes=64) for z in range(PASSES)]
         for z in range(PASSES):
             nc.sync.dma_start(w_codes[z][:].bitcast(I32), w1_words[z].rearrange("p n t -> p (n t)").bitcast(I32))
@@ -181,8 +183,7 @@ def tile_picked_lnfold_silu_l_kernel(tc, xT, mean, inv, gsum, b, w1_words, w1_sc
         window = window1[:]
         cast(window, raw[1], 0, 0, CUTS[1], True)
         cast(window, raw[1], 0, CUTS[1], T, False)
-        gather(flat0[:, 0:2, 1, :], window, 0, 2)
-        gather(flat0[:, 2:4, 1, :], window, 2, 4)
+        gather(flat0[:, :, 1, :], window, 0, BLOCKS)
         terms.extend([make_term(2), make_term(3)])
         sums = [lay_sum(c) for c in range(BLOCKS)]
         accs = [psum.tile([P, N], F32, name="y%d" % c, tag="acc%d" % c) for c in range(BLOCKS)]
@@ -190,17 +191,17 @@ def tile_picked_lnfold_silu_l_kernel(tc, xT, mean, inv, gsum, b, w1_words, w1_sc
         window = window2[:]
         cast(window, raw[2], 0, 0, CUTS[2], True)
         cast(window, raw[2], 0, CUTS[2], T, False)
-        woven0a = weave("woven0a", flat0[:, 0:2, :, :], True)
-        woven0b = weave("woven0b", flat0[:, 2:4, :, :], True)
+        woven0 = placed.tile([P, 2 * S], U32, name="woven0", align_bytes=64, offset=0)
+        nc.gpsimd.tensor_copy(woven0[:].rearrange("p (c n u) -> p c n u", n=P, u=2), flat0[:].rearrange("p c u n -> p c n u"))
         flat1 = keep.tile([P, 2 * BLOCKS, P], U32, name="flat1", align_bytes=64)
         gather(flat1[:, 0:BLOCKS, :], window, 0, BLOCKS)
-        quantize_multiply(0, 0, 2, woven0a)
 
-        window3 = placed.tile([P, T], U32, name="window3", align_bytes=64, offset=6 * T)
+        window3 = placed.tile([P, T], U32, name="window3", align_bytes=64, offset=4 * T)
         window = window3[:]
-        cast(window, raw[3], 0, 0, HALF, True)
-        cast(window, raw[3], 0, CUTS[3], T, False)
-        quantize_multiply(0, 2, 4, woven0b)
+        cast(window, last[0], 0, 0, HALF, True)
+        cast(window, last[1], HALF, HALF, CUTS[3], True)
+        cast(window, last[1], HALF, CUTS[3], T, False)
+        quantize_multiply(0, 0, BLOCKS, woven0)
 
         out_rows = out.rearrange("(p h) j -> p h j", h=HALVES)
 

@@ -24,9 +24,10 @@ BLOCKS = S // P
 HALVES = N // P
 LIST_COLS = P // 16
 MEAN_ROW, INV_ROW = P - 2, P - 1
+G_ROW, B_ROW = P - 2, P - 1
 HALF = T // 2
 
-CUTS = (352, 512, 512, 832)
+CUTS = (320, 352, 512, 736)
 
 
 def tile_picked_lnfold_silu_l_kernel(tc, xT, mean, inv, gsum, b, w1_words, w1_scales, offs, out):
@@ -62,13 +63,12 @@ def tile_picked_lnfold_silu_l_kernel(tc, xT, mean, inv, gsum, b, w1_words, w1_sc
         nc.scalar.dma_start(stats[INV_ROW : INV_ROW + 1, :], inv[0:1, :])
         nc.vector.memset(stats[0:MEAN_ROW, :], 0.0)
 
-        g_col = keep.tile([P, HALVES], F32, name="g_col")
-        b_col = keep.tile([P, HALVES], F32, name="b_col")
-        nc.sync.dma_start(b_col[:], b.rearrange("(p h) o -> p (h o)", h=HALVES))
-        nc.sync.dma_start(g_col[:], gsum.rearrange("(p h) o -> p (h o)", h=HALVES))
+        consts = keep.tile([P, N], F32, name="consts")
+        nc.sync.dma_start(consts[B_ROW : B_ROW + 1, :], b.rearrange("n o -> o n"))
+        nc.sync.dma_start(consts[G_ROW : G_ROW + 1, :], gsum.rearrange("n o -> o n"))
+        nc.vector.memset(consts[0:G_ROW, :], 0.0)
         load_run(0, T // 4, 2 * T)
-        load_run(1, 0, 3 * HALF)
-        load_run(1, 3 * HALF, 2 * T)
+        load_run(1, 0, 2 * T)
         load_run(2, 0, 3 * HALF)
         load_run(2, 3 * HALF, 2 * T)
         last = [keep.tile([P, 2, HALF], F32, name="last%d" % j, align_bytes=64) for j in range(2)]
@@ -89,28 +89,42 @@ def tile_picked_lnfold_silu_l_kernel(tc, xT, mean, inv, gsum, b, w1_words, w1_sc
         ident = keep.tile([P, P], F32, name="ident")
         make_identity(nc, ident[:])
 
-        b_bank = psum.tile([P, HALVES, P], F32, name="b_bank", tag="acc2")
+        upright = psum.tile([P, HALVES, P], F32, name="upright", tag="acc1")
         for h in range(HALVES):
-            nc.tensor.transpose(b_bank[:, h, :], b_col[:, h : h + 1].to_broadcast([P, P]), ident[:])
-        b_rows = keep.tile([P, HALVES, P], F32, name="b_rows")
-        nc.scalar.copy(b_rows[:], b_bank[:])
-        turned = []
-        for j, tag in enumerate(("acc0", "acc3")):
+            nc.tensor.transpose(upright[:, h, :], consts[:, h * P : (h + 1) * P], ident[:])
+        const_cols = keep.tile([P, HALVES, 2], F32, name="const_cols")
+        nc.scalar.copy(const_cols[:], upright[:, :, G_ROW:P])
+
+        def spread(name, which, tag):
+            bank = psum.tile([P, HALVES, P], F32, name=name, tag=tag)
+            for h in range(HALVES):
+                nc.tensor.transpose(bank[:, h, :], const_cols[:, h, which : which + 1].to_broadcast([P, P]), ident[:])
+            return bank
+
+        def turn(j, tag):
             picked = keep.tile([P, 2 * P], F32, name="picked%d" % j, align_bytes=64)
             nc.vector.tensor_copy(picked[:], stats[:].indirect(offsets[:, 2 * j * LIST_COLS : (2 * j + 2) * LIST_COLS]))
             bank = psum.tile([P, 2, P], F32, name="turned%d" % j, tag=tag)
             for c in range(2):
                 nc.tensor.transpose(bank[:, c, :], picked[:, c * P : (c + 1) * P], ident[:])
-            turned.append(bank)
-        g_bank = psum.tile([P, HALVES, P], F32, name="g_bank", tag="acc1")
-        for h in range(HALVES):
-            nc.tensor.transpose(g_bank[:, h, :], g_col[:, h : h + 1].to_broadcast([P, P]), ident[:])
-        inv_cols = keep.tile([P, BLOCKS], F32, name="inv_cols")
+            return bank
+
+        turned = [turn(0, "acc0")]
+        b_bank = spread("b_bank", 1, "acc2")
+        b_rows = keep.tile([P, HALVES, P], F32, name="b_rows")
+        nc.scalar.copy(b_rows[:], b_bank[:])
+        turned.append(turn(1, "acc3"))
+        g_bank = spread("g_bank", 0, "acc1")
+        stat_cols = [keep.tile([P, 2, 2], F32, name="stat_cols%d" % j) for j in range(2)]
 
         def make_shift(c):
             shift = keep.tile([P, 1], F32, name="shift%d" % c)
-            row = turned[c // 2][:, c % 2, :]
-            nc.vector.tensor_scalar(shift[:], row[:, MEAN_ROW : MEAN_ROW + 1], row[:, INV_ROW : INV_ROW + 1], -1.0, MULT, MULT)
+            if c < 2:
+                row = turned[0][:, c, :]
+                nc.vector.tensor_scalar(shift[:], row[:, MEAN_ROW : MEAN_ROW + 1], row[:, INV_ROW : INV_ROW + 1], -1.0, MULT, MULT)
+            else:
+                both = stat_cols[1][:, c - 2, :]
+                nc.gpsimd.tensor_scalar(shift[:], both[:, 0:1], both[:, 1:2], -1.0, MULT, MULT)
             return shift
 
         def make_term(c):
@@ -170,14 +184,14 @@ def tile_picked_lnfold_silu_l_kernel(tc, xT, mean, inv, gsum, b, w1_words, w1_sc
 
         flat0 = placed.tile([P, BLOCKS, 2, P], U32, name="flat0", align_bytes=64, offset=8 * T)
         shifts = [make_shift(0), make_shift(1)]
-        nc.scalar.copy(inv_cols[:, 0:2], turned[0][:, :, INV_ROW])
+        nc.scalar.copy(stat_cols[0][:], turned[0][:, :, MEAN_ROW:P])
         window0 = keep.tile([P, T], U32, name="window0", tag="picked0", align_bytes=64)
         window = window0[:]
         cast(window, raw[0], 0, 0, CUTS[0], True)
         cast(window, raw[0], 0, CUTS[0], T, False)
+        nc.scalar.copy(stat_cols[1][:], turned[1][:, :, MEAN_ROW:P])
         shifts.extend([make_shift(2), make_shift(3)])
         terms = [make_term(0), make_term(1)]
-        nc.scalar.copy(inv_cols[:, 2:4], turned[1][:, :, INV_ROW])
         gather(flat0[:, :, 0, :], window, 0, BLOCKS)
         window1 = keep.tile([P, T], U32, name="window1", tag="raw0", align_bytes=64)
         window = window1[:]
@@ -192,7 +206,10 @@ def tile_picked_lnfold_silu_l_kernel(tc, xT, mean, inv, gsum, b, w1_words, w1_sc
         cast(window, raw[2], 0, 0, CUTS[2], True)
         cast(window, raw[2], 0, CUTS[2], T, False)
         woven0 = placed.tile([P, 2 * S], U32, name="woven0", align_bytes=64, offset=0)
-        nc.gpsimd.tensor_copy(woven0[:].rearrange("p (c n u) -> p c n u", n=P, u=2), flat0[:].rearrange("p c u n -> p c n u"))
+        woven_blocks = woven0[:].rearrange("p (c n u) -> p c n u", n=P, u=2)
+        flat_blocks = flat0[:].rearrange("p c u n -> p c n u")
+        nc.gpsimd.tensor_copy(woven_blocks[:, 1:BLOCKS], flat_blocks[:, 1:BLOCKS])
+        nc.scalar.copy(woven_blocks[:, 0:1], flat_blocks[:, 0:1])
         flat1 = keep.tile([P, 2 * BLOCKS, P], U32, name="flat1", align_bytes=64)
         gather(flat1[:, 0:BLOCKS, :], window, 0, BLOCKS)
 
@@ -203,11 +220,11 @@ def tile_picked_lnfold_silu_l_kernel(tc, xT, mean, inv, gsum, b, w1_words, w1_sc
         cast(window, last[1], HALF, CUTS[3], T, False)
         quantize_multiply(0, 0, BLOCKS, woven0)
 
-        out_rows = out.rearrange("(p h) j -> p h j", h=HALVES)
+        out_rows = out.rearrange("(h p) j -> p h j", h=HALVES)
 
         def finish(c):
-            by_half = accs[c][:].rearrange("j (p h) -> j h p", h=HALVES)
-            factor = inv_cols[:, c : c + 1]
+            by_half = accs[c][:].rearrange("j (h p) -> j h p", h=HALVES)
+            factor = stat_cols[c // 2][:, c % 2, 1:2]
             step = 1 if c in (0, BLOCKS - 1) else HALVES
             for first in range(0, HALVES, step):
                 scaled = keep.tile([P, step, P], F32, name="scaled%d_%d" % (c, first))

@@ -25,31 +25,21 @@ HALVES = N // P
 LIST_COLS = P // 16
 MEAN_ROW, INV_ROW = P - 2, P - 1
 G_ROW, B_ROW = P - 2, P - 1
-HALF = T // 2
-
-CUTS = (320, 352, 512, 736)
 
 
 def tile_picked_lnfold_silu_l_kernel(tc, xT, mean, inv, gsum, b, w1_words, w1_scales, offs, out):
     nc = tc.nc
     with ExitStack() as ctx:
         keep = ctx.enter_context(tc.tile_pool(name="keep", bufs=1))
-        placed = ctx.enter_context(tc.tile_pool(name="placed", bufs=1))
         psum = ctx.enter_context(tc.psum_pool(name="psum", bufs=1))
 
-        def pair_rows(i):
-            z, u = divmod(i, 2)
-            return xT[K_PASS * z : K_PASS * (z + 1), :].rearrange("(p t) c -> p t c", t=PACK)[:, 2 * u : 2 * u + 2, :]
+        planes = [keep.tile([P, T], F32, name="plane%d" % i, align_bytes=64) for i in range(PASSES * PACK)]
 
-        def load_run(i, lo, hi):
-            nc.sync.dma_start(room[i][:, lo:hi], pair_rows(i).rearrange("p e c -> p (e c)")[:, lo:hi])
+        def load_plane(i):
+            z, t = divmod(i, PACK)
+            nc.sync.dma_start(planes[i][:], xT[K_PASS * z : K_PASS * (z + 1), :].rearrange("(p t) c -> p t c", t=PACK)[:, t, :])
 
-        room = [keep.tile([P, 2 * T], F32, name="raw%d" % i, align_bytes=64) for i in (0, 1)]
-        raw2 = placed.tile([P, 2 * T], F32, name="raw2", align_bytes=64, offset=0)
-        room = room + [raw2]
-        raw = [room[i][:, 0 : 2 * T].rearrange("p (e c) -> p e c", e=2) for i in range(3)]
-        load_run(0, 0, T // 4)
-
+        load_plane(0)
         offsets = keep.tile([P, S // 16], U16, name="offsets")
         nc.sync.dma_start(offsets[:], offs)
 
@@ -67,19 +57,13 @@ def tile_picked_lnfold_silu_l_kernel(tc, xT, mean, inv, gsum, b, w1_words, w1_sc
         nc.sync.dma_start(consts[B_ROW : B_ROW + 1, :], b.rearrange("n o -> o n"))
         nc.sync.dma_start(consts[G_ROW : G_ROW + 1, :], gsum.rearrange("n o -> o n"))
         nc.vector.memset(consts[0:G_ROW, :], 0.0)
-        load_run(0, T // 4, 2 * T)
-        load_run(1, 0, 2 * T)
-        load_run(2, 0, 3 * HALF)
-        load_run(2, 3 * HALF, 2 * T)
-        last = [keep.tile([P, 2, HALF], F32, name="last%d" % j, align_bytes=64) for j in range(2)]
-        for j in range(2):
-            nc.sync.dma_start(last[j][:], pair_rows(3)[:, :, j * HALF : (j + 1) * HALF])
+        for i in range(1, PASSES * PACK):
+            load_plane(i)
         w_codes = [keep.tile([P, N], U32, name="w_codes%d" % z, align_bytes=64) for z in range(PASSES)]
-        for z in range(PASSES):
-            nc.sync.dma_start(w_codes[z][:].bitcast(I32), w1_words[z].rearrange("p n t -> p (n t)").bitcast(I32))
-
         w_scales = keep.tile([P, PASSES, N], U8, name="w_scales", align_bytes=64)
         nc.gpsimd.memset(w_scales[:].bitcast(I32), 0)
+        for z in range(PASSES):
+            nc.sync.dma_start(w_codes[z][:].bitcast(I32), w1_words[z].rearrange("p n t -> p (n t)").bitcast(I32))
         for q in range(4):
             nc.sync.dma_start(
                 w_scales[32 * q : 32 * q + 4, :, :].bitcast(I32),
@@ -88,6 +72,53 @@ def tile_picked_lnfold_silu_l_kernel(tc, xT, mean, inv, gsum, b, w1_words, w1_sc
 
         ident = keep.tile([P, P], F32, name="ident")
         make_identity(nc, ident[:])
+
+        def listed(first, end):
+            return offsets[:, first * LIST_COLS : end * LIST_COLS]
+
+        picked = [keep.tile([P, PACK, S], BF16, name="picked%d" % z, align_bytes=64) for z in range(PASSES)]
+
+        def gather(i, first, end, on_scalar):
+            z, t = divmod(i, PACK)
+            dst = picked[z][:, t, first * P : end * P]
+            src = planes[i][:].indirect(listed(first, end))
+            if on_scalar:
+                nc.scalar.activation(dst, src, ACT.Copy)
+            else:
+                nc.vector.tensor_copy(dst, src)
+
+        def weave(z, first, end, on_scalar):
+            woven = keep.tile([P, (end - first) * P * PACK], BF16, name="woven%d_%d" % (z, first), align_bytes=64)
+            dst = woven[:].rearrange("p (c t) -> p c t", t=PACK)
+            src = picked[z][:, :, first * P : end * P].rearrange("p t c -> p c t")
+            if on_scalar:
+                nc.scalar.copy(dst, src)
+            else:
+                nc.vector.tensor_copy(dst, src)
+            return woven
+
+        def quantize(z, first, end, woven):
+            codes = keep.tile([P, (end - first) * P], U32, name="codes%d_%d" % (z, first), align_bytes=64)
+            scales = keep.tile([P, (end - first) * P], U8, name="scales%d_%d" % (z, first), align_bytes=64)
+            nc.vector.quantize_mx(codes[:].bitcast(FP8X4), scales[:], woven[:])
+            return codes, scales
+
+        def multiply(z, c, first, made):
+            codes, scales = made
+            cols = slice((c - first) * P, (c - first + 1) * P)
+            nc.tensor.matmul_mx(
+                accs[c][:],
+                lhsT=codes[:, cols].bitcast(FP8X4),
+                lhsT_scale=scales[:, cols],
+                rhs=w_codes[z][:].bitcast(FP8X4),
+                rhs_scale=w_scales[:, z, :],
+                start=(z == 0),
+                stop=(z == PASSES - 1),
+            )
+
+        picked_stats = keep.tile([P, S], F32, name="picked_stats", align_bytes=64)
+        nc.vector.tensor_copy(picked_stats[:], stats[:].indirect(offsets[:]))
+        gather(0, 0, BLOCKS, True)
 
         upright = psum.tile([P, HALVES, P], F32, name="upright", tag="acc1")
         for h in range(HALVES):
@@ -101,134 +132,57 @@ def tile_picked_lnfold_silu_l_kernel(tc, xT, mean, inv, gsum, b, w1_words, w1_sc
                 nc.tensor.transpose(bank[:, h, :], const_cols[:, h, which : which + 1].to_broadcast([P, P]), ident[:])
             return bank
 
-        def turn(j, tag):
-            picked = keep.tile([P, 2 * P], F32, name="picked%d" % j, align_bytes=64)
-            nc.vector.tensor_copy(picked[:], stats[:].indirect(offsets[:, 2 * j * LIST_COLS : (2 * j + 2) * LIST_COLS]))
-            bank = psum.tile([P, 2, P], F32, name="turned%d" % j, tag=tag)
-            for c in range(2):
-                nc.tensor.transpose(bank[:, c, :], picked[:, c * P : (c + 1) * P], ident[:])
-            return bank
-
-        turned = [turn(0, "acc0")]
+        turned = psum.tile([P, BLOCKS, P], F32, name="turned", tag="acc0")
+        for c in range(BLOCKS):
+            nc.tensor.transpose(turned[:, c, :], picked_stats[:, c * P : (c + 1) * P], ident[:])
+        gather(1, 0, BLOCKS, False)
+        stat_cols = keep.tile([P, BLOCKS, 2], F32, name="stat_cols")
+        nc.scalar.copy(stat_cols[:], turned[:, :, MEAN_ROW:P])
         b_bank = spread("b_bank", 1, "acc2")
+        g_bank = spread("g_bank", 0, "acc3")
         b_rows = keep.tile([P, HALVES, P], F32, name="b_rows")
         nc.scalar.copy(b_rows[:], b_bank[:])
-        turned.append(turn(1, "acc3"))
-        g_bank = spread("g_bank", 0, "acc1")
-        stat_cols = [keep.tile([P, 2, 2], F32, name="stat_cols%d" % j) for j in range(2)]
 
-        def make_shift(c):
+        shifts = []
+        for c in range(BLOCKS):
             shift = keep.tile([P, 1], F32, name="shift%d" % c)
-            if c < 2:
-                row = turned[0][:, c, :]
-                nc.vector.tensor_scalar(shift[:], row[:, MEAN_ROW : MEAN_ROW + 1], row[:, INV_ROW : INV_ROW + 1], -1.0, MULT, MULT)
-            else:
-                both = stat_cols[1][:, c - 2, :]
-                nc.gpsimd.tensor_scalar(shift[:], both[:, 0:1], both[:, 1:2], -1.0, MULT, MULT)
-            return shift
+            nc.gpsimd.tensor_scalar(shift[:], stat_cols[:, c, 0:1], stat_cols[:, c, 1:2], -1.0, MULT, MULT)
+            shifts.append(shift)
 
-        def make_term(c):
+        sums = []
+        for c in range(BLOCKS):
             term = keep.tile([P, HALVES, P], F32, name="term%d" % c)
-            nc.scalar.activation(term[:], g_bank[:], ACT.Copy, scale=shifts[c][:])
-            return term
-
-        def lay_sum(c):
-            term = terms[c]
+            nc.vector.tensor_scalar(term[:], g_bank[:], shifts[c][:], None, MULT)
             bank = psum.tile([P, HALVES, P], F32, name="sum%d" % c)
             for h in range(HALVES):
                 nc.tensor.matmul(bank[:, h, :], b_rows[:, h, :], ident[:], start=(h == 0), stop=False, is_transpose=True)
             for h in range(HALVES):
                 nc.tensor.matmul(bank[:, h, :], term[:, h, :], ident[:], start=False, stop=False, is_transpose=True)
-            return bank
+            sums.append(bank)
 
-        def words(window, lo, hi):
-            return window[:, lo:hi].bitcast(BF16).rearrange("p (c e) -> p c e", e=2)
+        gather(2, 0, BLOCKS, True)
+        gather(3, 0, 2, False)
+        gather(3, 2, BLOCKS, True)
+        gather(4, 0, BLOCKS, True)
+        woven0 = weave(0, 0, BLOCKS, False)
+        made0 = quantize(0, 0, BLOCKS, woven0)
+        gather(5, 0, BLOCKS, True)
+        gather(6, 0, 2, True)
+        gather(6, 2, BLOCKS, False)
 
-        def cast(window, src, first, lo, hi, on_scalar):
-            piece = src[:, :, lo - first : hi - first].rearrange("p e c -> p c e")
-            if on_scalar:
-                nc.scalar.copy(words(window, lo, hi), piece)
-            else:
-                nc.vector.tensor_copy(words(window, lo, hi), piece)
-
-        def gather(dst, window, first, end):
-            nc.vector.tensor_copy(dst, window.indirect(offsets[:, first * LIST_COLS : end * LIST_COLS]))
-
-        def weave(name, src, on_scalar, tag=None):
-            blocks = src.shape[1]
-            woven = keep.tile([P, blocks * P * 2], U32, name=name, tag=tag or name, align_bytes=64)
-            if on_scalar:
-                nc.scalar.copy(woven[:].rearrange("p (c n u) -> p c n u", n=P, u=2), src.rearrange("p c u n -> p c n u"))
-            else:
-                nc.vector.tensor_copy(
-                    woven[:].bitcast(I32).rearrange("p (c n u) -> p c n u", n=P, u=2),
-                    src.bitcast(I32).rearrange("p c u n -> p c n u"),
-                )
-            return woven
-
-        def quantize_multiply(z, first, end, woven):
-            codes = keep.tile([P, (end - first) * P], U32, name="codes%d_%d" % (z, first), align_bytes=64)
-            scales = keep.tile([P, (end - first) * P], U8, name="scales%d_%d" % (z, first), align_bytes=64)
-            nc.vector.quantize_mx(codes[:].bitcast(FP8X4), scales[:], woven[:].bitcast(BF16))
-            for c in range(first, end):
-                cols = slice((c - first) * P, (c - first + 1) * P)
-                nc.tensor.matmul_mx(
-                    accs[c][:],
-                    lhsT=codes[:, cols].bitcast(FP8X4),
-                    lhsT_scale=scales[:, cols],
-                    rhs=w_codes[z][:].bitcast(FP8X4),
-                    rhs_scale=w_scales[:, z, :],
-                    start=(z == 0),
-                    stop=(z == PASSES - 1),
-                )
-
-        flat0 = placed.tile([P, BLOCKS, 2, P], U32, name="flat0", align_bytes=64, offset=8 * T)
-        shifts = [make_shift(0), make_shift(1)]
-        nc.scalar.copy(stat_cols[0][:], turned[0][:, :, MEAN_ROW:P])
-        window0 = keep.tile([P, T], U32, name="window0", tag="picked0", align_bytes=64)
-        window = window0[:]
-        cast(window, raw[0], 0, 0, CUTS[0], True)
-        cast(window, raw[0], 0, CUTS[0], T, False)
-        nc.scalar.copy(stat_cols[1][:], turned[1][:, :, MEAN_ROW:P])
-        shifts.extend([make_shift(2), make_shift(3)])
-        terms = [make_term(0), make_term(1)]
-        gather(flat0[:, :, 0, :], window, 0, BLOCKS)
-        window1 = keep.tile([P, T], U32, name="window1", tag="raw0", align_bytes=64)
-        window = window1[:]
-        cast(window, raw[1], 0, 0, CUTS[1], True)
-        cast(window, raw[1], 0, CUTS[1], T, False)
-        gather(flat0[:, :, 1, :], window, 0, BLOCKS)
-        terms.extend([make_term(2), make_term(3)])
-        sums = [lay_sum(c) for c in range(BLOCKS)]
         accs = [psum.tile([P, N], F32, name="y%d" % c, tag="acc%d" % c) for c in range(BLOCKS)]
-        window2 = keep.tile([P, T], U32, name="window2", tag="raw1", align_bytes=64)
-        window = window2[:]
-        cast(window, raw[2], 0, 0, CUTS[2], True)
-        cast(window, raw[2], 0, CUTS[2], T, False)
-        woven0 = placed.tile([P, 2 * S], U32, name="woven0", align_bytes=64, offset=0)
-        woven_blocks = woven0[:].rearrange("p (c n u) -> p c n u", n=P, u=2)
-        flat_blocks = flat0[:].rearrange("p c u n -> p c n u")
-        nc.gpsimd.tensor_copy(woven_blocks[:, 1:BLOCKS], flat_blocks[:, 1:BLOCKS])
-        nc.scalar.copy(woven_blocks[:, 0:1], flat_blocks[:, 0:1])
-        flat1 = keep.tile([P, 2 * BLOCKS, P], U32, name="flat1", align_bytes=64)
-        gather(flat1[:, 0:BLOCKS, :], window, 0, BLOCKS)
-
-        window3 = placed.tile([P, T], U32, name="window3", align_bytes=64, offset=4 * T)
-        window = window3[:]
-        cast(window, last[0], 0, 0, HALF, True)
-        cast(window, last[1], HALF, HALF, CUTS[3], True)
-        cast(window, last[1], HALF, CUTS[3], T, False)
-        quantize_multiply(0, 0, BLOCKS, woven0)
+        for c in range(BLOCKS):
+            multiply(0, c, 0, made0)
 
         out_rows = out.rearrange("(h p) j -> p h j", h=HALVES)
 
-        def finish(c):
+        def finish(c, on_scalar):
             by_half = accs[c][:].rearrange("j (h p) -> j h p", h=HALVES)
-            factor = stat_cols[c // 2][:, c % 2, 1:2]
-            step = 1 if c in (0, BLOCKS - 1) else HALVES
+            factor = stat_cols[:, c, 1:2]
+            step = 1 if c == BLOCKS - 1 else HALVES
             for first in range(0, HALVES, step):
                 scaled = keep.tile([P, step, P], F32, name="scaled%d_%d" % (c, first))
-                if c == 0:
+                if on_scalar:
                     nc.scalar.activation(scaled[:], by_half[:, first : first + step, :], ACT.Copy, scale=factor)
                 else:
                     nc.vector.tensor_scalar(scaled[:], by_half[:, first : first + step, :], factor, None, MULT)
@@ -249,18 +203,15 @@ def tile_picked_lnfold_silu_l_kernel(tc, xT, mean, inv, gsum, b, w1_words, w1_sc
                 nc.scalar.activation(result[:, h : h + step, :], sums[c][:, h : h + step, :], ACT.Silu)
                 nc.sync.dma_start(out_rows[:, h : h + step, c * P : (c + 1) * P], result[:, h : h + step, :])
 
-        def both_pairs(c):
-            return flat1[:, c : c + BLOCKS + 1 : BLOCKS, :].unsqueeze(1)
-
-        woven1 = []
+        last = PASSES * PACK - 1
         for c in range(BLOCKS):
-            gather(flat1[:, BLOCKS + c, :], window, c, c + 1)
-            if c < BLOCKS - 1:
-                woven1.append(weave("woven1_%d" % c, both_pairs(c), True))
+            gather(last, c, c + 1, c != 1)
+        woven1 = [weave(1, 0, 1, False), weave(1, 1, 2, False)]
+        woven_last = weave(1, 3, 4, True)
+        multiply(1, 0, 0, quantize(1, 0, 1, woven1[0]))
+        woven1.extend([weave(1, 2, 3, False), woven_last])
+        for c in range(1, BLOCKS):
+            multiply(1, c, c, quantize(1, c, c + 1, woven1[c]))
         for c in range(BLOCKS):
-            if c == 2:
-                woven1.append(weave("woven1_3", both_pairs(BLOCKS - 1), False, "woven1_0"))
-            quantize_multiply(1, c, c + 1, woven1[c])
-        for c in range(BLOCKS):
-            finish(c)
+            finish(c, c == 0)
             leave(c)

@@ -15,6 +15,7 @@ U8 = mybir.dt.uint8
 FP8X4 = mybir.dt.float8_e4m3fn_x4
 ACT = mybir.ActivationFunctionType
 MULT = mybir.AluOpType.mult
+ADD = mybir.AluOpType.add
 
 P = 128
 PACK = 4
@@ -22,9 +23,9 @@ K_PASS = P * PACK
 PASSES = K // K_PASS
 BLOCKS = S // P
 HALVES = N // P
-LIST_COLS = P // 16
 MEAN_ROW, INV_ROW = P - 2, P - 1
 G_ROW, B_ROW = P - 2, P - 1
+FIRST_PIECE = T // 4
 
 
 def tile_picked_lnfold_silu_l_kernel(tc, xT, mean, inv, gsum, b, w1_words, w1_scales, offs, out):
@@ -35,11 +36,11 @@ def tile_picked_lnfold_silu_l_kernel(tc, xT, mean, inv, gsum, b, w1_words, w1_sc
 
         planes = [keep.tile([P, T], F32, name="plane%d" % i, align_bytes=64) for i in range(PASSES * PACK)]
 
-        def load_plane(i):
+        def load_plane(i, lo=0, hi=T):
             z, t = divmod(i, PACK)
-            nc.sync.dma_start(planes[i][:], xT[K_PASS * z : K_PASS * (z + 1), :].rearrange("(p t) c -> p t c", t=PACK)[:, t, :])
+            nc.sync.dma_start(planes[i][:, lo:hi], xT[K_PASS * z : K_PASS * (z + 1), :].rearrange("(p t) c -> p t c", t=PACK)[:, t, lo:hi])
 
-        load_plane(0)
+        load_plane(0, 0, FIRST_PIECE)
         offsets = keep.tile([P, S // 16], U16, name="offsets")
         nc.sync.dma_start(offsets[:], offs)
 
@@ -57,39 +58,39 @@ def tile_picked_lnfold_silu_l_kernel(tc, xT, mean, inv, gsum, b, w1_words, w1_sc
         nc.sync.dma_start(consts[B_ROW : B_ROW + 1, :], b.rearrange("n o -> o n"))
         nc.sync.dma_start(consts[G_ROW : G_ROW + 1, :], gsum.rearrange("n o -> o n"))
         nc.vector.memset(consts[0:G_ROW, :], 0.0)
-        for i in range(1, PASSES * PACK):
+        load_plane(0, FIRST_PIECE, T)
+        w_scales = keep.tile([P, N], U8, name="w_scales", align_bytes=64)
+        nc.gpsimd.memset(w_scales[:].bitcast(I32), 0)
+        for i in range(1, 3):
+            load_plane(i)
+        for q in range(4):
+            nc.sync.dma_start(w_scales[32 * q : 32 * q + 4 * PASSES, :].bitcast(I32), w1_scales[:, 4 * q : 4 * q + 4, :].bitcast(I32))
+        for i in range(3, PASSES * PACK):
             load_plane(i)
         w_codes = [keep.tile([P, N], U32, name="w_codes%d" % z, align_bytes=64) for z in range(PASSES)]
-        w_scales = keep.tile([P, PASSES, N], U8, name="w_scales", align_bytes=64)
-        nc.gpsimd.memset(w_scales[:].bitcast(I32), 0)
         for z in range(PASSES):
             nc.sync.dma_start(w_codes[z][:].bitcast(I32), w1_words[z].rearrange("p n t -> p (n t)").bitcast(I32))
-        for q in range(4):
-            nc.sync.dma_start(
-                w_scales[32 * q : 32 * q + 4, :, :].bitcast(I32),
-                w1_scales[:, 4 * q : 4 * q + 4, :].rearrange("z r c -> r z c").bitcast(I32),
-            )
 
         ident = keep.tile([P, P], F32, name="ident")
         make_identity(nc, ident[:])
 
         def listed(first, end):
-            return offsets[:, first * LIST_COLS : end * LIST_COLS]
+            return offsets[:, first // 16 : end // 16]
 
-        picked = [keep.tile([P, PACK, S], BF16, name="picked%d" % z, align_bytes=64) for z in range(PASSES)]
+        rows = keep.tile([P, PACK + 2, S], F32, name="rows", align_bytes=64)
+        picked = [rows[:, 2 : PACK + 2, :], rows[:, 0:PACK, :]]
 
         def gather(i, first, end, on_scalar):
             z, t = divmod(i, PACK)
-            dst = picked[z][:, t, first * P : end * P]
+            dst = picked[z][:, t, first:end]
             src = planes[i][:].indirect(listed(first, end))
             if on_scalar:
                 nc.scalar.activation(dst, src, ACT.Copy)
             else:
                 nc.vector.tensor_copy(dst, src)
 
-        def weave(z, first, end, on_scalar):
-            woven = keep.tile([P, (end - first) * P * PACK], BF16, name="woven%d_%d" % (z, first), align_bytes=64)
-            dst = woven[:].rearrange("p (c t) -> p c t", t=PACK)
+        def weave(z, first, end, woven, on_scalar=False):
+            dst = woven.rearrange("p (c t) -> p c t", t=PACK)
             src = picked[z][:, :, first * P : end * P].rearrange("p t c -> p c t")
             if on_scalar:
                 nc.scalar.copy(dst, src)
@@ -97,10 +98,13 @@ def tile_picked_lnfold_silu_l_kernel(tc, xT, mean, inv, gsum, b, w1_words, w1_sc
                 nc.vector.tensor_copy(dst, src)
             return woven
 
+        def woven_tile(name, blocks, tag=None):
+            return keep.tile([P, blocks * P * PACK], BF16, name=name, tag=tag or name, align_bytes=64)
+
         def quantize(z, first, end, woven):
             codes = keep.tile([P, (end - first) * P], U32, name="codes%d_%d" % (z, first), align_bytes=64)
             scales = keep.tile([P, (end - first) * P], U8, name="scales%d_%d" % (z, first), align_bytes=64)
-            nc.vector.quantize_mx(codes[:].bitcast(FP8X4), scales[:], woven[:])
+            nc.vector.quantize_mx(codes[:].bitcast(FP8X4), scales[:], woven)
             return codes, scales
 
         def multiply(z, c, first, made):
@@ -111,107 +115,94 @@ def tile_picked_lnfold_silu_l_kernel(tc, xT, mean, inv, gsum, b, w1_words, w1_sc
                 lhsT=codes[:, cols].bitcast(FP8X4),
                 lhsT_scale=scales[:, cols],
                 rhs=w_codes[z][:].bitcast(FP8X4),
-                rhs_scale=w_scales[:, z, :],
+                rhs_scale=w_scales[4 * z : P, :],
                 start=(z == 0),
                 stop=(z == PASSES - 1),
             )
-
-        picked_stats = keep.tile([P, S], F32, name="picked_stats", align_bytes=64)
-        nc.vector.tensor_copy(picked_stats[:], stats[:].indirect(offsets[:]))
-        gather(0, 0, BLOCKS, True)
 
         upright = psum.tile([P, HALVES, P], F32, name="upright", tag="acc1")
         for h in range(HALVES):
             nc.tensor.transpose(upright[:, h, :], consts[:, h * P : (h + 1) * P], ident[:])
         const_cols = keep.tile([P, HALVES, 2], F32, name="const_cols")
-        nc.scalar.copy(const_cols[:], upright[:, :, G_ROW:P])
-
-        def spread(name, which, tag):
-            bank = psum.tile([P, HALVES, P], F32, name=name, tag=tag)
-            for h in range(HALVES):
-                nc.tensor.transpose(bank[:, h, :], const_cols[:, h, which : which + 1].to_broadcast([P, P]), ident[:])
-            return bank
-
+        nc.vector.tensor_copy(const_cols[:], upright[:, :, G_ROW:P])
         turned = psum.tile([P, BLOCKS, P], F32, name="turned", tag="acc0")
-        for c in range(BLOCKS):
-            nc.tensor.transpose(turned[:, c, :], picked_stats[:, c * P : (c + 1) * P], ident[:])
-        gather(1, 0, BLOCKS, False)
-        stat_cols = keep.tile([P, BLOCKS, 2], F32, name="stat_cols")
-        nc.scalar.copy(stat_cols[:], turned[:, :, MEAN_ROW:P])
-        b_bank = spread("b_bank", 1, "acc2")
-        g_bank = spread("g_bank", 0, "acc3")
-        b_rows = keep.tile([P, HALVES, P], F32, name="b_rows")
-        nc.scalar.copy(b_rows[:], b_bank[:])
+        picked_stats = keep.tile([P, S], F32, name="picked_stats", align_bytes=64)
+        for first in range(0, BLOCKS, 2):
+            nc.vector.tensor_copy(picked_stats[:, first * P : (first + 2) * P], stats[:].indirect(listed(first * P, (first + 2) * P)))
+            for c in (first, first + 1):
+                nc.tensor.transpose(turned[:, c, :], picked_stats[:, c * P : (c + 1) * P], ident[:])
+        gather(0, 0, S, True)
+        gather(1, 0, S, True)
 
-        shifts = []
-        for c in range(BLOCKS):
-            shift = keep.tile([P, 1], F32, name="shift%d" % c)
-            nc.gpsimd.tensor_scalar(shift[:], stat_cols[:, c, 0:1], stat_cols[:, c, 1:2], -1.0, MULT, MULT)
-            shifts.append(shift)
+        g_bank = psum.tile([P, HALVES, P], F32, name="g_bank", tag="acc3")
+        for h in range(HALVES):
+            nc.tensor.transpose(g_bank[:, h, :], const_cols[:, h, 0:1].to_broadcast([P, P]), ident[:])
+        g_rows = keep.tile([P, N], F32, name="g_rows")
+        nc.vector.tensor_copy(g_rows[:], g_bank[:].rearrange("p h m -> p (h m)"))
+        seam = (PACK + 1) * S
+        mean_cols = rows[:].rearrange("p r c -> p (r c)")[:, seam - BLOCKS // 2 : seam + BLOCKS // 2]
+        nc.vector.tensor_copy(mean_cols, turned[:, :, MEAN_ROW])
+        inv_cols = keep.tile([P, BLOCKS], F32, name="inv_cols")
+        nc.vector.tensor_copy(inv_cols[:], turned[:, :, INV_ROW])
+        shifts = keep.tile([P, BLOCKS], F32, name="shifts")
+        nc.vector.scalar_tensor_tensor(shifts[:], mean_cols, -1.0, inv_cols[:], MULT, MULT)
+        gather(2, 0, S, False)
 
-        sums = []
+        sums = [[psum.tile([P, 2, P], F32, name="sum%d_%d" % (d, h)) for h in range(HALVES)] for d in range(BLOCKS // 2)]
         for c in range(BLOCKS):
-            term = keep.tile([P, HALVES, P], F32, name="term%d" % c)
-            nc.vector.tensor_scalar(term[:], g_bank[:], shifts[c][:], None, MULT)
-            bank = psum.tile([P, HALVES, P], F32, name="sum%d" % c)
+            term = keep.tile([P, N], F32, name="term%d" % c)
+            nc.gpsimd.tensor_scalar(term[:], g_rows[:], shifts[:, c : c + 1], 0.0, MULT, ADD)
             for h in range(HALVES):
-                nc.tensor.matmul(bank[:, h, :], b_rows[:, h, :], ident[:], start=(h == 0), stop=False, is_transpose=True)
-            for h in range(HALVES):
-                nc.tensor.matmul(bank[:, h, :], term[:, h, :], ident[:], start=False, stop=False, is_transpose=True)
-            sums.append(bank)
+                nc.tensor.matmul(sums[c // 2][h][:, c % 2, :], term[:, h * P : (h + 1) * P], ident[:], start=(c % 2 == 0), stop=False, is_transpose=True)
 
-        gather(2, 0, BLOCKS, True)
-        gather(3, 0, 2, False)
-        gather(3, 2, BLOCKS, True)
-        gather(4, 0, BLOCKS, True)
-        woven0 = weave(0, 0, BLOCKS, False)
-        made0 = quantize(0, 0, BLOCKS, woven0)
-        gather(5, 0, BLOCKS, True)
-        gather(6, 0, 2, True)
-        gather(6, 2, BLOCKS, False)
+        gather(3, 0, S // 2, False)
+        gather(3, S // 2, S, True)
+        gather(4, 0, S, True)
+        both = woven_tile("woven0", BLOCKS)
+        woven0 = [weave(0, first, first + 2, both[:, first * P * PACK : (first + 2) * P * PACK]) for first in (0, 2)]
+        made0 = [quantize(0, 0, 2, woven0[0]), quantize(0, 2, BLOCKS, woven0[1])]
+        gather(5, 0, S, True)
+        gather(6, 0, 320, False)
+        gather(6, 320, S, True)
 
         accs = [psum.tile([P, N], F32, name="y%d" % c, tag="acc%d" % c) for c in range(BLOCKS)]
         for c in range(BLOCKS):
-            multiply(0, c, 0, made0)
+            multiply(0, c, c // 2 * 2, made0[c // 2])
 
-        out_rows = out.rearrange("(h p) j -> p h j", h=HALVES)
+        def scale(c, on_scalar):
+            factor = inv_cols[:, c : c + 1]
+            scaled = keep.tile([P, N], F32, name="scaled%d" % c)
+            if on_scalar:
+                nc.scalar.activation(scaled[:], accs[c][:], ACT.Copy, scale=factor)
+            else:
+                width = P if c == BLOCKS - 1 else N
+                for lo in range(0, N, width):
+                    nc.vector.tensor_scalar(scaled[:, lo : lo + width], accs[c][:, lo : lo + width], factor, None, MULT)
+            return scaled
 
-        def finish(c, on_scalar):
-            by_half = accs[c][:].rearrange("j (h p) -> j h p", h=HALVES)
-            factor = stat_cols[:, c, 1:2]
-            step = 1 if c == BLOCKS - 1 else HALVES
-            for first in range(0, HALVES, step):
-                scaled = keep.tile([P, step, P], F32, name="scaled%d_%d" % (c, first))
-                if on_scalar:
-                    nc.scalar.activation(scaled[:], by_half[:, first : first + step, :], ACT.Copy, scale=factor)
-                else:
-                    nc.vector.tensor_scalar(scaled[:], by_half[:, first : first + step, :], factor, None, MULT)
-                for h in range(first, first + step):
-                    nc.tensor.matmul(
-                        sums[c][:, h, :],
-                        scaled[:, h - first, :],
-                        ident[:],
-                        start=False,
-                        stop=(h == HALVES - 1),
-                        is_transpose=True,
-                    )
-
-        def leave(c):
-            result = keep.tile([P, HALVES, P], F32, name="result%d" % c)
-            step = 1 if c == BLOCKS - 1 else HALVES
-            for h in range(0, HALVES, step):
-                nc.scalar.activation(result[:, h : h + step, :], sums[c][:, h : h + step, :], ACT.Silu)
-                nc.sync.dma_start(out_rows[:, h : h + step, c * P : (c + 1) * P], result[:, h : h + step, :])
+        def leave(d, scaled):
+            for h in range(HALVES):
+                for e in range(2):
+                    nc.tensor.matmul(sums[d][h][:, e, :], scaled[e][:, h * P : (h + 1) * P], ident[:], start=False, stop=(e == 1), is_transpose=True)
+                result = keep.tile([P, 2 * P], F32, name="result%d_%d" % (d, h))
+                nc.scalar.activation(result[:], sums[d][h][:].rearrange("p e j -> p (e j)"), ACT.Silu, bias=const_cols[:, h, 1:2])
+                nc.sync.dma_start(out[h * P : (h + 1) * P, 2 * d * P : 2 * (d + 1) * P], result[:])
 
         last = PASSES * PACK - 1
-        for c in range(BLOCKS):
-            gather(last, c, c + 1, c != 1)
-        woven1 = [weave(1, 0, 1, False), weave(1, 1, 2, False)]
-        woven_last = weave(1, 3, 4, True)
-        multiply(1, 0, 0, quantize(1, 0, 1, woven1[0]))
-        woven1.extend([weave(1, 2, 3, False), woven_last])
-        for c in range(1, BLOCKS):
+        for c in range(2):
+            gather(last, c * P, c * P + P // 2, False)
+            gather(last, c * P + P // 2, (c + 1) * P, True)
+        for c in range(2, BLOCKS):
+            gather(last, c * P, (c + 1) * P, True)
+        woven1 = [woven_tile("woven1_%d" % c, 1)[:] for c in range(BLOCKS)]
+        weave(1, 0, 1, woven1[0])
+        weave(1, 1, 2, woven1[1])
+        weave(1, 2, 3, woven1[2], True)
+        for c in range(2):
             multiply(1, c, c, quantize(1, c, c + 1, woven1[c]))
-        for c in range(BLOCKS):
-            finish(c, c == 0)
-            leave(c)
+        weave(1, 3, 4, woven1[3])
+        for c in range(2, BLOCKS):
+            multiply(1, c, c, quantize(1, c, c + 1, woven1[c]))
+        scaled = [scale(c, c % 2 == 0) for c in range(BLOCKS)]
+        for d in range(BLOCKS // 2):
+            leave(d, scaled[2 * d : 2 * d + 2])

@@ -34,13 +34,15 @@ def tile_picked_lnfold_silu_l_kernel(tc, xT, mean, inv, gsum, b, w1_words, w1_sc
         keep = ctx.enter_context(tc.tile_pool(name="keep", bufs=1))
         psum = ctx.enter_context(tc.psum_pool(name="psum", bufs=1))
 
-        planes = [keep.tile([P, T], F32, name="plane%d" % i, align_bytes=64) for i in range(PASSES * PACK)]
+        pairs = [keep.tile([P, 2 * T], F32, name="pair%d" % u, align_bytes=64) for u in range(2)]
+        singles = [keep.tile([P, T], F32, name="single%d" % t, align_bytes=64) for t in range(PACK)]
+        planes = [pairs[t // 2][:, t % 2 * T : (t % 2 + 1) * T] for t in range(PACK)] + [tile[:] for tile in singles]
 
-        def load_plane(i, lo=0, hi=T):
-            z, t = divmod(i, PACK)
-            nc.sync.dma_start(planes[i][:, lo:hi], xT[K_PASS * z : K_PASS * (z + 1), :].rearrange("(p t) c -> p t c", t=PACK)[:, t, lo:hi])
+        def load_run(dst, z, first):
+            runs = xT[K_PASS * z : K_PASS * (z + 1), :].rearrange("(p t) c -> p (t c)", t=PACK)
+            nc.sync.dma_start(dst, runs[:, first : first + dst.shape[1]])
 
-        load_plane(0, 0, FIRST_PIECE)
+        load_run(pairs[0][:, 0:FIRST_PIECE], 0, 0)
         offsets = keep.tile([P, S // 16], U16, name="offsets")
         nc.sync.dma_start(offsets[:], offs)
 
@@ -58,15 +60,15 @@ def tile_picked_lnfold_silu_l_kernel(tc, xT, mean, inv, gsum, b, w1_words, w1_sc
         nc.sync.dma_start(consts[B_ROW : B_ROW + 1, :], b.rearrange("n o -> o n"))
         nc.sync.dma_start(consts[G_ROW : G_ROW + 1, :], gsum.rearrange("n o -> o n"))
         nc.vector.memset(consts[0:G_ROW, :], 0.0)
-        load_plane(0, FIRST_PIECE, T)
+        load_run(pairs[0][:, FIRST_PIECE : 2 * T], 0, FIRST_PIECE)
         w_scales = keep.tile([P, N], U8, name="w_scales", align_bytes=64)
         nc.gpsimd.memset(w_scales[:].bitcast(I32), 0)
-        for i in range(1, 3):
-            load_plane(i)
+        load_run(pairs[1][:], 0, 2 * T)
+        load_run(singles[0][:], 1, 0)
         for q in range(4):
             nc.sync.dma_start(w_scales[32 * q : 32 * q + 4 * PASSES, :].bitcast(I32), w1_scales[:, 4 * q : 4 * q + 4, :].bitcast(I32))
-        for i in range(3, PASSES * PACK):
-            load_plane(i)
+        for t in range(1, PACK):
+            load_run(singles[t][:], 1, t * T)
         w_codes = [keep.tile([P, N], U32, name="w_codes%d" % z, align_bytes=64) for z in range(PASSES)]
         for z in range(PASSES):
             nc.sync.dma_start(w_codes[z][:].bitcast(I32), w1_words[z].rearrange("p n t -> p (n t)").bitcast(I32))
@@ -83,15 +85,15 @@ def tile_picked_lnfold_silu_l_kernel(tc, xT, mean, inv, gsum, b, w1_words, w1_sc
         def gather(i, first, end, on_scalar):
             z, t = divmod(i, PACK)
             dst = picked[z][:, t, first:end]
-            src = planes[i][:].indirect(listed(first, end))
+            src = planes[i].indirect(listed(first, end))
             if on_scalar:
                 nc.scalar.activation(dst, src, ACT.Copy)
             else:
                 nc.vector.tensor_copy(dst, src)
 
-        def weave(z, first, end, woven, on_scalar=False):
-            dst = woven.rearrange("p (c t) -> p c t", t=PACK)
-            src = picked[z][:, :, first * P : end * P].rearrange("p t c -> p c t")
+        def weave(z, first, end, woven, on_scalar=False, depth=PACK):
+            dst = woven.rearrange("p (c t) -> p c t", t=PACK)[:, :, 0:depth]
+            src = picked[z][:, 0:depth, first * P : end * P].rearrange("p t c -> p c t")
             if on_scalar:
                 nc.scalar.copy(dst, src)
             else:
@@ -132,21 +134,20 @@ def tile_picked_lnfold_silu_l_kernel(tc, xT, mean, inv, gsum, b, w1_words, w1_sc
             for c in (first, first + 1):
                 nc.tensor.transpose(turned[:, c, :], picked_stats[:, c * P : (c + 1) * P], ident[:])
         gather(0, 0, S, True)
-        gather(1, 0, S, True)
 
         g_bank = psum.tile([P, HALVES, P], F32, name="g_bank", tag="acc3")
         for h in range(HALVES):
             nc.tensor.transpose(g_bank[:, h, :], const_cols[:, h, 0:1].to_broadcast([P, P]), ident[:])
         g_rows = keep.tile([P, N], F32, name="g_rows")
         nc.vector.tensor_copy(g_rows[:], g_bank[:].rearrange("p h m -> p (h m)"))
-        seam = (PACK + 1) * S
-        mean_cols = rows[:].rearrange("p r c -> p (r c)")[:, seam - BLOCKS // 2 : seam + BLOCKS // 2]
+        mean_cols = picked[0].rearrange("p t (u c) -> p (t u) c", u=2)[:, 3 : 3 + BLOCKS, 0]
         nc.vector.tensor_copy(mean_cols, turned[:, :, MEAN_ROW])
         inv_cols = keep.tile([P, BLOCKS], F32, name="inv_cols")
         nc.vector.tensor_copy(inv_cols[:], turned[:, :, INV_ROW])
         shifts = keep.tile([P, BLOCKS], F32, name="shifts")
         nc.vector.scalar_tensor_tensor(shifts[:], mean_cols, -1.0, inv_cols[:], MULT, MULT)
-        gather(2, 0, S, False)
+        gather(1, 0, S // 2, True)
+        gather(1, S // 2, S, False)
 
         sums = [[psum.tile([P, 2, P], F32, name="sum%d_%d" % (d, h)) for h in range(HALVES)] for d in range(BLOCKS // 2)]
         for c in range(BLOCKS):
@@ -155,18 +156,22 @@ def tile_picked_lnfold_silu_l_kernel(tc, xT, mean, inv, gsum, b, w1_words, w1_sc
             for h in range(HALVES):
                 nc.tensor.matmul(sums[c // 2][h][:, c % 2, :], term[:, h * P : (h + 1) * P], ident[:], start=(c % 2 == 0), stop=False, is_transpose=True)
 
-        gather(3, 0, S // 2, False)
-        gather(3, S // 2, S, True)
+        for first in (0, S // 2):
+            gather(2, first, first + S // 2, False)
+            gather(3, first, first + S // 2, True)
         gather(4, 0, S, True)
         both = woven_tile("woven0", BLOCKS)
         woven0 = [weave(0, first, first + 2, both[:, first * P * PACK : (first + 2) * P * PACK]) for first in (0, 2)]
         made0 = [quantize(0, 0, 2, woven0[0]), quantize(0, 2, BLOCKS, woven0[1])]
         gather(5, 0, S, True)
-        gather(6, 0, 320, False)
-        gather(6, 320, S, True)
+        for c in range(2):
+            gather(6, c * P, (c + 1) * P, False)
+        gather(6, 2 * P, S, True)
+        early = woven_tile("early", 2, "woven0")
+        woven1 = [weave(1, c, c + 1, early[:, c * P * PACK : (c + 1) * P * PACK], depth=PACK - 1) for c in range(2)]
 
         accs = [psum.tile([P, N], F32, name="y%d" % c, tag="acc%d" % c) for c in range(BLOCKS)]
-        for c in range(BLOCKS):
+        for c in range(BLOCKS - 1):
             multiply(0, c, c // 2 * 2, made0[c // 2])
 
         def scale(c, on_scalar):
@@ -180,29 +185,29 @@ def tile_picked_lnfold_silu_l_kernel(tc, xT, mean, inv, gsum, b, w1_words, w1_sc
                     nc.vector.tensor_scalar(scaled[:, lo : lo + width], accs[c][:, lo : lo + width], factor, None, MULT)
             return scaled
 
-        def leave(d, scaled):
-            for h in range(HALVES):
-                for e in range(2):
-                    nc.tensor.matmul(sums[d][h][:, e, :], scaled[e][:, h * P : (h + 1) * P], ident[:], start=False, stop=(e == 1), is_transpose=True)
-                result = keep.tile([P, 2 * P], F32, name="result%d_%d" % (d, h))
-                nc.scalar.activation(result[:], sums[d][h][:].rearrange("p e j -> p (e j)"), ACT.Silu, bias=const_cols[:, h, 1:2])
-                nc.sync.dma_start(out[h * P : (h + 1) * P, 2 * d * P : 2 * (d + 1) * P], result[:])
+        def leave(d, h, scaled):
+            for e in range(2):
+                nc.tensor.matmul(sums[d][h][:, e, :], scaled[e][:, h * P : (h + 1) * P], ident[:], start=False, stop=(e == 1), is_transpose=True)
+            result = keep.tile([P, 2 * P], F32, name="result%d_%d" % (d, h))
+            nc.scalar.activation(result[:], sums[d][h][:].rearrange("p e j -> p (e j)"), ACT.Silu, bias=const_cols[:, h, 1:2])
+            nc.sync.dma_start(out[h * P : (h + 1) * P, 2 * d * P : 2 * (d + 1) * P], result[:])
 
         last = PASSES * PACK - 1
         for c in range(2):
-            gather(last, c * P, c * P + P // 2, False)
-            gather(last, c * P + P // 2, (c + 1) * P, True)
+            slot = woven1[c].rearrange("p (c t) -> p c t", t=PACK)[:, :, PACK - 1]
+            nc.vector.tensor_copy(slot, planes[last].indirect(listed(c * P, (c + 1) * P)))
         for c in range(2, BLOCKS):
             gather(last, c * P, (c + 1) * P, True)
-        woven1 = [woven_tile("woven1_%d" % c, 1)[:] for c in range(BLOCKS)]
-        weave(1, 0, 1, woven1[0])
-        weave(1, 1, 2, woven1[1])
+            woven1.append(woven_tile("woven1_%d" % c, 1)[:])
         weave(1, 2, 3, woven1[2], True)
         for c in range(2):
             multiply(1, c, c, quantize(1, c, c + 1, woven1[c]))
+        multiply(0, 3, 2, made0[1])
         weave(1, 3, 4, woven1[3])
-        for c in range(2, BLOCKS):
-            multiply(1, c, c, quantize(1, c, c + 1, woven1[c]))
-        scaled = [scale(c, c % 2 == 0) for c in range(BLOCKS)]
+        scaled = [scale(0, True)]
+        multiply(1, 2, 2, quantize(1, 2, 3, woven1[2]))
+        multiply(1, 3, 3, quantize(1, 3, 4, woven1[3]))
+        scaled.extend([scale(1, True), scale(2, False), scale(3, False)])
         for d in range(BLOCKS // 2):
-            leave(d, scaled[2 * d : 2 * d + 2])
+            for h in range(HALVES):
+                leave(d, h, scaled[2 * d : 2 * d + 2])

@@ -91,9 +91,9 @@ def tile_picked_lnfold_silu_l_kernel(tc, xT, mean, inv, gsum, b, w1_words, w1_sc
             else:
                 nc.vector.tensor_copy(dst, src)
 
-        def weave(z, first, end, woven, on_scalar=False, depth=PACK):
-            dst = woven.rearrange("p (c t) -> p c t", t=PACK)[:, :, 0:depth]
-            src = picked[z][:, 0:depth, first * P : end * P].rearrange("p t c -> p c t")
+        def weave(z, first, end, woven, on_scalar=False):
+            dst = woven.rearrange("p (c i t) -> p c t i", t=PACK, i=4)
+            src = picked[z][:, :, first * P : end * P].rearrange("p t (c i) -> p c t i", i=4)
             if on_scalar:
                 nc.scalar.copy(dst, src)
             else:
@@ -164,14 +164,11 @@ def tile_picked_lnfold_silu_l_kernel(tc, xT, mean, inv, gsum, b, w1_words, w1_sc
         woven0 = [weave(0, first, first + 2, both[:, first * P * PACK : (first + 2) * P * PACK]) for first in (0, 2)]
         made0 = [quantize(0, 0, 2, woven0[0]), quantize(0, 2, BLOCKS, woven0[1])]
         gather(5, 0, S, True)
-        for c in range(2):
-            gather(6, c * P, (c + 1) * P, False)
-        gather(6, 2 * P, S, True)
-        early = woven_tile("early", 2, "woven0")
-        woven1 = [weave(1, c, c + 1, early[:, c * P * PACK : (c + 1) * P * PACK], depth=PACK - 1) for c in range(2)]
+        gather(6, 0, 384, False)
+        gather(6, 384, S, True)
 
         accs = [psum.tile([P, N], F32, name="y%d" % c, tag="acc%d" % c) for c in range(BLOCKS)]
-        for c in range(BLOCKS - 1):
+        for c in range(BLOCKS):
             multiply(0, c, c // 2 * 2, made0[c // 2])
 
         def scale(c, on_scalar):
@@ -185,29 +182,29 @@ def tile_picked_lnfold_silu_l_kernel(tc, xT, mean, inv, gsum, b, w1_words, w1_sc
                     nc.vector.tensor_scalar(scaled[:, lo : lo + width], accs[c][:, lo : lo + width], factor, None, MULT)
             return scaled
 
-        def leave(d, h, scaled):
-            for e in range(2):
-                nc.tensor.matmul(sums[d][h][:, e, :], scaled[e][:, h * P : (h + 1) * P], ident[:], start=False, stop=(e == 1), is_transpose=True)
-            result = keep.tile([P, 2 * P], F32, name="result%d_%d" % (d, h))
-            nc.scalar.activation(result[:], sums[d][h][:].rearrange("p e j -> p (e j)"), ACT.Silu, bias=const_cols[:, h, 1:2])
-            nc.sync.dma_start(out[h * P : (h + 1) * P, 2 * d * P : 2 * (d + 1) * P], result[:])
+        def leave(d, scaled):
+            for h in range(HALVES):
+                for e in range(2):
+                    nc.tensor.matmul(sums[d][h][:, e, :], scaled[e][:, h * P : (h + 1) * P], ident[:], start=False, stop=(e == 1), is_transpose=True)
+                result = keep.tile([P, 2 * P], F32, name="result%d_%d" % (d, h))
+                nc.scalar.activation(result[:], sums[d][h][:].rearrange("p e j -> p (e j)"), ACT.Silu, bias=const_cols[:, h, 1:2])
+                nc.sync.dma_start(out[h * P : (h + 1) * P, 2 * d * P : 2 * (d + 1) * P], result[:])
 
         last = PASSES * PACK - 1
         for c in range(2):
-            slot = woven1[c].rearrange("p (c t) -> p c t", t=PACK)[:, :, PACK - 1]
-            nc.vector.tensor_copy(slot, planes[last].indirect(listed(c * P, (c + 1) * P)))
+            gather(last, c * P, c * P + P // 2, False)
+            gather(last, c * P + P // 2, (c + 1) * P, True)
         for c in range(2, BLOCKS):
             gather(last, c * P, (c + 1) * P, True)
-            woven1.append(woven_tile("woven1_%d" % c, 1)[:])
+        woven1 = [woven_tile("woven1_%d" % c, 1)[:] for c in range(BLOCKS)]
+        weave(1, 0, 1, woven1[0])
+        weave(1, 1, 2, woven1[1])
         weave(1, 2, 3, woven1[2], True)
         for c in range(2):
             multiply(1, c, c, quantize(1, c, c + 1, woven1[c]))
-        multiply(0, 3, 2, made0[1])
         weave(1, 3, 4, woven1[3])
-        scaled = [scale(0, True)]
-        multiply(1, 2, 2, quantize(1, 2, 3, woven1[2]))
-        multiply(1, 3, 3, quantize(1, 3, 4, woven1[3]))
-        scaled.extend([scale(1, True), scale(2, False), scale(3, False)])
+        for c in range(2, BLOCKS):
+            multiply(1, c, c, quantize(1, c, c + 1, woven1[c]))
+        scaled = [scale(c, c % 2 == 0) for c in range(BLOCKS)]
         for d in range(BLOCKS // 2):
-            for h in range(HALVES):
-                leave(d, h, scaled[2 * d : 2 * d + 2])
+            leave(d, scaled[2 * d : 2 * d + 2])

@@ -93,7 +93,7 @@ def tile_picked_lnfold_silu_l_kernel(tc, xT, mean, inv, gsum, b, w1_words, w1_sc
 
         def weave(z, first, end, woven, on_scalar=False):
             dst = woven.rearrange("p (c i t) -> p c t i", t=PACK, i=4)
-            src = picked[z][:, :, first * P : end * P].rearrange("p t (c i) -> p c t i", i=4)
+            src = picked[z][:, :, first:end].rearrange("p t (c i) -> p c t i", i=4)
             if on_scalar:
                 nc.scalar.copy(dst, src)
             else:
@@ -149,19 +149,20 @@ def tile_picked_lnfold_silu_l_kernel(tc, xT, mean, inv, gsum, b, w1_words, w1_sc
         gather(1, 0, S // 2, True)
         gather(1, S // 2, S, False)
 
-        sums = [[psum.tile([P, 2, P], F32, name="sum%d_%d" % (d, h)) for h in range(HALVES)] for d in range(BLOCKS // 2)]
+        terms = [keep.tile([P, N], F32, name="term%d" % c) for c in range(BLOCKS)]
         for c in range(BLOCKS):
-            term = keep.tile([P, N], F32, name="term%d" % c)
-            nc.gpsimd.tensor_scalar(term[:], g_rows[:], shifts[:, c : c + 1], 0.0, MULT, ADD)
+            nc.gpsimd.tensor_scalar(terms[c][:], g_rows[:], shifts[:, c : c + 1], 0.0, MULT, ADD)
+        sums = [[psum.tile([P, 2, P], F32, name="sum%d_%d" % (d, h)) for h in range(HALVES)] for d in range(BLOCKS // 2)]
+        for d in range(BLOCKS // 2):
             for h in range(HALVES):
-                nc.tensor.matmul(sums[c // 2][h][:, c % 2, :], term[:, h * P : (h + 1) * P], ident[:], start=(c % 2 == 0), stop=False, is_transpose=True)
+                nc.tensor.matmul(sums[d][h][:, 0, :], terms[2 * d][:, h * P : (h + 1) * P], ident[:], start=True, stop=False, is_transpose=True)
 
         for first in (0, S // 2):
             gather(2, first, first + S // 2, False)
             gather(3, first, first + S // 2, True)
         gather(4, 0, S, True)
         both = woven_tile("woven0", BLOCKS)
-        woven0 = [weave(0, first, first + 2, both[:, first * P * PACK : (first + 2) * P * PACK]) for first in (0, 2)]
+        woven0 = [weave(0, first, first + S // 2, both[:, first * PACK : (first + S // 2) * PACK]) for first in (0, S // 2)]
         made0 = [quantize(0, 0, 2, woven0[0]), quantize(0, 2, BLOCKS, woven0[1])]
         gather(5, 0, S, True)
         gather(6, 0, 384, False)
@@ -171,40 +172,38 @@ def tile_picked_lnfold_silu_l_kernel(tc, xT, mean, inv, gsum, b, w1_words, w1_sc
         for c in range(BLOCKS):
             multiply(0, c, c // 2 * 2, made0[c // 2])
 
-        def scale(c, on_scalar):
-            factor = inv_cols[:, c : c + 1]
+        def scale(c):
             scaled = keep.tile([P, N], F32, name="scaled%d" % c)
-            if on_scalar:
-                nc.scalar.activation(scaled[:], accs[c][:], ACT.Copy, scale=factor)
-            else:
-                width = P if c == BLOCKS - 1 else N
-                for lo in range(0, N, width):
-                    nc.vector.tensor_scalar(scaled[:, lo : lo + width], accs[c][:, lo : lo + width], factor, None, MULT)
+            if c % 2 == 0:
+                nc.scalar.activation(scaled[:], accs[c][:], ACT.Copy, scale=inv_cols[:, c : c + 1])
+                return scaled
+            width = P if c == BLOCKS - 1 else N
+            for lo in range(0, N, width):
+                cols = slice(lo, lo + width)
+                nc.vector.scalar_tensor_tensor(scaled[:, cols], accs[c][:, cols], inv_cols[:, c : c + 1], terms[c][:, cols], MULT, ADD)
             return scaled
 
-        def leave(d, scaled):
-            for h in range(HALVES):
-                for e in range(2):
-                    nc.tensor.matmul(sums[d][h][:, e, :], scaled[e][:, h * P : (h + 1) * P], ident[:], start=False, stop=(e == 1), is_transpose=True)
-                result = keep.tile([P, 2 * P], F32, name="result%d_%d" % (d, h))
-                nc.scalar.activation(result[:], sums[d][h][:].rearrange("p e j -> p (e j)"), ACT.Silu, bias=const_cols[:, h, 1:2])
-                nc.sync.dma_start(out[h * P : (h + 1) * P, 2 * d * P : 2 * (d + 1) * P], result[:])
+        def leave(h, first, end, bank, laid):
+            for c in range(first, end):
+                nc.tensor.matmul(bank[:, c - first, :], scaled[c][:, h * P : (h + 1) * P], ident[:], start=not laid, stop=(c == end - 1), is_transpose=True)
+            result = keep.tile([P, end - first, P], F32, name="result%d_%d" % (h, first))
+            nc.scalar.activation(result[:], bank[:, 0 : end - first, :], ACT.Silu, bias=const_cols[:, h, 1:2])
+            nc.sync.dma_start(out[h * P : (h + 1) * P, first * P : end * P], result[:].rearrange("p e j -> p (e j)"))
 
         last = PASSES * PACK - 1
-        for c in range(2):
-            gather(last, c * P, c * P + P // 2, False)
-            gather(last, c * P + P // 2, (c + 1) * P, True)
-        for c in range(2, BLOCKS):
-            gather(last, c * P, (c + 1) * P, True)
+        for c in range(BLOCKS):
+            gather(last, c * P, (c + 1) * P, c >= 2)
         woven1 = [woven_tile("woven1_%d" % c, 1)[:] for c in range(BLOCKS)]
-        weave(1, 0, 1, woven1[0])
-        weave(1, 1, 2, woven1[1])
-        weave(1, 2, 3, woven1[2], True)
-        for c in range(2):
+        for c in range(BLOCKS - 1):
+            weave(1, c * P, (c + 1) * P, woven1[c], c == 2)
+        for e in range(2):
+            first = S - P + e * P // 2
+            weave(1, first, first + P // 2, woven1[3][:, e * P * PACK // 2 : (e + 1) * P * PACK // 2], e == 1)
+        for c in range(BLOCKS):
             multiply(1, c, c, quantize(1, c, c + 1, woven1[c]))
-        weave(1, 3, 4, woven1[3])
-        for c in range(2, BLOCKS):
-            multiply(1, c, c, quantize(1, c, c + 1, woven1[c]))
-        scaled = [scale(c, c % 2 == 0) for c in range(BLOCKS)]
-        for d in range(BLOCKS // 2):
-            leave(d, scaled[2 * d : 2 * d + 2])
+        scaled = [scale(c) for c in range(BLOCKS)]
+        leave(0, 0, 1, sums[0][0], True)
+        leave(0, 1, 2, psum.tile([P, 1, P], F32, name="spare", tag="acc0"), False)
+        leave(1, 0, 2, sums[0][1], True)
+        for h in range(HALVES):
+            leave(h, 2, BLOCKS, sums[1][h], True)

@@ -25,7 +25,7 @@ BLOCKS = S // P
 HALVES = N // P
 MEAN_ROW, INV_ROW = P - 2, P - 1
 G_ROW, B_ROW = P - 2, P - 1
-FIRST_PIECE = T // 4
+FIRST_PIECE = T // 2
 
 
 def tile_picked_lnfold_silu_l_kernel(tc, xT, mean, inv, gsum, b, w1_words, w1_scales, offs, out):
@@ -140,7 +140,7 @@ def tile_picked_lnfold_silu_l_kernel(tc, xT, mean, inv, gsum, b, w1_words, w1_sc
             nc.tensor.transpose(g_bank[:, h, :], const_cols[:, h, 0:1].to_broadcast([P, P]), ident[:])
         g_rows = keep.tile([P, N], F32, name="g_rows")
         nc.vector.tensor_copy(g_rows[:], g_bank[:].rearrange("p h m -> p (h m)"))
-        mean_cols = picked[0].rearrange("p t (u c) -> p (t u) c", u=2)[:, 3 : 3 + BLOCKS, 0]
+        mean_cols = picked[0].rearrange("p t (u c) -> p (t u) c", u=BLOCKS)[:, 7 : 7 + BLOCKS, 0]
         nc.vector.tensor_copy(mean_cols, turned[:, :, MEAN_ROW])
         inv_cols = keep.tile([P, BLOCKS], F32, name="inv_cols")
         nc.vector.tensor_copy(inv_cols[:], turned[:, :, INV_ROW])
@@ -174,13 +174,13 @@ def tile_picked_lnfold_silu_l_kernel(tc, xT, mean, inv, gsum, b, w1_words, w1_sc
 
         def scale(c):
             scaled = keep.tile([P, N], F32, name="scaled%d" % c)
-            if c % 2 == 0:
-                nc.scalar.activation(scaled[:], accs[c][:], ACT.Copy, scale=inv_cols[:, c : c + 1])
-                return scaled
-            width = P if c == BLOCKS - 1 else N
+            width = P if c in (0, BLOCKS - 1) else N
             for lo in range(0, N, width):
                 cols = slice(lo, lo + width)
-                nc.vector.scalar_tensor_tensor(scaled[:, cols], accs[c][:, cols], inv_cols[:, c : c + 1], terms[c][:, cols], MULT, ADD)
+                if c % 2 == 0:
+                    nc.scalar.activation(scaled[:, cols], accs[c][:, cols], ACT.Copy, scale=inv_cols[:, c : c + 1])
+                else:
+                    nc.vector.scalar_tensor_tensor(scaled[:, cols], accs[c][:, cols], inv_cols[:, c : c + 1], terms[c][:, cols], MULT, ADD)
             return scaled
 
         def leave(h, first, end, bank, laid):

@@ -25,7 +25,9 @@ BLOCKS = S // P
 HALVES = N // P
 MEAN_ROW, INV_ROW = P - 2, P - 1
 G_ROW, B_ROW = P - 2, P - 1
-FIRST_PIECE = T // 2
+ROW_AT = [896, 1408, 1920, 2432, 384, 2944, 0, 640]
+STATS_AT = ROW_AT[3] - (S - P // 2)
+ROWS = ROW_AT[4] + 2 * (ROW_AT[5] - ROW_AT[4])
 
 
 def tile_picked_lnfold_silu_l_kernel(tc, xT, mean, inv, gsum, b, w1_words, w1_scales, offs, out):
@@ -34,15 +36,15 @@ def tile_picked_lnfold_silu_l_kernel(tc, xT, mean, inv, gsum, b, w1_words, w1_sc
         keep = ctx.enter_context(tc.tile_pool(name="keep", bufs=1))
         psum = ctx.enter_context(tc.psum_pool(name="psum", bufs=1))
 
-        pairs = [keep.tile([P, 2 * T], F32, name="pair%d" % u, align_bytes=64) for u in range(2)]
-        singles = [keep.tile([P, T], F32, name="single%d" % t, align_bytes=64) for t in range(PACK)]
-        planes = [pairs[t // 2][:, t % 2 * T : (t % 2 + 1) * T] for t in range(PACK)] + [tile[:] for tile in singles]
+        pair = keep.tile([P, 2 * T], F32, name="pair", align_bytes=64)
+        singles = {i: keep.tile([P, T], F32, name="plane%d" % i, align_bytes=64) for i in (0, 3, 4, 5, 6, 7)}
+        planes = [singles[i][:] if i in singles else pair[:, (i - 1) * T : i * T] for i in range(PASSES * PACK)]
 
         def load_run(dst, z, first):
             runs = xT[K_PASS * z : K_PASS * (z + 1), :].rearrange("(p t) c -> p (t c)", t=PACK)
             nc.sync.dma_start(dst, runs[:, first : first + dst.shape[1]])
 
-        load_run(pairs[0][:, 0:FIRST_PIECE], 0, 0)
+        load_run(planes[0], 0, 0)
         offsets = keep.tile([P, S // 16], U16, name="offsets")
         nc.sync.dma_start(offsets[:], offs)
 
@@ -60,18 +62,24 @@ def tile_picked_lnfold_silu_l_kernel(tc, xT, mean, inv, gsum, b, w1_words, w1_sc
         nc.sync.dma_start(consts[B_ROW : B_ROW + 1, :], b.rearrange("n o -> o n"))
         nc.sync.dma_start(consts[G_ROW : G_ROW + 1, :], gsum.rearrange("n o -> o n"))
         nc.vector.memset(consts[0:G_ROW, :], 0.0)
-        load_run(pairs[0][:, FIRST_PIECE : 2 * T], 0, FIRST_PIECE)
-        w_scales = keep.tile([P, N], U8, name="w_scales", align_bytes=64)
+        load_run(pair[:], 0, T)
+        w_scales = keep.tile([P, PASSES * N], U8, name="w_scales", align_bytes=64)
         nc.gpsimd.memset(w_scales[:].bitcast(I32), 0)
-        load_run(pairs[1][:], 0, 2 * T)
-        load_run(singles[0][:], 1, 0)
+        load_run(planes[3], 0, 3 * T)
+        load_run(planes[4], 1, 0)
         for q in range(4):
-            nc.sync.dma_start(w_scales[32 * q : 32 * q + 4 * PASSES, :].bitcast(I32), w1_scales[:, 4 * q : 4 * q + 4, :].bitcast(I32))
-        for t in range(1, PACK):
-            load_run(singles[t][:], 1, t * T)
+            dst = w_scales[32 * q : 32 * q + 4, :].bitcast(I32).rearrange("i (z n) -> i z n", z=PASSES)
+            nc.sync.dma_start(dst, w1_scales[:, 4 * q : 4 * q + 4, :].bitcast(I32).rearrange("z i n -> i z n"))
         w_codes = [keep.tile([P, N], U32, name="w_codes%d" % z, align_bytes=64) for z in range(PASSES)]
-        for z in range(PASSES):
+
+        def load_words(z):
             nc.sync.dma_start(w_codes[z][:].bitcast(I32), w1_words[z].rearrange("p n t -> p (n t)").bitcast(I32))
+
+        for t in range(1, PACK - 1):
+            load_run(planes[PACK + t], 1, t * T)
+        load_words(0)
+        load_run(planes[2 * PACK - 1], 1, (PACK - 1) * T)
+        load_words(1)
 
         ident = keep.tile([P, P], F32, name="ident")
         make_identity(nc, ident[:])
@@ -79,26 +87,34 @@ def tile_picked_lnfold_silu_l_kernel(tc, xT, mean, inv, gsum, b, w1_words, w1_sc
         def listed(first, end):
             return offsets[:, first // 16 : end // 16]
 
-        rows = keep.tile([P, PACK + 2, S], F32, name="rows", align_bytes=64)
-        picked = [rows[:, 2 : PACK + 2, :], rows[:, 0:PACK, :]]
+        rows = keep.tile([P, ROWS], F32, name="rows", align_bytes=64)
+        picked0 = rows[:, ROW_AT[0] : ROW_AT[0] + PACK * S].rearrange("p (t c) -> p t c", t=PACK)
+
+        def pair_rows(i):
+            step = ROW_AT[i + 1] - ROW_AT[i]
+            return rows[:, ROW_AT[i] : ROW_AT[i] + 2 * step].rearrange("p (t c) -> p t c", t=2)
 
         def gather(i, first, end, on_scalar):
-            z, t = divmod(i, PACK)
-            dst = picked[z][:, t, first:end]
+            dst = rows[:, ROW_AT[i] + first : ROW_AT[i] + end]
             src = planes[i].indirect(listed(first, end))
             if on_scalar:
                 nc.scalar.activation(dst, src, ACT.Copy)
             else:
                 nc.vector.tensor_copy(dst, src)
 
-        def weave(z, first, end, woven, on_scalar=False):
+        def weave(first, end, woven):
             dst = woven.rearrange("p (c i t) -> p c t i", t=PACK, i=4)
-            src = picked[z][:, :, first:end].rearrange("p t (c i) -> p c t i", i=4)
+            src = picked0[:, :, first:end].rearrange("p t (c i) -> p c t i", i=4)
+            nc.vector.tensor_copy(dst, src)
+            return woven
+
+        def weave_pair(u, first, end, on_scalar=False):
+            dst = woven1[:, first * PACK : end * PACK].rearrange("p (c i t) -> p c t i", t=PACK, i=4)[:, :, 2 * u : 2 * u + 2, :]
+            src = pair_rows(PACK + 2 * u)[:, :, first:end].rearrange("p t (c i) -> p c t i", i=4)
             if on_scalar:
                 nc.scalar.copy(dst, src)
             else:
                 nc.vector.tensor_copy(dst, src)
-            return woven
 
         def woven_tile(name, blocks, tag=None):
             return keep.tile([P, blocks * P * PACK], BF16, name=name, tag=tag or name, align_bytes=64)
@@ -117,7 +133,7 @@ def tile_picked_lnfold_silu_l_kernel(tc, xT, mean, inv, gsum, b, w1_words, w1_sc
                 lhsT=codes[:, cols].bitcast(FP8X4),
                 lhsT_scale=scales[:, cols],
                 rhs=w_codes[z][:].bitcast(FP8X4),
-                rhs_scale=w_scales[4 * z : P, :],
+                rhs_scale=w_scales[:, z * N : (z + 1) * N],
                 start=(z == 0),
                 stop=(z == PASSES - 1),
             )
@@ -125,48 +141,54 @@ def tile_picked_lnfold_silu_l_kernel(tc, xT, mean, inv, gsum, b, w1_words, w1_sc
         upright = psum.tile([P, HALVES, P], F32, name="upright", tag="acc1")
         for h in range(HALVES):
             nc.tensor.transpose(upright[:, h, :], consts[:, h * P : (h + 1) * P], ident[:])
-        const_cols = keep.tile([P, HALVES, 2], F32, name="const_cols")
-        nc.vector.tensor_copy(const_cols[:], upright[:, :, G_ROW:P])
         turned = psum.tile([P, BLOCKS, P], F32, name="turned", tag="acc0")
-        picked_stats = keep.tile([P, S], F32, name="picked_stats", align_bytes=64)
-        for first in range(0, BLOCKS, 2):
+        picked_stats = rows[:, STATS_AT : STATS_AT + S]
+
+        def pick_stats(first):
             nc.vector.tensor_copy(picked_stats[:, first * P : (first + 2) * P], stats[:].indirect(listed(first * P, (first + 2) * P)))
             for c in (first, first + 1):
                 nc.tensor.transpose(turned[:, c, :], picked_stats[:, c * P : (c + 1) * P], ident[:])
-        gather(0, 0, S, True)
 
+        pick_stats(0)
+        const_cols = keep.tile([P, HALVES, 2], F32, name="const_cols")
+        nc.vector.tensor_copy(const_cols[:], upright[:, :, G_ROW:P])
         g_bank = psum.tile([P, HALVES, P], F32, name="g_bank", tag="acc3")
         for h in range(HALVES):
             nc.tensor.transpose(g_bank[:, h, :], const_cols[:, h, 0:1].to_broadcast([P, P]), ident[:])
-        g_rows = keep.tile([P, N], F32, name="g_rows")
-        nc.vector.tensor_copy(g_rows[:], g_bank[:].rearrange("p h m -> p (h m)"))
-        mean_cols = picked[0].rearrange("p t (u c) -> p (t u) c", u=BLOCKS)[:, 7 : 7 + BLOCKS, 0]
-        nc.vector.tensor_copy(mean_cols, turned[:, :, MEAN_ROW])
-        inv_cols = keep.tile([P, BLOCKS], F32, name="inv_cols")
-        nc.vector.tensor_copy(inv_cols[:], turned[:, :, INV_ROW])
-        shifts = keep.tile([P, BLOCKS], F32, name="shifts")
-        nc.vector.scalar_tensor_tensor(shifts[:], mean_cols, -1.0, inv_cols[:], MULT, MULT)
-        gather(1, 0, S // 2, True)
-        gather(1, S // 2, S, False)
+        pick_stats(2)
+        gather(0, 0, S, True)
+        minus_g = keep.tile([P, N], F32, name="minus_g")
+        nc.vector.tensor_scalar_mul(minus_g[:], g_bank[:].rearrange("p h m -> p (h m)"), -1.0)
+        stat_cols = keep.tile([P, BLOCKS, 2], F32, name="stat_cols")
+        nc.vector.tensor_copy(stat_cols[:], turned[:, :, MEAN_ROW:P])
+        inv_cols = stat_cols[:, :, 1]
+        gather(1, 0, S, True)
+        gather(2, 0, S, False)
 
+        shifts = keep.tile([P, BLOCKS], F32, name="shifts")
+        nc.gpsimd.tensor_tensor(shifts[:], stat_cols[:, :, 0], inv_cols, MULT)
         terms = [keep.tile([P, N], F32, name="term%d" % c) for c in range(BLOCKS)]
-        for c in range(BLOCKS):
-            nc.gpsimd.tensor_scalar(terms[c][:], g_rows[:], shifts[:, c : c + 1], 0.0, MULT, ADD)
+        for c in range(0, BLOCKS, 2):
+            nc.gpsimd.tensor_scalar(terms[c][:], minus_g[:], shifts[:, c : c + 1], 0.0, MULT, ADD)
         sums = [[psum.tile([P, 2, P], F32, name="sum%d_%d" % (d, h)) for h in range(HALVES)] for d in range(BLOCKS // 2)]
         for d in range(BLOCKS // 2):
             for h in range(HALVES):
                 nc.tensor.matmul(sums[d][h][:, 0, :], terms[2 * d][:, h * P : (h + 1) * P], ident[:], start=True, stop=False, is_transpose=True)
 
-        for first in (0, S // 2):
-            gather(2, first, first + S // 2, False)
-            gather(3, first, first + S // 2, True)
+        gather(3, 0, S // 2, False)
+        gather(3, S // 2, S, True)
+        for c in range(1, BLOCKS, 2):
+            nc.vector.tensor_scalar(terms[c][:], minus_g[:], stat_cols[:, c, 0:1], stat_cols[:, c, 1:2], MULT, MULT)
         gather(4, 0, S, True)
         both = woven_tile("woven0", BLOCKS)
-        woven0 = [weave(0, first, first + S // 2, both[:, first * PACK : (first + S // 2) * PACK]) for first in (0, S // 2)]
+        woven0 = [weave(first, first + S // 2, both[:, first * PACK : (first + S // 2) * PACK]) for first in (0, S // 2)]
         made0 = [quantize(0, 0, 2, woven0[0]), quantize(0, 2, BLOCKS, woven0[1])]
-        gather(5, 0, S, True)
-        gather(6, 0, 384, False)
-        gather(6, 384, S, True)
+        woven1 = woven_tile("woven1", BLOCKS)
+        for first in (0, S // 2):
+            gather(5, first, first + S // 2, True)
+            weave_pair(0, first, first + S // 2)
+        gather(6, 0, S - P, True)
+        gather(6, S - P, S, False)
 
         accs = [psum.tile([P, N], F32, name="y%d" % c, tag="acc%d" % c) for c in range(BLOCKS)]
         for c in range(BLOCKS):
@@ -191,16 +213,15 @@ def tile_picked_lnfold_silu_l_kernel(tc, xT, mean, inv, gsum, b, w1_words, w1_sc
             nc.sync.dma_start(out[h * P : (h + 1) * P, first * P : end * P], result[:].rearrange("p e j -> p (e j)"))
 
         last = PASSES * PACK - 1
+        gather(last, 0, P, False)
+        gather(last, P, P + P // 2, False)
+        gather(last, P + P // 2, 2 * P, True)
+        for c in range(2, BLOCKS):
+            gather(last, c * P, (c + 1) * P, True)
         for c in range(BLOCKS):
-            gather(last, c * P, (c + 1) * P, c >= 2)
-        woven1 = [woven_tile("woven1_%d" % c, 1)[:] for c in range(BLOCKS)]
-        for c in range(BLOCKS - 1):
-            weave(1, c * P, (c + 1) * P, woven1[c], c == 2)
-        for e in range(2):
-            first = S - P + e * P // 2
-            weave(1, first, first + P // 2, woven1[3][:, e * P * PACK // 2 : (e + 1) * P * PACK // 2], e == 1)
+            weave_pair(1, c * P, (c + 1) * P, c == BLOCKS - 1)
         for c in range(BLOCKS):
-            multiply(1, c, c, quantize(1, c, c + 1, woven1[c]))
+            multiply(1, c, c, quantize(1, c, c + 1, woven1[:, c * P * PACK : (c + 1) * P * PACK]))
         scaled = [scale(c) for c in range(BLOCKS)]
         leave(0, 0, 1, sums[0][0], True)
         leave(0, 1, 2, psum.tile([P, 1, P], F32, name="spare", tag="acc0"), False)

@@ -109,8 +109,8 @@ def tile_picked_lnfold_silu_l_kernel(tc, xT, mean, inv, gsum, b, w1_words, w1_sc
             return woven
 
         def weave_pair(u, first, end, on_scalar=False):
-            dst = woven1[:, first * PACK : end * PACK].rearrange("p (c i t) -> p c t i", t=PACK, i=4)[:, :, 2 * u : 2 * u + 2, :]
-            src = pair_rows(PACK + 2 * u)[:, :, first:end].rearrange("p t (c i) -> p c t i", i=4)
+            dst = woven1[:, first * PACK : end * PACK].rearrange("p (c t) -> p c t", t=PACK)[:, :, 2 * u : 2 * u + 2]
+            src = pair_rows(PACK + 2 * u)[:, :, first:end].rearrange("p t c -> p c t")
             if on_scalar:
                 nc.scalar.copy(dst, src)
             else:
@@ -170,10 +170,9 @@ def tile_picked_lnfold_silu_l_kernel(tc, xT, mean, inv, gsum, b, w1_words, w1_sc
         terms = [keep.tile([P, N], F32, name="term%d" % c) for c in range(BLOCKS)]
         for c in range(0, BLOCKS, 2):
             nc.gpsimd.tensor_scalar(terms[c][:], minus_g[:], shifts[:, c : c + 1], 0.0, MULT, ADD)
-        sums = [[psum.tile([P, 2, P], F32, name="sum%d_%d" % (d, h)) for h in range(HALVES)] for d in range(BLOCKS // 2)]
-        for d in range(BLOCKS // 2):
-            for h in range(HALVES):
-                nc.tensor.matmul(sums[d][h][:, 0, :], terms[2 * d][:, h * P : (h + 1) * P], ident[:], start=True, stop=False, is_transpose=True)
+        laid = [psum.tile([P, 2, P], F32, name="laid%d" % h) for h in range(HALVES)]
+        for h in range(HALVES):
+            nc.tensor.matmul(laid[h][:, 0, :], terms[0][:, h * P : (h + 1) * P], ident[:], start=True, stop=False, is_transpose=True)
 
         gather(3, 0, S // 2, False)
         gather(3, S // 2, S, True)
@@ -199,18 +198,27 @@ def tile_picked_lnfold_silu_l_kernel(tc, xT, mean, inv, gsum, b, w1_words, w1_sc
             width = P if c in (0, BLOCKS - 1) else N
             for lo in range(0, N, width):
                 cols = slice(lo, lo + width)
-                if c % 2 == 0:
+                if c == 0:
                     nc.scalar.activation(scaled[:, cols], accs[c][:, cols], ACT.Copy, scale=inv_cols[:, c : c + 1])
                 else:
                     nc.vector.scalar_tensor_tensor(scaled[:, cols], accs[c][:, cols], inv_cols[:, c : c + 1], terms[c][:, cols], MULT, ADD)
             return scaled
 
-        def leave(h, first, end, bank, laid):
+        def turn(h, first, end, bank, opened):
             for c in range(first, end):
-                nc.tensor.matmul(bank[:, c - first, :], scaled[c][:, h * P : (h + 1) * P], ident[:], start=not laid, stop=(c == end - 1), is_transpose=True)
-            result = keep.tile([P, end - first, P], F32, name="result%d_%d" % (h, first))
-            nc.scalar.activation(result[:], bank[:, 0 : end - first, :], ACT.Silu, bias=const_cols[:, h, 1:2])
+                nc.tensor.matmul(bank[:, c - first, :], scaled[c][:, h * P : (h + 1) * P], ident[:], start=(c == first and not opened), stop=(c == end - 1), is_transpose=True)
+
+        def activate(h, dst, bank):
+            nc.scalar.activation(dst, bank, ACT.Silu, bias=const_cols[:, h, 1:2])
+
+        def store(h, first, end, result):
             nc.sync.dma_start(out[h * P : (h + 1) * P, first * P : end * P], result[:].rearrange("p e j -> p (e j)"))
+
+        def leave(h, first, end, bank, opened):
+            turn(h, first, end, bank, opened)
+            result = keep.tile([P, end - first, P], F32, name="result%d_%d" % (h, first))
+            activate(h, result[:], bank[:, 0 : end - first, :])
+            store(h, first, end, result)
 
         last = PASSES * PACK - 1
         gather(last, 0, P, False)
@@ -218,13 +226,19 @@ def tile_picked_lnfold_silu_l_kernel(tc, xT, mean, inv, gsum, b, w1_words, w1_sc
         gather(last, P + P // 2, 2 * P, True)
         for c in range(2, BLOCKS):
             gather(last, c * P, (c + 1) * P, True)
+        weave_pair(1, 0, P)
         for c in range(BLOCKS):
-            weave_pair(1, c * P, (c + 1) * P, c == BLOCKS - 1)
-        for c in range(BLOCKS):
+            if c + 1 < BLOCKS:
+                weave_pair(1, (c + 1) * P, (c + 2) * P, c + 2 == BLOCKS)
             multiply(1, c, c, quantize(1, c, c + 1, woven1[:, c * P * PACK : (c + 1) * P * PACK]))
         scaled = [scale(c) for c in range(BLOCKS)]
-        leave(0, 0, 1, sums[0][0], True)
-        leave(0, 1, 2, psum.tile([P, 1, P], F32, name="spare", tag="acc0"), False)
-        leave(1, 0, 2, sums[0][1], True)
-        for h in range(HALVES):
-            leave(h, 2, BLOCKS, sums[1][h], True)
+        leave(0, 0, 1, laid[0], True)
+        leave(0, 1, 2, psum.tile([P, 1, P], F32, name="spare0", tag="acc0"), False)
+        leave(1, 0, 2, laid[1], True)
+        leave(0, 2, BLOCKS, psum.tile([P, 2, P], F32, name="late0"), False)
+        result = keep.tile([P, 2, P], F32, name="result_last")
+        for c, tag in ((2, "late1"), (3, "acc1")):
+            bank = psum.tile([P, 1, P], F32, name="late1_%d" % c, tag=tag)
+            turn(1, c, c + 1, bank, False)
+            activate(1, result[:, c - 2 : c - 1, :], bank[:])
+        store(1, 2, BLOCKS, result)

@@ -25,9 +25,9 @@ BLOCKS = S // P
 HALVES = N // P
 MEAN_ROW, INV_ROW = P - 2, P - 1
 G_ROW, B_ROW = P - 2, P - 1
-ROW_AT = [896, 1408, 1920, 2432, 384, 2944, 0, 640]
+ROW_AT = [(2 + t) * S for t in range(PACK)] + [t * S for t in range(PACK)]
 STATS_AT = ROW_AT[3] - (S - P // 2)
-ROWS = ROW_AT[4] + 2 * (ROW_AT[5] - ROW_AT[4])
+ROWS = (PACK + 2) * S
 
 
 def tile_picked_lnfold_silu_l_kernel(tc, xT, mean, inv, gsum, b, w1_words, w1_scales, offs, out):
@@ -66,20 +66,14 @@ def tile_picked_lnfold_silu_l_kernel(tc, xT, mean, inv, gsum, b, w1_words, w1_sc
         w_scales = keep.tile([P, PASSES * N], U8, name="w_scales", align_bytes=64)
         nc.gpsimd.memset(w_scales[:].bitcast(I32), 0)
         load_run(planes[3], 0, 3 * T)
-        load_run(planes[4], 1, 0)
+        for t in range(PACK):
+            load_run(planes[PACK + t], 1, t * T)
         for q in range(4):
             dst = w_scales[32 * q : 32 * q + 4, :].bitcast(I32).rearrange("i (z n) -> i z n", z=PASSES)
             nc.sync.dma_start(dst, w1_scales[:, 4 * q : 4 * q + 4, :].bitcast(I32).rearrange("z i n -> i z n"))
         w_codes = [keep.tile([P, N], U32, name="w_codes%d" % z, align_bytes=64) for z in range(PASSES)]
-
-        def load_words(z):
+        for z in range(PASSES):
             nc.sync.dma_start(w_codes[z][:].bitcast(I32), w1_words[z].rearrange("p n t -> p (n t)").bitcast(I32))
-
-        for t in range(1, PACK - 1):
-            load_run(planes[PACK + t], 1, t * T)
-        load_words(0)
-        load_run(planes[2 * PACK - 1], 1, (PACK - 1) * T)
-        load_words(1)
 
         ident = keep.tile([P, P], F32, name="ident")
         make_identity(nc, ident[:])
@@ -88,11 +82,7 @@ def tile_picked_lnfold_silu_l_kernel(tc, xT, mean, inv, gsum, b, w1_words, w1_sc
             return offsets[:, first // 16 : end // 16]
 
         rows = keep.tile([P, ROWS], F32, name="rows", align_bytes=64)
-        picked0 = rows[:, ROW_AT[0] : ROW_AT[0] + PACK * S].rearrange("p (t c) -> p t c", t=PACK)
-
-        def pair_rows(i):
-            step = ROW_AT[i + 1] - ROW_AT[i]
-            return rows[:, ROW_AT[i] : ROW_AT[i] + 2 * step].rearrange("p (t c) -> p t c", t=2)
+        picked = [rows[:, ROW_AT[PACK * z] : ROW_AT[PACK * z] + PACK * S].rearrange("p (t c) -> p t c", t=PACK) for z in range(PASSES)]
 
         def gather(i, first, end, on_scalar):
             dst = rows[:, ROW_AT[i] + first : ROW_AT[i] + end]
@@ -102,19 +92,14 @@ def tile_picked_lnfold_silu_l_kernel(tc, xT, mean, inv, gsum, b, w1_words, w1_sc
             else:
                 nc.vector.tensor_copy(dst, src)
 
-        def weave(first, end, woven):
+        def weave(z, first, end, woven, on_scalar=False):
             dst = woven.rearrange("p (c i t) -> p c t i", t=PACK, i=4)
-            src = picked0[:, :, first:end].rearrange("p t (c i) -> p c t i", i=4)
-            nc.vector.tensor_copy(dst, src)
-            return woven
-
-        def weave_pair(u, first, end, on_scalar=False):
-            dst = woven1[:, first * PACK : end * PACK].rearrange("p (c t) -> p c t", t=PACK)[:, :, 2 * u : 2 * u + 2]
-            src = pair_rows(PACK + 2 * u)[:, :, first:end].rearrange("p t c -> p c t")
+            src = picked[z][:, :, first:end].rearrange("p t (c i) -> p c t i", i=4)
             if on_scalar:
                 nc.scalar.copy(dst, src)
             else:
                 nc.vector.tensor_copy(dst, src)
+            return woven
 
         def woven_tile(name, blocks, tag=None):
             return keep.tile([P, blocks * P * PACK], BF16, name=name, tag=tag or name, align_bytes=64)
@@ -170,9 +155,10 @@ def tile_picked_lnfold_silu_l_kernel(tc, xT, mean, inv, gsum, b, w1_words, w1_sc
         terms = [keep.tile([P, N], F32, name="term%d" % c) for c in range(BLOCKS)]
         for c in range(0, BLOCKS, 2):
             nc.gpsimd.tensor_scalar(terms[c][:], minus_g[:], shifts[:, c : c + 1], 0.0, MULT, ADD)
-        laid = [psum.tile([P, 2, P], F32, name="laid%d" % h) for h in range(HALVES)]
-        for h in range(HALVES):
-            nc.tensor.matmul(laid[h][:, 0, :], terms[0][:, h * P : (h + 1) * P], ident[:], start=True, stop=False, is_transpose=True)
+        laid = [[psum.tile([P, 2, P], F32, name="laid%d_%d" % (d, h)) for h in range(HALVES)] for d in range(BLOCKS // 2)]
+        for d in range(BLOCKS // 2):
+            for h in range(HALVES):
+                nc.tensor.matmul(laid[d][h][:, 0, :], terms[2 * d][:, h * P : (h + 1) * P], ident[:], start=True, stop=False, is_transpose=True)
 
         gather(3, 0, S // 2, False)
         gather(3, S // 2, S, True)
@@ -180,14 +166,11 @@ def tile_picked_lnfold_silu_l_kernel(tc, xT, mean, inv, gsum, b, w1_words, w1_sc
             nc.vector.tensor_scalar(terms[c][:], minus_g[:], stat_cols[:, c, 0:1], stat_cols[:, c, 1:2], MULT, MULT)
         gather(4, 0, S, True)
         both = woven_tile("woven0", BLOCKS)
-        woven0 = [weave(first, first + S // 2, both[:, first * PACK : (first + S // 2) * PACK]) for first in (0, S // 2)]
+        woven0 = [weave(0, first, first + S // 2, both[:, first * PACK : (first + S // 2) * PACK]) for first in (0, S // 2)]
         made0 = [quantize(0, 0, 2, woven0[0]), quantize(0, 2, BLOCKS, woven0[1])]
-        woven1 = woven_tile("woven1", BLOCKS)
-        for first in (0, S // 2):
-            gather(5, first, first + S // 2, True)
-            weave_pair(0, first, first + S // 2)
-        gather(6, 0, S - P, True)
-        gather(6, S - P, S, False)
+        gather(5, 0, S, True)
+        gather(6, 0, S // 2, False)
+        gather(6, S // 2, S, True)
 
         accs = [psum.tile([P, N], F32, name="y%d" % c, tag="acc%d" % c) for c in range(BLOCKS)]
         for c in range(BLOCKS):
@@ -198,7 +181,7 @@ def tile_picked_lnfold_silu_l_kernel(tc, xT, mean, inv, gsum, b, w1_words, w1_sc
             width = P if c in (0, BLOCKS - 1) else N
             for lo in range(0, N, width):
                 cols = slice(lo, lo + width)
-                if c == 0:
+                if c % 2 == 0:
                     nc.scalar.activation(scaled[:, cols], accs[c][:, cols], ACT.Copy, scale=inv_cols[:, c : c + 1])
                 else:
                     nc.vector.scalar_tensor_tensor(scaled[:, cols], accs[c][:, cols], inv_cols[:, c : c + 1], terms[c][:, cols], MULT, ADD)
@@ -221,24 +204,25 @@ def tile_picked_lnfold_silu_l_kernel(tc, xT, mean, inv, gsum, b, w1_words, w1_sc
             store(h, first, end, result)
 
         last = PASSES * PACK - 1
-        gather(last, 0, P, False)
-        gather(last, P, P + P // 2, False)
-        gather(last, P + P // 2, 2 * P, True)
-        for c in range(2, BLOCKS):
-            gather(last, c * P, (c + 1) * P, True)
-        weave_pair(1, 0, P)
         for c in range(BLOCKS):
-            if c + 1 < BLOCKS:
-                weave_pair(1, (c + 1) * P, (c + 2) * P, c + 2 == BLOCKS)
-            multiply(1, c, c, quantize(1, c, c + 1, woven1[:, c * P * PACK : (c + 1) * P * PACK]))
+            gather(last, c * P, (c + 1) * P, c >= 2)
+        woven1 = [woven_tile("woven1_%d" % c, 1)[:] for c in range(BLOCKS)]
+        weave(1, 0, P, woven1[0])
+        weave(1, P, 2 * P, woven1[1])
+        weave(1, 2 * P, 3 * P, woven1[2], True)
+        multiply(1, 0, 0, quantize(1, 0, 1, woven1[0]))
+        for e in range(2):
+            first = S - P + e * P // 2
+            weave(1, first, first + P // 2, woven1[3][:, e * P * PACK // 2 : (e + 1) * P * PACK // 2], e == 1)
+        for c in range(1, BLOCKS):
+            multiply(1, c, c, quantize(1, c, c + 1, woven1[c]))
         scaled = [scale(c) for c in range(BLOCKS)]
-        leave(0, 0, 1, laid[0], True)
+        leave(0, 0, 1, laid[0][0], True)
         leave(0, 1, 2, psum.tile([P, 1, P], F32, name="spare0", tag="acc0"), False)
-        leave(1, 0, 2, laid[1], True)
-        leave(0, 2, BLOCKS, psum.tile([P, 2, P], F32, name="late0"), False)
+        leave(1, 0, 2, laid[0][1], True)
+        leave(0, 2, BLOCKS, laid[1][0], True)
         result = keep.tile([P, 2, P], F32, name="result_last")
-        for c, tag in ((2, "late1"), (3, "acc1")):
-            bank = psum.tile([P, 1, P], F32, name="late1_%d" % c, tag=tag)
-            turn(1, c, c + 1, bank, False)
-            activate(1, result[:, c - 2 : c - 1, :], bank[:])
+        for c, bank in ((2, laid[1][1]), (3, psum.tile([P, 1, P], F32, name="spare1", tag="acc1"))):
+            turn(1, c, c + 1, bank, c == 2)
+            activate(1, result[:, c - 2 : c - 1, :], bank[:, 0:1, :])
         store(1, 2, BLOCKS, result)

@@ -66,14 +66,16 @@ def tile_picked_lnfold_silu_l_kernel(tc, xT, mean, inv, gsum, b, w1_words, w1_sc
         w_scales = keep.tile([P, PASSES * N], U8, name="w_scales", align_bytes=64)
         nc.gpsimd.memset(w_scales[:].bitcast(I32), 0)
         load_run(planes[3], 0, 3 * T)
-        for t in range(PACK):
-            load_run(planes[PACK + t], 1, t * T)
+        load_run(planes[PACK], 1, 0)
         for q in range(4):
             dst = w_scales[32 * q : 32 * q + 4, :].bitcast(I32).rearrange("i (z n) -> i z n", z=PASSES)
             nc.sync.dma_start(dst, w1_scales[:, 4 * q : 4 * q + 4, :].bitcast(I32).rearrange("z i n -> i z n"))
-        w_codes = [keep.tile([P, N], U32, name="w_codes%d" % z, align_bytes=64) for z in range(PASSES)]
-        for z in range(PASSES):
-            nc.sync.dma_start(w_codes[z][:].bitcast(I32), w1_words[z].rearrange("p n t -> p (n t)").bitcast(I32))
+        for t in range(1, PACK):
+            load_run(planes[PACK + t], 1, t * T)
+        w_codes = {}
+        for z, lo, hi in ((0, 0, P), (0, P, N), (1, 0, N)):
+            w_codes[z, lo] = keep.tile([P, hi - lo], U32, name="w_codes%d_%d" % (z, lo), align_bytes=64)
+            nc.sync.dma_start(w_codes[z, lo][:].bitcast(I32), w1_words[z].rearrange("p n t -> p (n t)").bitcast(I32)[:, lo:hi])
 
         ident = keep.tile([P, P], F32, name="ident")
         make_identity(nc, ident[:])
@@ -110,16 +112,16 @@ def tile_picked_lnfold_silu_l_kernel(tc, xT, mean, inv, gsum, b, w1_words, w1_sc
             nc.vector.quantize_mx(codes[:].bitcast(FP8X4), scales[:], woven)
             return codes, scales
 
-        def multiply(z, c, first, made):
+        def multiply(z, c, first, made, lo=0, hi=N):
             codes, scales = made
             cols = slice((c - first) * P, (c - first + 1) * P)
             nc.tensor.matmul_mx(
-                accs[c][:],
+                accs[c][:, lo:hi],
                 lhsT=codes[:, cols].bitcast(FP8X4),
                 lhsT_scale=scales[:, cols],
-                rhs=w_codes[z][:].bitcast(FP8X4),
-                rhs_scale=w_scales[:, z * N : (z + 1) * N],
-                start=(z == 0),
+                rhs=w_codes[z, lo][:].bitcast(FP8X4),
+                rhs_scale=w_scales[:, z * N + lo : z * N + hi],
+                start=(z == 0 and lo == 0),
                 stop=(z == PASSES - 1),
             )
 
@@ -173,8 +175,9 @@ def tile_picked_lnfold_silu_l_kernel(tc, xT, mean, inv, gsum, b, w1_words, w1_sc
         gather(6, S // 2, S, True)
 
         accs = [psum.tile([P, N], F32, name="y%d" % c, tag="acc%d" % c) for c in range(BLOCKS)]
-        for c in range(BLOCKS):
-            multiply(0, c, c // 2 * 2, made0[c // 2])
+        for lo in range(0, N, P):
+            for c in range(BLOCKS):
+                multiply(0, c, c // 2 * 2, made0[c // 2], lo, lo + P)
 
         def scale(c):
             scaled = keep.tile([P, N], F32, name="scaled%d" % c)

from contextlib import ExitStack

import concourse.mybir as mybir
from concourse.masks import make_identity

K, T, S, N = 1024, 1024, 512, 256
FLOPS = 2 * K * S * N

F32 = mybir.dt.float32
BF16 = mybir.dt.bfloat16
I32 = mybir.dt.int32
U32 = mybir.dt.uint32
U16 = mybir.dt.uint16
U8 = mybir.dt.uint8
FP8X4 = mybir.dt.float8_e4m3fn_x4
ACT = mybir.ActivationFunctionType
MULT = mybir.AluOpType.mult
ADD = mybir.AluOpType.add

P = 128
PACK = 4
K_PASS = P * PACK
PASSES = K // K_PASS
BLOCKS = S // P
HALVES = N // P
MEAN_ROW, INV_ROW = P - 2, P - 1
G_ROW, B_ROW = P - 2, P - 1
ROW_AT = [(2 + t) * S for t in range(PACK)] + [t * S for t in range(PACK)]
STATS_AT = ROW_AT[3] - (S - P // 2)
ROWS = (PACK + 2) * S


def tile_picked_lnfold_silu_l_kernel(tc, xT, mean, inv, gsum, b, w1_words, w1_scales, offs, out):
    nc = tc.nc
    with ExitStack() as ctx:
        keep = ctx.enter_context(tc.tile_pool(name="keep", bufs=1))
        psum = ctx.enter_context(tc.psum_pool(name="psum", bufs=1))

        pair = keep.tile([P, 2 * T], F32, name="pair", align_bytes=64)
        singles = {i: keep.tile([P, T], F32, name="plane%d" % i, align_bytes=64) for i in (0, 3, 4, 5, 6, 7)}
        planes = [singles[i][:] if i in singles else pair[:, (i - 1) * T : i * T] for i in range(PASSES * PACK)]

        def load_run(dst, z, first):
            runs = xT[K_PASS * z : K_PASS * (z + 1), :].rearrange("(p t) c -> p (t c)", t=PACK)
            nc.sync.dma_start(dst, runs[:, first : first + dst.shape[1]])

        load_run(planes[0], 0, 0)
        offsets = keep.tile([P, S // 16], U16, name="offsets")
        nc.sync.dma_start(offsets[:], offs)

        warm_in = keep.tile([P, 1], F32, name="warm_in")
        warm_out = keep.tile([P, 1], F32, name="warm_out")
        nc.vector.memset(warm_in[:], 0.0)
        nc.scalar.activation(warm_out[:], warm_in[:], ACT.Silu)

        stats = keep.tile([P, T], F32, name="stats", align_bytes=64)
        nc.scalar.dma_start(stats[MEAN_ROW : MEAN_ROW + 1, :], mean[0:1, :])
        nc.scalar.dma_start(stats[INV_ROW : INV_ROW + 1, :], inv[0:1, :])
        nc.vector.memset(stats[0:MEAN_ROW, :], 0.0)

        consts = keep.tile([P, N], F32, name="consts")
        nc.sync.dma_start(consts[B_ROW : B_ROW + 1, :], b.rearrange("n o -> o n"))
        nc.sync.dma_start(consts[G_ROW : G_ROW + 1, :], gsum.rearrange("n o -> o n"))
        nc.vector.memset(consts[0:G_ROW, :], 0.0)
        load_run(pair[:], 0, T)
        w_scales = keep.tile([P, PASSES * N], U8, name="w_scales", align_bytes=64)
        nc.gpsimd.memset(w_scales[:].bitcast(I32), 0)
        load_run(planes[3], 0, 3 * T)
        load_run(planes[PACK], 1, 0)
        for q in range(4):
            dst = w_scales[32 * q : 32 * q + 4, :].bitcast(I32).rearrange("i (z n) -> i z n", z=PASSES)
            nc.sync.dma_start(dst, w1_scales[:, 4 * q : 4 * q + 4, :].bitcast(I32).rearrange("z i n -> i z n"))
        for t in range(1, PACK):
            load_run(planes[PACK + t], 1, t * T)
        w_codes = {}
        for z, lo, hi in ((0, 0, P), (0, P, N), (1, 0, N)):
            w_codes[z, lo] = keep.tile([P, hi - lo], U32, name="w_codes%d_%d" % (z, lo), align_bytes=64)
            nc.sync.dma_start(w_codes[z, lo][:].bitcast(I32), w1_words[z].rearrange("p n t -> p (n t)").bitcast(I32)[:, lo:hi])

        ident = keep.tile([P, P], F32, name="ident")
        make_identity(nc, ident[:])

        def listed(first, end):
            return offsets[:, first // 16 : end // 16]

        rows = keep.tile([P, ROWS], F32, name="rows", align_bytes=64)
        picked = [rows[:, ROW_AT[PACK * z] : ROW_AT[PACK * z] + PACK * S].rearrange("p (t c) -> p t c", t=PACK) for z in range(PASSES)]

        def gather(i, first, end, on_scalar):
            dst = rows[:, ROW_AT[i] + first : ROW_AT[i] + end]
            src = planes[i].indirect(listed(first, end))
            if on_scalar:
                nc.scalar.activation(dst, src, ACT.Copy)
            else:
                nc.vector.tensor_copy(dst, src)

        def weave(z, first, end, woven, on_scalar=False):
            dst = woven.rearrange("p (c i t) -> p c t i", t=PACK, i=4)
            src = picked[z][:, :, first:end].rearrange("p t (c i) -> p c t i", i=4)
            if on_scalar:
                nc.scalar.copy(dst, src)
            else:
                nc.vector.tensor_copy(dst, src)
            return woven

        def woven_tile(name, blocks, tag=None):
            return keep.tile([P, blocks * P * PACK], BF16, name=name, tag=tag or name, align_bytes=64)

        def quantize(z, first, end, woven):
            codes = keep.tile([P, (end - first) * P], U32, name="codes%d_%d" % (z, first), align_bytes=64)
            scales = keep.tile([P, (end - first) * P], U8, name="scales%d_%d" % (z, first), align_bytes=64)
            nc.vector.quantize_mx(codes[:].bitcast(FP8X4), scales[:], woven)
            return codes, scales

        def multiply(z, c, first, made, lo=0, hi=N):
            codes, scales = made
            cols = slice((c - first) * P, (c - first + 1) * P)
            nc.tensor.matmul_mx(
                accs[c][:, lo:hi],
                lhsT=codes[:, cols].bitcast(FP8X4),
                lhsT_scale=scales[:, cols],
                rhs=w_codes[z, lo][:].bitcast(FP8X4),
                rhs_scale=w_scales[:, z * N + lo : z * N + hi],
                start=(z == 0 and lo == 0),
                stop=(z == PASSES - 1),
            )

        upright = psum.tile([P, HALVES, P], F32, name="upright", tag="acc1")
        for h in range(HALVES):
            nc.tensor.transpose(upright[:, h, :], consts[:, h * P : (h + 1) * P], ident[:])
        turned = psum.tile([P, BLOCKS, P], F32, name="turned", tag="acc0")
        picked_stats = rows[:, STATS_AT : STATS_AT + S]

        def pick_stats(first):
            nc.vector.tensor_copy(picked_stats[:, first * P : (first + 2) * P], stats[:].indirect(listed(first * P, (first + 2) * P)))
            for c in (first, first + 1):
                nc.tensor.transpose(turned[:, c, :], picked_stats[:, c * P : (c + 1) * P], ident[:])

        pick_stats(0)
        const_cols = keep.tile([P, HALVES, 2], F32, name="const_cols")
        nc.vector.tensor_copy(const_cols[:], upright[:, :, G_ROW:P])
        g_bank = psum.tile([P, HALVES, P], F32, name="g_bank", tag="acc3")
        for h in range(HALVES):
            nc.tensor.transpose(g_bank[:, h, :], const_cols[:, h, 0:1].to_broadcast([P, P]), ident[:])
        pick_stats(2)
        gather(0, 0, S, True)
        minus_g = keep.tile([P, N], F32, name="minus_g")
        nc.vector.tensor_scalar_mul(minus_g[:], g_bank[:].rearrange("p h m -> p (h m)"), -1.0)
        stat_cols = keep.tile([P, BLOCKS, 2], F32, name="stat_cols")
        nc.vector.tensor_copy(stat_cols[:], turned[:, :, MEAN_ROW:P])
        inv_cols = stat_cols[:, :, 1]
        gather(1, 0, S, True)
        gather(2, 0, S, False)

        shifts = keep.tile([P, BLOCKS], F32, name="shifts")
        nc.gpsimd.tensor_tensor(shifts[:], stat_cols[:, :, 0], inv_cols, MULT)
        terms = [keep.tile([P, N], F32, name="term%d" % c) for c in range(BLOCKS)]
        for c in range(0, BLOCKS, 2):
            nc.gpsimd.tensor_scalar(terms[c][:], minus_g[:], shifts[:, c : c + 1], 0.0, MULT, ADD)
        laid = [[psum.tile([P, 2, P], F32, name="laid%d_%d" % (d, h)) for h in range(HALVES)] for d in range(BLOCKS // 2)]
        for d in range(BLOCKS // 2):
            for h in range(HALVES):
                nc.tensor.matmul(laid[d][h][:, 0, :], terms[2 * d][:, h * P : (h + 1) * P], ident[:], start=True, stop=False, is_transpose=True)

        gather(3, 0, S // 2, False)
        gather(3, S // 2, S, True)
        for c in range(1, BLOCKS, 2):
            nc.vector.tensor_scalar(terms[c][:], minus_g[:], stat_cols[:, c, 0:1], stat_cols[:, c, 1:2], MULT, MULT)
        gather(4, 0, S, True)
        both = woven_tile("woven0", BLOCKS)
        woven0 = [weave(0, first, first + S // 2, both[:, first * PACK : (first + S // 2) * PACK]) for first in (0, S // 2)]
        made0 = [quantize(0, 0, 2, woven0[0]), quantize(0, 2, BLOCKS, woven0[1])]
        gather(5, 0, S, True)
        gather(6, 0, S // 2, False)
        gather(6, S // 2, S, True)

        accs = [psum.tile([P, N], F32, name="y%d" % c, tag="acc%d" % c) for c in range(BLOCKS)]
        for lo in range(0, N, P):
            for c in range(BLOCKS):
                multiply(0, c, c // 2 * 2, made0[c // 2], lo, lo + P)

        def scale(c):
            scaled = keep.tile([P, N], F32, name="scaled%d" % c)
            width = P if c in (0, BLOCKS - 1) else N
            for lo in range(0, N, width):
                cols = slice(lo, lo + width)
                if c % 2 == 0:
                    nc.scalar.activation(scaled[:, cols], accs[c][:, cols], ACT.Copy, scale=inv_cols[:, c : c + 1])
                else:
                    nc.vector.scalar_tensor_tensor(scaled[:, cols], accs[c][:, cols], inv_cols[:, c : c + 1], terms[c][:, cols], MULT, ADD)
            return scaled

        def turn(h, first, end, bank, opened):
            for c in range(first, end):
                nc.tensor.matmul(bank[:, c - first, :], scaled[c][:, h * P : (h + 1) * P], ident[:], start=(c == first and not opened), stop=(c == end - 1), is_transpose=True)

        def activate(h, dst, bank):
            nc.scalar.activation(dst, bank, ACT.Silu, bias=const_cols[:, h, 1:2])

        def store(h, first, end, result):
            nc.sync.dma_start(out[h * P : (h + 1) * P, first * P : end * P], result[:].rearrange("p e j -> p (e j)"))

        def leave(h, first, end, bank, opened):
            turn(h, first, end, bank, opened)
            result = keep.tile([P, end - first, P], F32, name="result%d_%d" % (h, first))
            activate(h, result[:], bank[:, 0 : end - first, :])
            store(h, first, end, result)

        last = PASSES * PACK - 1
        for c in range(BLOCKS):
            gather(last, c * P, (c + 1) * P, c >= 2)
        woven1 = [woven_tile("woven1_%d" % c, 1)[:] for c in range(BLOCKS)]
        weave(1, 0, P, woven1[0])
        weave(1, P, 2 * P, woven1[1])
        weave(1, 2 * P, 3 * P, woven1[2], True)
        multiply(1, 0, 0, quantize(1, 0, 1, woven1[0]))
        for e in range(2):
            first = S - P + e * P // 2
            weave(1, first, first + P // 2, woven1[3][:, e * P * PACK // 2 : (e + 1) * P * PACK // 2], e == 1)
        for c in range(1, BLOCKS):
            multiply(1, c, c, quantize(1, c, c + 1, woven1[c]))
        scaled = [scale(c) for c in range(BLOCKS)]
        leave(0, 0, 1, laid[0][0], True)
        leave(0, 1, 2, psum.tile([P, 1, P], F32, name="spare0", tag="acc0"), False)
        leave(1, 0, 2, laid[0][1], True)
        leave(0, 2, BLOCKS, laid[1][0], True)
        result = keep.tile([P, 2, P], F32, name="result_last")
        for c, bank in ((2, laid[1][1]), (3, psum.tile([P, 1, P], F32, name="spare1", tag="acc1"))):
            turn(1, c, c + 1, bank, c == 2)
            activate(1, result[:, c - 2 : c - 1, :], bank[:, 0:1, :])
        store(1, 2, BLOCKS, result)
